import numpy as np
import ml_dtypes


def mxq(x, axis, fmt="e4m3"):
    dtype, down = {"e4m3": (ml_dtypes.float8_e4m3fn, 7), "e5m2": (ml_dtypes.float8_e5m2, 14)}[fmt]
    v = np.moveaxis(np.asarray(x, np.float32).astype(ml_dtypes.bfloat16).astype(np.float64), axis, -1)
    blocks = v.reshape(v.shape[:-1] + (-1, 32))
    amax = np.abs(blocks).max(-1, keepdims=True)
    byte = np.maximum(np.where(amax > 0, np.frexp(amax)[1] - 1 + 127, 0) - down, 1)
    scale = np.exp2(byte - 127.0)
    codes = (blocks / scale).astype(np.float32).astype(dtype).astype(np.float64)
    return np.moveaxis((codes * scale).reshape(v.shape), -1, axis)


WIDE = False


def mx_kscale(k):
    if not WIDE:
        return np.ones(k)
    levels = np.array([24, -24, 12, -12, 0])
    if k % 512:
        return np.exp2(np.random.permutation(np.resize(levels, k // 32))).repeat(32)
    a = np.empty((k // 512, 16))
    for p in range(k // 512):
        a[p, :8] = np.random.permutation(np.resize(levels, 8))
        for g in range(8):
            far = levels[np.abs(levels - a[p, g]) >= 10]
            a[p, g + 8] = far[np.random.randint(len(far))]
    return np.exp2(a.ravel()).repeat(32)


def f64(x):
    return np.asarray(x).astype(np.float64)


def striped(idx):
    return np.tile(idx.reshape(-1, 16).T, (8, 1)).astype(np.uint16)


def unstriped(offs):
    return offs[:16].T.reshape(-1).astype(np.int64)


def striped8(idx):
    return np.concatenate([v.reshape(-1, 16).T for v in idx]).astype(np.uint16)


def unstriped8(offs):
    return np.stack([offs[16 * g:16 * g + 16].T.reshape(-1) for g in range(8)]).astype(np.int64)


E2M1 = np.array([0.0, 0.5, 1.0, 1.5, 2.0, 3.0, 4.0, 6.0, -0.0, -0.5, -1.0, -1.5, -2.0, -3.0, -4.0, -6.0])


def pack_weight(w, fmt):
    k, n = w.shape
    w = f64(np.asarray(w, np.float32).astype(ml_dtypes.bfloat16)).reshape(k // 32, 32, n)
    amax = np.abs(w).max(1)
    if fmt == "e4m3":
        byte = np.frexp(amax)[1] - 1 + 127 - 7
    else:
        mant, ex = np.frexp(amax / 6.0)
        byte = np.where(mant > 0.5, ex, ex - 1) + 127
    byte = np.clip(np.where(amax > 0, byte, 1), 1, 254)
    scaled = (w * np.exp2(127.0 - byte)[:, None, :]).reshape(k, n).astype(np.float32)
    by_word = np.ascontiguousarray(scaled.reshape(k // 512, 128, 4, n).transpose(0, 1, 3, 2))
    if fmt == "e4m3":
        words = by_word.astype(ml_dtypes.float8_e4m3fn).view(np.uint8)
    else:
        c = by_word.astype(ml_dtypes.float4_e2m1fn).view(np.uint8) & 0xF
        words = (c[..., 0::2] | (c[..., 1::2] << 4)).reshape(k // 512, 128, 2 * n)
    return np.ascontiguousarray(words), np.ascontiguousarray(byte.astype(np.uint8).reshape(k // 512, 16, n))


def unpack_weight(words, scales, fmt):
    g, _, n = scales.shape
    words = np.ascontiguousarray(words).reshape(g, 128, n, -1)
    if fmt == "e4m3":
        vals = words.view(ml_dtypes.float8_e4m3fn).astype(np.float64)
    else:
        nib = np.empty((g, 128, n, 4), np.uint8)
        nib[..., 0::2] = words & 0xF
        nib[..., 1::2] = words >> 4
        vals = E2M1[nib]
    vals = vals * np.repeat(np.exp2(scales.astype(np.float64) - 127.0), 8, axis=1)[..., None]
    return vals.transpose(0, 1, 3, 2).reshape(g * 512, n)


def planes(y):
    n, m = y.shape
    v = y.astype(np.float32).astype(ml_dtypes.bfloat16).astype(np.float64).reshape(n // 32, 32, m)
    top = np.abs(v).max(1)
    byte = np.clip(np.where(top > 0, np.frexp(top)[1] - 1 + 127 - 7, 1), 1, 254)
    codes = (v * np.exp2(127.0 - byte)[:, None, :]).reshape(n, m).astype(np.float32).astype(ml_dtypes.float8_e4m3fn).view(np.uint8)
    words = codes.reshape(n // 512, 128, 4, m).transpose(0, 1, 3, 2)
    return np.ascontiguousarray(words), np.ascontiguousarray(byte.astype(np.uint8).reshape(n // 512, 16, m))


K, L, R, N, T, J = 512, 512, 512, 512, 2048, 1024


def setup_inputs():
    n = np.random.standard_normal
    s = mx_kscale(K)[:, None]
    s2 = mx_kscale(L)[:, None]
    u = mx_kscale(R)[:, None]
    p_tab = pack_weight(n((L, T)) * s2, "e4m3")
    p_wa = pack_weight(n((K, R)) / np.sqrt(K) / s * u.T, "e2m1")
    p_wd = pack_weight(n((R, N)) / np.sqrt(R) / u, "e2m1")
    return {
        "tab_words": p_tab[0],
        "tab_scales": p_tab[1],
        "xT": (n((K, T)) * s).astype(np.float32),
        "wgt2": np.repeat(np.random.uniform(0.5, 2.0, (8, J)), 16, axis=0).astype(np.float32),
        "wa_words": p_wa[0],
        "wa_scales": p_wa[1],
        "wb": (n((L, R)) / np.sqrt(L) / s2).astype(np.float32),
        "wd_words": p_wd[0],
        "wd_scales": p_wd[1],
        "offs": striped(np.random.permutation(T)[:J]),
        "offs2": striped8(np.stack([np.random.permutation(T)[:J] for _ in range(8)])),
    }


def reference(tab_words, tab_scales, xT, wgt2, wa_words, wa_scales, wb, wd_words, wd_scales, offs, offs2):
    idx = unstriped(offs)
    idx2 = unstriped8(offs2)
    tab_ = unpack_weight(tab_words, tab_scales, "e4m3")[:, idx]
    rows = np.arange(K)
    xg = f64(wgt2)[rows // 4 % 128] * f64(xT)[rows[:, None], idx2[rows % 512 // 64]]
    xT_ = mxq(xg, 0, "e4m3")
    wa_ = unpack_weight(wa_words, wa_scales, "e2m1")
    wb_ = mxq(f64(wb), 0, "e4m3")
    ya = wa_.T @ xT_
    yb = wb_.T @ tab_
    h = ya * yb
    h_ = mxq(h, 0, "e4m3")
    wd_ = unpack_weight(wd_words, wd_scales, "e2m1")
    y = wd_.T @ h_
    return (y,) + planes(y)

@@ -1,0 +1,209 @@
+from contextlib import ExitStack
+
+import concourse.mybir as mybir
+
+K, T, J = 512, 2048, 1024
+FLOPS = 3 * 2 * K * K * J
+
+F32 = mybir.dt.float32
+BF16 = mybir.dt.bfloat16
+I32 = mybir.dt.int32
+U32 = mybir.dt.uint32
+U16 = mybir.dt.uint16
+U8 = mybir.dt.uint8
+E4M3 = mybir.dt.float8_e4m3fn_x4
+E2M1 = mybir.dt.float4_e2m1fn_x4
+MULT = mybir.AluOpType.mult
+
+P = 128
+PACK = 4
+BANK = 128
+HALF = 512
+CHUNK = 256
+STRIPE = 16
+SCALAR_ROUNDS = 1
+
+
+def tile_list_htabg_mul_noneP_kernel(
+    tc, tab_words, tab_scales, xT, wgt2, wa_words, wa_scales, wb, wd_words, wd_scales, offs, offs2, out_0, out_1, out_2
+):
+    nc = tc.nc
+    with ExitStack() as ctx:
+        keep = ctx.enter_context(tc.tile_pool(name="keep", bufs=1))
+        psum = ctx.enter_context(tc.psum_pool(name="psum", bufs=1))
+
+        def load_scale_rows(queue, plane, rows):
+            for q in range(4):
+                queue.dma_start(out=plane[32 * q : 32 * q + 4, :].bitcast(I32), in_=rows[4 * q : 4 * q + 4, :].bitcast(I32))
+
+        tab_list = keep.tile([P, J // STRIPE], U16, name="tab_list")
+        x_lists = keep.tile([P, J // STRIPE], U16, name="x_lists")
+        tab_s = keep.tile([P, T], U8, name="tab_s", align_bytes=64)
+        tab_w = keep.tile([P, T], U32, name="tab_w", align_bytes=64)
+        w4_s_raw = keep.tile([P, 2 * K], U8, name="w4_s_raw", align_bytes=64)
+        w4_w_raw = keep.tile([P, 4 * K], U8, name="w4_w_raw", align_bytes=64)
+        wgt = [keep.tile([P, HALF], F32, name="wgt%d" % h) for h in range(2)]
+        x_planes = [keep.tile([P, T], F32, name="x_plane%d" % i) for i in range(PACK)]
+        wb_raw = keep.tile([P, PACK, K], F32, name="wb_raw")
+
+        nc.vector.memset(tab_s[:].bitcast(I32), 0)
+        nc.gpsimd.memset(w4_s_raw[:].bitcast(I32), 0)
+
+        x_rows = xT.rearrange("(p i) t -> p i t", i=PACK)
+        nc.sync.dma_start(tab_list[:], offs)
+        load_scale_rows(nc.scalar, tab_s, tab_scales[0])
+        nc.sync.dma_start(out=wb_raw[:], in_=wb.rearrange("(p i) r -> p i r", i=PACK))
+        nc.sync.dma_start(out=tab_w[:].bitcast(I32), in_=tab_words[0].rearrange("p t i -> p (t i)").bitcast(I32))
+        nc.sync.dma_start(x_lists[:], offs2)
+        nc.sync.dma_start(out=wgt[0][:], in_=wgt2[:, 0:HALF])
+        nc.sync.dma_start(out=x_planes[0][:], in_=x_rows[:, 0, :])
+        nc.sync.dma_start(out=w4_w_raw[:, 0 : 2 * K].bitcast(I32), in_=wa_words[0].bitcast(I32))
+        load_scale_rows(nc.sync, w4_s_raw[:, 0:K], wa_scales[0])
+        nc.sync.dma_start(out=wgt[1][:], in_=wgt2[:, HALF:J])
+        nc.sync.dma_start(out=x_planes[1][:], in_=x_rows[:, 1, :])
+        nc.sync.dma_start(out=w4_w_raw[:, 2 * K : 4 * K].bitcast(I32), in_=wd_words[0].bitcast(I32))
+        load_scale_rows(nc.sync, w4_s_raw[:, K : 2 * K], wd_scales[0])
+        nc.sync.dma_start(out=x_planes[2][:], in_=x_rows[:, 2, :])
+        nc.sync.dma_start(out=x_planes[3][:], in_=x_rows[:, 3, :])
+
+        v_s = keep.tile([P, J], U8, name="v_s", align_bytes=64)
+        v_w = keep.tile([P, J], U32, name="v_w", align_bytes=64)
+        nc.vector.tensor_copy(v_s[:], tab_s[:].indirect(tab_list[:]))
+        nc.vector.tensor_copy(v_w[:], tab_w[:].indirect(tab_list[:]))
+
+        picked = [keep.tile([P, PACK, HALF], F32, name="picked%d" % h) for h in range(2)]
+
+        def gather(i, j0, n):
+            h, c0 = divmod(j0, HALF)
+            nc.vector.tensor_tensor(
+                picked[h][:, i, c0 : c0 + n],
+                x_planes[i][:].indirect(x_lists[:, j0 // STRIPE : (j0 + n) // STRIPE]),
+                wgt[h][:, c0 : c0 + n],
+                MULT,
+            )
+
+        for i in range(2):
+            for h in range(2):
+                gather(i, h * HALF, HALF)
+
+        wb_bf = keep.tile([P, K * PACK], BF16, name="wb_bf", align_bytes=64)
+        wb_w = keep.tile([P, K], U32, name="wb_w", align_bytes=64)
+        wb_s = keep.tile([P, K], U8, name="wb_s", align_bytes=64)
+        nc.scalar.copy(
+            out=wb_bf[:].rearrange("p (t m i) -> p t m i", t=PACK, i=PACK),
+            in_=wb_raw[:].rearrange("p i (m t) -> p t m i", t=PACK),
+        )
+        nc.vector.quantize_mx(out=wb_w[:].bitcast(E4M3), scales=wb_s[:], in_=wb_bf[:])
+
+        w4_w = keep.tile([P, 4 * K], U8, name="w4_w", align_bytes=64)
+        w4_s = keep.tile([P, 2 * K], U8, name="w4_s", align_bytes=64)
+        nc.vector.tensor_copy(
+            out=w4_w[:].bitcast(U16).rearrange("p (w t m) -> p w t m", w=2, t=PACK),
+            in_=w4_w_raw[:].bitcast(U16).rearrange("p (w m t) -> p w t m", w=2, t=PACK),
+        )
+        nc.vector.tensor_copy(
+            out=w4_s[:].rearrange("p (w t m) -> p w t m", w=2, t=PACK),
+            in_=w4_s_raw[:].rearrange("p (w m t) -> p w t m", w=2, t=PACK),
+        )
+
+        def fp4_slice(w, t):
+            c0 = w * K + t * P
+            return w4_w[:, 2 * c0 : 2 * (c0 + P)].bitcast(E2M1), w4_s[:, c0 : c0 + P]
+
+        def wb_slice(t):
+            return wb_w[:, t * P : (t + 1) * P].bitcast(E4M3), wb_s[:, t * P : (t + 1) * P]
+
+        def product(bank, weights, words, scales):
+            for t in range(PACK):
+                w_words, w_scales = weights(t)
+                nc.tensor.matmul_mx(
+                    out=bank[:, t, :], lhsT=w_words, lhsT_scale=w_scales, rhs=words.bitcast(E4M3), rhs_scale=scales,
+                    start=True, stop=True,
+                )
+
+        yb = [keep.tile([P, BANK, PACK], F32, name="yb%d" % b) for b in range(J // BANK)]
+        for b in range(J // BANK):
+            cols = slice(b * BANK, (b + 1) * BANK)
+            bank = psum.tile([P, PACK, BANK], F32, name="yb_bank", bufs=2)
+            product(bank, wb_slice, v_w[:, cols], v_s[:, cols])
+            nc.scalar.copy(out=yb[b][:], in_=bank[:].rearrange("p t j -> p j t"))
+
+        for h in range(2):
+            gather(2, h * HALF, HALF)
+        for c in range(J // CHUNK):
+            gather(3, c * CHUNK, CHUNK)
+
+        y_s = keep.tile([P, J], U8, name="y_s", align_bytes=64)
+        y_rows = out_0.rearrange("(p t) j -> p t j", t=PACK)
+        y_words = out_1[0].rearrange("p j i -> p (j i)").bitcast(I32)
+        nchunks = J // CHUNK
+        x_q, h_bf, h_q, y_bf = {}, {}, {}, {}
+
+        def quantised(name, src):
+            words = keep.tile([P, CHUNK], U32, name=name + "_w", align_bytes=64)
+            scales = keep.tile([P, CHUNK], U8, name=name + "_s", align_bytes=64)
+            nc.vector.quantize_mx(out=words[:].bitcast(E4M3), scales=scales[:], in_=src[:])
+            return words, scales
+
+        def stage_x(c):
+            h, c0 = divmod(c * CHUNK, HALF)
+            x_bf = keep.tile([P, CHUNK * PACK], BF16, name="x_bf%d" % c, align_bytes=64)
+            nc.scalar.copy(
+                out=x_bf[:].rearrange("p (g e i) -> p g i e", e=4, i=PACK),
+                in_=picked[h][:, :, c0 : c0 + CHUNK].rearrange("p i (g e) -> p g i e", e=4),
+            )
+            x_q[c] = quantised("x%d" % c, x_bf)
+
+        def stage_h(c):
+            words, scales = x_q[c]
+            h_bf[c] = keep.tile([P, CHUNK * PACK], BF16, name="h_bf%d" % c, align_bytes=64)
+            for u in range(CHUNK // BANK):
+                cols = slice(u * BANK, (u + 1) * BANK)
+                bank = psum.tile([P, PACK, BANK], F32, name="ya_bank", bufs=3)
+                product(bank, lambda t: fp4_slice(0, t), words[:, cols], scales[:, cols])
+                nc.vector.tensor_tensor(
+                    h_bf[c][:, u * BANK * PACK : (u + 1) * BANK * PACK].rearrange("p (j t) -> p j t", t=PACK),
+                    bank[:].rearrange("p t j -> p j t"),
+                    yb[c * (CHUNK // BANK) + u][:],
+                    MULT,
+                )
+
+        def stage_hq(c):
+            h_q[c] = quantised("h%d" % c, h_bf[c])
+
+        def stage_y(c):
+            words, scales = h_q[c]
+            y_f = keep.tile([P, PACK, CHUNK], F32, name="y_f%d" % c)
+            y_bf[c] = keep.tile([P, CHUNK * PACK], BF16, name="y_bf%d" % c, align_bytes=64)
+            for u in range(CHUNK // BANK):
+                cols = slice(u * BANK, (u + 1) * BANK)
+                bank = psum.tile([P, PACK, BANK], F32, name="y_bank", bufs=3)
+                product(bank, lambda t: fp4_slice(1, t), words[:, cols], scales[:, cols])
+                if c < SCALAR_ROUNDS:
+                    nc.scalar.copy(
+                        out=y_bf[c][:, u * BANK * PACK : (u + 1) * BANK * PACK].rearrange("p (j t) -> p j t", t=PACK),
+                        in_=bank[:].rearrange("p t j -> p j t"),
+                    )
+                nc.scalar.copy(out=y_f[:, :, cols], in_=bank[:])
+            if c >= SCALAR_ROUNDS:
+                nc.vector.tensor_copy(
+                    out=y_bf[c][:].rearrange("p (g e t) -> p g t e", e=4, t=PACK),
+                    in_=y_f[:].rearrange("p t (g e) -> p g t e", e=4),
+                )
+            nc.sync.dma_start(out=y_rows[:, :, c * CHUNK : (c + 1) * CHUNK], in_=y_f[:])
+
+        def stage_yq(c):
+            cols = slice(c * CHUNK, (c + 1) * CHUNK)
+            words = keep.tile([P, CHUNK], U32, name="y_w%d" % c, align_bytes=64)
+            nc.vector.quantize_mx(out=words[:].bitcast(E4M3), scales=y_s[:, cols], in_=y_bf[c][:])
+            nc.sync.dma_start(out=y_words[:, cols], in_=words[:].bitcast(I32))
+
+        stages = [stage_x, stage_h, stage_hq, stage_y, stage_yq]
+        for step in range(nchunks + len(stages) - 1):
+            for s in reversed(range(len(stages))):
+                if 0 <= step - s < nchunks:
+                    stages[s](step - s)
+        for q in range(4):
+            nc.sync.dma_start(
+                out=out_2[0, 4 * q : 4 * q + 4, :].bitcast(I32), in_=y_s[32 * q : 32 * q + 4, :].bitcast(I32)
+            )

@@ -46,30 +46,62 @@ def tile_list_htabg_mul_noneP_kernel(
         x_planes = [keep.tile([P, T], F32, name="x_plane%d" % i) for i in range(PACK)]
         wb_raw = keep.tile([P, PACK, K], F32, name="wb_raw")
 
-        nc.vector.memset(tab_s[:].bitcast(I32), 0)
         nc.gpsimd.memset(w4_s_raw[:].bitcast(I32), 0)
 
         x_rows = xT.rearrange("(p i) t -> p i t", i=PACK)
         nc.sync.dma_start(tab_list[:], offs)
-        load_scale_rows(nc.scalar, tab_s, tab_scales[0])
+        for q in range(4):
+            nc.sync.dma_start(
+                out=tab_s[32 * q : 32 * (q + 1), :].bitcast(I32),
+                in_=tab_scales[0, 4 * q : 4 * q + 4, :].bitcast(I32).partition_broadcast(8),
+            )
         nc.sync.dma_start(out=wb_raw[:], in_=wb.rearrange("(p i) r -> p i r", i=PACK))
+        nc.sync.dma_start(out=w4_w_raw[:, 0 : 2 * K].bitcast(I32), in_=wa_words[0].bitcast(I32))
+        nc.sync.dma_start(out=w4_w_raw[:, 2 * K : 4 * K].bitcast(I32), in_=wd_words[0].bitcast(I32))
+        load_scale_rows(nc.sync, w4_s_raw[:, 0:K], wa_scales[0])
         nc.sync.dma_start(out=tab_w[:].bitcast(I32), in_=tab_words[0].rearrange("p t i -> p (t i)").bitcast(I32))
         nc.sync.dma_start(x_lists[:], offs2)
         nc.sync.dma_start(out=wgt[0][:], in_=wgt2[:, 0:HALF])
         nc.sync.dma_start(out=x_planes[0][:], in_=x_rows[:, 0, :])
-        nc.sync.dma_start(out=w4_w_raw[:, 0 : 2 * K].bitcast(I32), in_=wa_words[0].bitcast(I32))
-        load_scale_rows(nc.sync, w4_s_raw[:, 0:K], wa_scales[0])
         nc.sync.dma_start(out=wgt[1][:], in_=wgt2[:, HALF:J])
         nc.sync.dma_start(out=x_planes[1][:], in_=x_rows[:, 1, :])
-        nc.sync.dma_start(out=w4_w_raw[:, 2 * K : 4 * K].bitcast(I32), in_=wd_words[0].bitcast(I32))
         load_scale_rows(nc.sync, w4_s_raw[:, K : 2 * K], wd_scales[0])
         nc.sync.dma_start(out=x_planes[2][:], in_=x_rows[:, 2, :])
         nc.sync.dma_start(out=x_planes[3][:], in_=x_rows[:, 3, :])
 
         v_s = keep.tile([P, J], U8, name="v_s", align_bytes=64)
-        v_w = keep.tile([P, J], U32, name="v_w", align_bytes=64)
         nc.vector.tensor_copy(v_s[:], tab_s[:].indirect(tab_list[:]))
-        nc.vector.tensor_copy(v_w[:], tab_w[:].indirect(tab_list[:]))
+
+        wb_bf = keep.tile([P, K * PACK], BF16, name="wb_bf", align_bytes=64)
+        wb_w = keep.tile([P, K], U32, name="wb_w", align_bytes=64)
+        wb_s = keep.tile([P, K], U8, name="wb_s", align_bytes=64)
+        wb_from = wb_raw[:].rearrange("p i (m t) -> p m i t", t=PACK)
+        wb_to = wb_bf[:].rearrange("p (t m i) -> p m i t", t=PACK, i=PACK)
+        nc.vector.tensor_copy(out=wb_to[:, :, :, 0:2], in_=wb_from[:, :, :, 0:2])
+        nc.scalar.copy(out=wb_to[:, :, :, 2:4], in_=wb_from[:, :, :, 2:4])
+
+        w4_w = keep.tile([P, 4 * K], U8, name="w4_w", align_bytes=64)
+        w4_s = [keep.tile([P, K], U8, name="w4_s%d" % w, align_bytes=64) for w in range(2)]
+        nc.vector.tensor_copy(
+            out=w4_w[:].bitcast(U16).rearrange("p (w t m) -> p w t m", w=2, t=PACK),
+            in_=w4_w_raw[:].bitcast(U16).rearrange("p (w m t) -> p w t m", w=2, t=PACK),
+        )
+
+        def deal_scales(w):
+            nc.vector.tensor_copy(
+                out=w4_s[w][:].rearrange("p (t m) -> p t m", t=PACK),
+                in_=w4_s_raw[:, w * K : (w + 1) * K].rearrange("p (m t) -> p t m", t=PACK),
+            )
+
+        deal_scales(0)
+        nc.vector.quantize_mx(out=wb_w[:].bitcast(E4M3), scales=wb_s[:], in_=wb_bf[:])
+
+        v_w = keep.tile([P, J], U32, name="v_w", align_bytes=64)
+        for h in range(2):
+            nc.vector.tensor_copy(
+                v_w[:, h * HALF : (h + 1) * HALF],
+                tab_w[:].indirect(tab_list[:, h * HALF // STRIPE : (h + 1) * HALF // STRIPE]),
+            )
 
         picked = [keep.tile([P, PACK, HALF], F32, name="picked%d" % h) for h in range(2)]
 
@@ -86,29 +118,11 @@ def tile_list_htabg_mul_noneP_kernel(
             for h in range(2):
                 gather(i, h * HALF, HALF)
 
-        wb_bf = keep.tile([P, K * PACK], BF16, name="wb_bf", align_bytes=64)
-        wb_w = keep.tile([P, K], U32, name="wb_w", align_bytes=64)
-        wb_s = keep.tile([P, K], U8, name="wb_s", align_bytes=64)
-        nc.scalar.copy(
-            out=wb_bf[:].rearrange("p (t m i) -> p t m i", t=PACK, i=PACK),
-            in_=wb_raw[:].rearrange("p i (m t) -> p t m i", t=PACK),
-        )
-        nc.vector.quantize_mx(out=wb_w[:].bitcast(E4M3), scales=wb_s[:], in_=wb_bf[:])
-
-        w4_w = keep.tile([P, 4 * K], U8, name="w4_w", align_bytes=64)
-        w4_s = keep.tile([P, 2 * K], U8, name="w4_s", align_bytes=64)
-        nc.vector.tensor_copy(
-            out=w4_w[:].bitcast(U16).rearrange("p (w t m) -> p w t m", w=2, t=PACK),
-            in_=w4_w_raw[:].bitcast(U16).rearrange("p (w m t) -> p w t m", w=2, t=PACK),
-        )
-        nc.vector.tensor_copy(
-            out=w4_s[:].rearrange("p (w t m) -> p w t m", w=2, t=PACK),
-            in_=w4_s_raw[:].rearrange("p (w m t) -> p w t m", w=2, t=PACK),
-        )
+        deal_scales(1)
 
         def fp4_slice(w, t):
             c0 = w * K + t * P
-            return w4_w[:, 2 * c0 : 2 * (c0 + P)].bitcast(E2M1), w4_s[:, c0 : c0 + P]
+            return w4_w[:, 2 * c0 : 2 * (c0 + P)].bitcast(E2M1), w4_s[w][:, t * P : (t + 1) * P]
 
         def wb_slice(t):
             return wb_w[:, t * P : (t + 1) * P].bitcast(E4M3), wb_s[:, t * P : (t + 1) * P]
@@ -198,12 +212,15 @@ def tile_list_htabg_mul_noneP_kernel(
             nc.vector.quantize_mx(out=words[:].bitcast(E4M3), scales=y_s[:, cols], in_=y_bf[c][:])
             nc.sync.dma_start(out=y_words[:, cols], in_=words[:].bitcast(I32))
 
-        stages = [stage_x, stage_h, stage_hq, stage_y, stage_yq]
-        for step in range(nchunks + len(stages) - 1):
-            for s in reversed(range(len(stages))):
-                if 0 <= step - s < nchunks:
-                    stages[s](step - s)
+        later = [stage_yq, stage_y, stage_hq, stage_h]
+        for step in range(nchunks + len(later) + 1):
+            if step < nchunks:
+                stage_x(step)
+            for lag, stage in zip(range(len(later) + 1, 1, -1), later):
+                if 0 <= step - lag < nchunks:
+                    stage(step - lag)
         for q in range(4):
-            nc.sync.dma_start(
+            queue = nc.scalar if q % 2 else nc.sync
+            queue.dma_start(
                 out=out_2[0, 4 * q : 4 * q + 4, :].bitcast(I32), in_=y_s[32 * q : 32 * q + 4, :].bitcast(I32)
             )

@@ -60,12 +60,12 @@ def tile_list_htabg_mul_noneP_kernel(
         nc.sync.dma_start(out=w4_w_raw[:, 2 * K : 4 * K].bitcast(I32), in_=wd_words[0].bitcast(I32))
         load_scale_rows(nc.sync, w4_s_raw[:, 0:K], wa_scales[0])
         nc.sync.dma_start(out=tab_w[:].bitcast(I32), in_=tab_words[0].rearrange("p t i -> p (t i)").bitcast(I32))
+        load_scale_rows(nc.sync, w4_s_raw[:, K : 2 * K], wd_scales[0])
         nc.sync.dma_start(x_lists[:], offs2)
         nc.sync.dma_start(out=wgt[0][:], in_=wgt2[:, 0:HALF])
         nc.sync.dma_start(out=x_planes[0][:], in_=x_rows[:, 0, :])
         nc.sync.dma_start(out=wgt[1][:], in_=wgt2[:, HALF:J])
         nc.sync.dma_start(out=x_planes[1][:], in_=x_rows[:, 1, :])
-        load_scale_rows(nc.sync, w4_s_raw[:, K : 2 * K], wd_scales[0])
         nc.sync.dma_start(out=x_planes[2][:], in_=x_rows[:, 2, :])
         nc.sync.dma_start(out=x_planes[3][:], in_=x_rows[:, 3, :])
 
@@ -103,12 +103,23 @@ def tile_list_htabg_mul_noneP_kernel(
                 tab_w[:].indirect(tab_list[:, h * HALF // STRIPE : (h + 1) * HALF // STRIPE]),
             )
 
-        picked = [keep.tile([P, PACK, HALF], F32, name="picked%d" % h) for h in range(2)]
+        deal_scales(1)
+
+        picked = [[keep.tile([P, 2, HALF], F32, name="picked%d_%d" % (u, h)) for h in range(2)] for u in range(2)]
+        x_bf = [keep.tile([P, CHUNK * PACK], BF16, name="x_bf%d" % c, align_bytes=64) for c in range(J // CHUNK)]
+
+        def weave(u, c):
+            h, c0 = divmod(c * CHUNK, HALF)
+            nc.scalar.copy(
+                out=x_bf[c][:].rearrange("p (j u e) -> p j u e", u=2, e=2)[:, :, u, :],
+                in_=picked[u][h][:, :, c0 : c0 + CHUNK].rearrange("p e j -> p j e"),
+            )
+
 
         def gather(i, j0, n):
             h, c0 = divmod(j0, HALF)
             nc.vector.tensor_tensor(
-                picked[h][:, i, c0 : c0 + n],
+                picked[i // 2][h][:, i % 2, c0 : c0 + n],
                 x_planes[i][:].indirect(x_lists[:, j0 // STRIPE : (j0 + n) // STRIPE]),
                 wgt[h][:, c0 : c0 + n],
                 MULT,
@@ -117,8 +128,6 @@ def tile_list_htabg_mul_noneP_kernel(
         for i in range(2):
             for h in range(2):
                 gather(i, h * HALF, HALF)
-
-        deal_scales(1)
 
         def fp4_slice(w, t):
             c0 = w * K + t * P
@@ -142,6 +151,8 @@ def tile_list_htabg_mul_noneP_kernel(
             product(bank, wb_slice, v_w[:, cols], v_s[:, cols])
             nc.scalar.copy(out=yb[b][:], in_=bank[:].rearrange("p t j -> p j t"))
 
+        for c in range(J // CHUNK):
+            weave(0, c)
         for h in range(2):
             gather(2, h * HALF, HALF)
         for c in range(J // CHUNK):
@@ -151,7 +162,7 @@ def tile_list_htabg_mul_noneP_kernel(
         y_rows = out_0.rearrange("(p t) j -> p t j", t=PACK)
         y_words = out_1[0].rearrange("p j i -> p (j i)").bitcast(I32)
         nchunks = J // CHUNK
-        x_q, h_bf, h_q, y_bf = {}, {}, {}, {}
+        x_q, h_bf, h_q, y_bf, y_fs = {}, {}, {}, {}, {}
 
         def quantised(name, src):
             words = keep.tile([P, CHUNK], U32, name=name + "_w", align_bytes=64)
@@ -160,13 +171,8 @@ def tile_list_htabg_mul_noneP_kernel(
             return words, scales
 
         def stage_x(c):
-            h, c0 = divmod(c * CHUNK, HALF)
-            x_bf = keep.tile([P, CHUNK * PACK], BF16, name="x_bf%d" % c, align_bytes=64)
-            nc.scalar.copy(
-                out=x_bf[:].rearrange("p (g e i) -> p g i e", e=4, i=PACK),
-                in_=picked[h][:, :, c0 : c0 + CHUNK].rearrange("p i (g e) -> p g i e", e=4),
-            )
-            x_q[c] = quantised("x%d" % c, x_bf)
+            weave(1, c)
+            x_q[c] = quantised("x%d" % c, x_bf[c])
 
         def stage_h(c):
             words, scales = x_q[c]
@@ -188,35 +194,34 @@ def tile_list_htabg_mul_noneP_kernel(
         def stage_y(c):
             words, scales = h_q[c]
             y_f = keep.tile([P, PACK, CHUNK], F32, name="y_f%d" % c)
+            y_fs[c] = y_f
             y_bf[c] = keep.tile([P, CHUNK * PACK], BF16, name="y_bf%d" % c, align_bytes=64)
             for u in range(CHUNK // BANK):
                 cols = slice(u * BANK, (u + 1) * BANK)
                 bank = psum.tile([P, PACK, BANK], F32, name="y_bank", bufs=3)
                 product(bank, lambda t: fp4_slice(1, t), words[:, cols], scales[:, cols])
-                if c < SCALAR_ROUNDS:
+                nc.scalar.copy(out=y_f[:, :, cols], in_=bank[:])
+                if c >= nchunks - SCALAR_ROUNDS:
                     nc.scalar.copy(
                         out=y_bf[c][:, u * BANK * PACK : (u + 1) * BANK * PACK].rearrange("p (j t) -> p j t", t=PACK),
                         in_=bank[:].rearrange("p t j -> p j t"),
                     )
-                nc.scalar.copy(out=y_f[:, :, cols], in_=bank[:])
-            if c >= SCALAR_ROUNDS:
-                nc.vector.tensor_copy(
-                    out=y_bf[c][:].rearrange("p (g e t) -> p g t e", e=4, t=PACK),
-                    in_=y_f[:].rearrange("p t (g e) -> p g t e", e=4),
-                )
             nc.sync.dma_start(out=y_rows[:, :, c * CHUNK : (c + 1) * CHUNK], in_=y_f[:])
 
         def stage_yq(c):
+            if c < nchunks - SCALAR_ROUNDS:
+                nc.vector.tensor_copy(
+                    out=y_bf[c][:].rearrange("p (g e t) -> p g t e", e=4, t=PACK),
+                    in_=y_fs[c][:].rearrange("p t (g e) -> p g t e", e=4),
+                )
             cols = slice(c * CHUNK, (c + 1) * CHUNK)
             words = keep.tile([P, CHUNK], U32, name="y_w%d" % c, align_bytes=64)
             nc.vector.quantize_mx(out=words[:].bitcast(E4M3), scales=y_s[:, cols], in_=y_bf[c][:])
             nc.sync.dma_start(out=y_words[:, cols], in_=words[:].bitcast(I32))
 
-        later = [stage_yq, stage_y, stage_hq, stage_h]
-        for step in range(nchunks + len(later) + 1):
-            if step < nchunks:
-                stage_x(step)
-            for lag, stage in zip(range(len(later) + 1, 1, -1), later):
+        stages = [(stage_x, 0), (stage_y, 4), (stage_hq, 3), (stage_h, 2), (stage_yq, 6)]
+        for step in range(nchunks + 6):
+            for stage, lag in stages:
                 if 0 <= step - lag < nchunks:
                     stage(step - lag)
         for q in range(4):

@@ -147,7 +147,7 @@ def tile_list_htabg_mul_noneP_kernel(
         yb = [keep.tile([P, BANK, PACK], F32, name="yb%d" % b) for b in range(J // BANK)]
         for b in range(J // BANK):
             cols = slice(b * BANK, (b + 1) * BANK)
-            bank = psum.tile([P, PACK, BANK], F32, name="yb_bank", bufs=2)
+            bank = psum.tile([P, PACK, BANK], F32, name="out_bank", bufs=5)
             product(bank, wb_slice, v_w[:, cols], v_s[:, cols])
             nc.scalar.copy(out=yb[b][:], in_=bank[:].rearrange("p t j -> p j t"))
 
@@ -198,7 +198,7 @@ def tile_list_htabg_mul_noneP_kernel(
             y_bf[c] = keep.tile([P, CHUNK * PACK], BF16, name="y_bf%d" % c, align_bytes=64)
             for u in range(CHUNK // BANK):
                 cols = slice(u * BANK, (u + 1) * BANK)
-                bank = psum.tile([P, PACK, BANK], F32, name="y_bank", bufs=3)
+                bank = psum.tile([P, PACK, BANK], F32, name="out_bank", bufs=5)
                 product(bank, lambda t: fp4_slice(1, t), words[:, cols], scales[:, cols])
                 nc.scalar.copy(out=y_f[:, :, cols], in_=bank[:])
                 if c >= nchunks - SCALAR_ROUNDS:

@@ -19,9 +19,19 @@ P = 128
 PACK = 4
 BANK = 128
 HALF = 512
-CHUNK = 256
 STRIPE = 16
-SCALAR_ROUNDS = 1
+V_WIDTHS = [256, 768]
+X_WIDTHS = [128, 128, 256, 256, 256]
+H_WIDTHS = [128, 128, 256, 256, 128, 128]
+Y_WIDTHS = [128, 128, 256, 256, 128, 128]
+Q_WIDTHS = [256, 256, 256, 128, 128]
+W_WIDTHS = [512, 384, 128]
+VECTOR_ROUNDS = (4, 5, 6)
+ROUND_FIRST = (7,)
+
+
+def cuts(widths):
+    return [(sum(widths[:c]), n) for c, n in enumerate(widths)]
 
 
 def tile_list_htabg_mul_noneP_kernel(
@@ -44,28 +54,30 @@ def tile_list_htabg_mul_noneP_kernel(
         w4_w_raw = keep.tile([P, 4 * K], U8, name="w4_w_raw", align_bytes=64)
         wgt = [keep.tile([P, HALF], F32, name="wgt%d" % h) for h in range(2)]
         x_planes = [keep.tile([P, T], F32, name="x_plane%d" % i) for i in range(PACK)]
-        wb_raw = keep.tile([P, PACK, K], F32, name="wb_raw")
+        wb_raw = [keep.tile([P, PACK, K // 2], F32, name="wb_raw%d" % h) for h in range(2)]
 
         nc.gpsimd.memset(w4_s_raw[:].bitcast(I32), 0)
 
         x_rows = xT.rearrange("(p i) t -> p i t", i=PACK)
+        wb_rows = wb.rearrange("(p i) r -> p i r", i=PACK)
         nc.sync.dma_start(tab_list[:], offs)
         for q in range(4):
             nc.sync.dma_start(
                 out=tab_s[32 * q : 32 * (q + 1), :].bitcast(I32),
                 in_=tab_scales[0, 4 * q : 4 * q + 4, :].bitcast(I32).partition_broadcast(8),
             )
-        nc.sync.dma_start(out=wb_raw[:], in_=wb.rearrange("(p i) r -> p i r", i=PACK))
+        nc.sync.dma_start(out=wb_raw[0][:], in_=wb_rows[:, :, 0 : K // 2])
+        nc.sync.dma_start(out=wb_raw[1][:], in_=wb_rows[:, :, K // 2 : K])
         nc.sync.dma_start(out=w4_w_raw[:, 0 : 2 * K].bitcast(I32), in_=wa_words[0].bitcast(I32))
         nc.sync.dma_start(out=w4_w_raw[:, 2 * K : 4 * K].bitcast(I32), in_=wd_words[0].bitcast(I32))
-        load_scale_rows(nc.sync, w4_s_raw[:, 0:K], wa_scales[0])
         nc.sync.dma_start(out=tab_w[:].bitcast(I32), in_=tab_words[0].rearrange("p t i -> p (t i)").bitcast(I32))
-        load_scale_rows(nc.sync, w4_s_raw[:, K : 2 * K], wd_scales[0])
+        load_scale_rows(nc.sync, w4_s_raw[:, 0:K], wa_scales[0])
         nc.sync.dma_start(x_lists[:], offs2)
         nc.sync.dma_start(out=wgt[0][:], in_=wgt2[:, 0:HALF])
         nc.sync.dma_start(out=x_planes[0][:], in_=x_rows[:, 0, :])
         nc.sync.dma_start(out=wgt[1][:], in_=wgt2[:, HALF:J])
         nc.sync.dma_start(out=x_planes[1][:], in_=x_rows[:, 1, :])
+        load_scale_rows(nc.sync, w4_s_raw[:, K : 2 * K], wd_scales[0])
         nc.sync.dma_start(out=x_planes[2][:], in_=x_rows[:, 2, :])
         nc.sync.dma_start(out=x_planes[3][:], in_=x_rows[:, 3, :])
 
@@ -75,10 +87,11 @@ def tile_list_htabg_mul_noneP_kernel(
         wb_bf = keep.tile([P, K * PACK], BF16, name="wb_bf", align_bytes=64)
         wb_w = keep.tile([P, K], U32, name="wb_w", align_bytes=64)
         wb_s = keep.tile([P, K], U8, name="wb_s", align_bytes=64)
-        wb_from = wb_raw[:].rearrange("p i (m t) -> p m i t", t=PACK)
         wb_to = wb_bf[:].rearrange("p (t m i) -> p m i t", t=PACK, i=PACK)
-        nc.vector.tensor_copy(out=wb_to[:, :, :, 0:2], in_=wb_from[:, :, :, 0:2])
-        nc.scalar.copy(out=wb_to[:, :, :, 2:4], in_=wb_from[:, :, :, 2:4])
+        for h in range(2):
+            nc.scalar.copy(
+                out=wb_to[:, h * P // 2 : (h + 1) * P // 2], in_=wb_raw[h][:].rearrange("p i (m t) -> p m i t", t=PACK)
+            )
 
         w4_w = keep.tile([P, 4 * K], U8, name="w4_w", align_bytes=64)
         w4_s = [keep.tile([P, K], U8, name="w4_s%d" % w, align_bytes=64) for w in range(2)]
@@ -86,6 +99,13 @@ def tile_list_htabg_mul_noneP_kernel(
             out=w4_w[:].bitcast(U16).rearrange("p (w t m) -> p w t m", w=2, t=PACK),
             in_=w4_w_raw[:].bitcast(U16).rearrange("p (w m t) -> p w t m", w=2, t=PACK),
         )
+        nc.vector.quantize_mx(out=wb_w[:].bitcast(E4M3), scales=wb_s[:], in_=wb_bf[:])
+
+        v_w = keep.tile([P, J], U32, name="v_w", align_bytes=64)
+        for j0, n in cuts(V_WIDTHS):
+            nc.vector.tensor_copy(
+                v_w[:, j0 : j0 + n], tab_w[:].indirect(tab_list[:, j0 // STRIPE : (j0 + n) // STRIPE])
+            )
 
         def deal_scales(w):
             nc.vector.tensor_copy(
@@ -93,28 +113,20 @@ def tile_list_htabg_mul_noneP_kernel(
                 in_=w4_s_raw[:, w * K : (w + 1) * K].rearrange("p (m t) -> p t m", t=PACK),
             )
 
-        deal_scales(0)
-        nc.vector.quantize_mx(out=wb_w[:].bitcast(E4M3), scales=wb_s[:], in_=wb_bf[:])
-
-        v_w = keep.tile([P, J], U32, name="v_w", align_bytes=64)
-        for h in range(2):
-            nc.vector.tensor_copy(
-                v_w[:, h * HALF : (h + 1) * HALF],
-                tab_w[:].indirect(tab_list[:, h * HALF // STRIPE : (h + 1) * HALF // STRIPE]),
-            )
-
-        deal_scales(1)
-
-        picked = [[keep.tile([P, 2, HALF], F32, name="picked%d_%d" % (u, h)) for h in range(2)] for u in range(2)]
-        x_bf = [keep.tile([P, CHUNK * PACK], BF16, name="x_bf%d" % c, align_bytes=64) for c in range(J // CHUNK)]
+        late = keep.tile([P, 2 * HALF + 2 * BANK], F32, name="late", align_bytes=64)
+        picked = [[keep.tile([P, 2, HALF], F32, name="picked%d_%d" % (u, h))[:] for h in range(2 - u)] for u in range(2)]
+        picked[1].append(late[:, 0 : 2 * HALF].rearrange("p (e j) -> p e j", e=2))
+        x_cuts = cuts(X_WIDTHS)
+        x_bf = [late[:, HALF : HALF + 2 * BANK].bitcast(BF16)]
+        x_bf.extend(keep.tile([P, n * PACK], BF16, name="x_bf%d" % j0, align_bytes=64)[:] for j0, n in x_cuts[1:])
 
         def weave(u, c):
-            h, c0 = divmod(c * CHUNK, HALF)
+            j0, n = x_cuts[c]
+            h, c0 = divmod(j0, HALF)
             nc.scalar.copy(
-                out=x_bf[c][:].rearrange("p (j u e) -> p j u e", u=2, e=2)[:, :, u, :],
-                in_=picked[u][h][:, :, c0 : c0 + CHUNK].rearrange("p e j -> p j e"),
+                out=x_bf[c].rearrange("p (j u e) -> p j u e", u=2, e=2)[:, :, u, :],
+                in_=picked[u][h][:, :, c0 : c0 + n].rearrange("p e j -> p j e"),
             )
-
 
         def gather(i, j0, n):
             h, c0 = divmod(j0, HALF)
@@ -128,6 +140,7 @@ def tile_list_htabg_mul_noneP_kernel(
         for i in range(2):
             for h in range(2):
                 gather(i, h * HALF, HALF)
+            deal_scales(i)
 
         def fp4_slice(w, t):
             c0 = w * K + t * P
@@ -144,86 +157,117 @@ def tile_list_htabg_mul_noneP_kernel(
                     start=True, stop=True,
                 )
 
-        yb = [keep.tile([P, BANK, PACK], F32, name="yb%d" % b) for b in range(J // BANK)]
+        yb = [late[:, HALF + 2 * BANK :].rearrange("p (j t) -> p j t", t=PACK)]
+        yb.extend(keep.tile([P, BANK, PACK], F32, name="yb%d" % b)[:] for b in range(1, J // BANK))
         for b in range(J // BANK):
             cols = slice(b * BANK, (b + 1) * BANK)
             bank = psum.tile([P, PACK, BANK], F32, name="out_bank", bufs=5)
             product(bank, wb_slice, v_w[:, cols], v_s[:, cols])
-            nc.scalar.copy(out=yb[b][:], in_=bank[:].rearrange("p t j -> p j t"))
+            nc.scalar.copy(out=yb[b], in_=bank[:].rearrange("p t j -> p j t"))
 
-        for c in range(J // CHUNK):
-            weave(0, c)
+        weave(0, 0)
         for h in range(2):
             gather(2, h * HALF, HALF)
-        for c in range(J // CHUNK):
-            gather(3, c * CHUNK, CHUNK)
 
         y_s = keep.tile([P, J], U8, name="y_s", align_bytes=64)
+        y_w = keep.tile([P, J], U32, name="y_w", align_bytes=64)
         y_rows = out_0.rearrange("(p t) j -> p t j", t=PACK)
         y_words = out_1[0].rearrange("p j i -> p (j i)").bitcast(I32)
-        nchunks = J // CHUNK
-        x_q, h_bf, h_q, y_bf, y_fs = {}, {}, {}, {}, {}
+        h_cuts, y_cuts, q_cuts, w_cuts = cuts(H_WIDTHS), cuts(Y_WIDTHS), cuts(Q_WIDTHS), cuts(W_WIDTHS)
+        h_bf = [keep.tile([P, n * PACK], BF16, name="h_bf%d" % j0, align_bytes=64) for j0, n in h_cuts]
+        y_f = [keep.tile([P, PACK, n], F32, name="y_f%d" % j0) for j0, n in y_cuts]
+        y_bf = [keep.tile([P, n * PACK], BF16, name="y_bf%d" % j0, align_bytes=64) for j0, n in q_cuts]
+        x_q, h_q = {}, {}
 
-        def quantised(name, src):
-            words = keep.tile([P, CHUNK], U32, name=name + "_w", align_bytes=64)
-            scales = keep.tile([P, CHUNK], U8, name=name + "_s", align_bytes=64)
-            nc.vector.quantize_mx(out=words[:].bitcast(E4M3), scales=scales[:], in_=src[:])
+        def holder(pieces, j):
+            for c, (j0, n) in enumerate(pieces):
+                if j0 <= j < j0 + n:
+                    return c, j - j0, j + BANK == j0 + n
+
+        def quantised(name, src, n):
+            words = keep.tile([P, n], U32, name=name + "_w", align_bytes=64)
+            scales = keep.tile([P, n], U8, name=name + "_s", align_bytes=64)
+            nc.vector.quantize_mx(out=words[:].bitcast(E4M3), scales=scales[:], in_=src)
             return words, scales
 
-        def stage_x(c):
+        def finish_x(c):
+            gather(3, *x_cuts[c])
+            if c:
+                weave(0, c)
             weave(1, c)
-            x_q[c] = quantised("x%d" % c, x_bf[c])
 
-        def stage_h(c):
+        def quantise_x(c):
+            x_q[c] = quantised("x%d" % c, x_bf[c], x_cuts[c][1])
+
+        def stage_h(j):
+            c, c0, whole = holder(x_cuts, j)
             words, scales = x_q[c]
-            h_bf[c] = keep.tile([P, CHUNK * PACK], BF16, name="h_bf%d" % c, align_bytes=64)
-            for u in range(CHUNK // BANK):
-                cols = slice(u * BANK, (u + 1) * BANK)
-                bank = psum.tile([P, PACK, BANK], F32, name="ya_bank", bufs=3)
-                product(bank, lambda t: fp4_slice(0, t), words[:, cols], scales[:, cols])
-                nc.vector.tensor_tensor(
-                    h_bf[c][:, u * BANK * PACK : (u + 1) * BANK * PACK].rearrange("p (j t) -> p j t", t=PACK),
-                    bank[:].rearrange("p t j -> p j t"),
-                    yb[c * (CHUNK // BANK) + u][:],
-                    MULT,
-                )
+            bank = psum.tile([P, PACK, BANK], F32, name="ya_bank", bufs=3)
+            product(bank, lambda t: fp4_slice(0, t), words[:, c0 : c0 + BANK], scales[:, c0 : c0 + BANK])
+            c, c0, whole = holder(h_cuts, j)
+            nc.vector.tensor_tensor(
+                h_bf[c][:, c0 * PACK : (c0 + BANK) * PACK].rearrange("p (j t) -> p j t", t=PACK),
+                bank[:].rearrange("p t j -> p j t"),
+                yb[j // BANK],
+                MULT,
+            )
 
-        def stage_hq(c):
-            h_q[c] = quantised("h%d" % c, h_bf[c])
+        def finish_h(j):
+            c, c0, whole = holder(h_cuts, j)
+            if whole:
+                h_q[c] = quantised("h%d" % c, h_bf[c][:], h_cuts[c][1])
+                for jj in range(h_cuts[c][0], j + BANK, BANK):
+                    stage_y(jj)
 
-        def stage_y(c):
+        def stage_y(j):
+            c, c0, whole = holder(h_cuts, j)
             words, scales = h_q[c]
-            y_f = keep.tile([P, PACK, CHUNK], F32, name="y_f%d" % c)
-            y_fs[c] = y_f
-            y_bf[c] = keep.tile([P, CHUNK * PACK], BF16, name="y_bf%d" % c, align_bytes=64)
-            for u in range(CHUNK // BANK):
-                cols = slice(u * BANK, (u + 1) * BANK)
-                bank = psum.tile([P, PACK, BANK], F32, name="out_bank", bufs=5)
-                product(bank, lambda t: fp4_slice(1, t), words[:, cols], scales[:, cols])
-                nc.scalar.copy(out=y_f[:, :, cols], in_=bank[:])
-                if c >= nchunks - SCALAR_ROUNDS:
-                    nc.scalar.copy(
-                        out=y_bf[c][:, u * BANK * PACK : (u + 1) * BANK * PACK].rearrange("p (j t) -> p j t", t=PACK),
-                        in_=bank[:].rearrange("p t j -> p j t"),
-                    )
-            nc.sync.dma_start(out=y_rows[:, :, c * CHUNK : (c + 1) * CHUNK], in_=y_f[:])
+            bank = psum.tile([P, PACK, BANK], F32, name="out_bank", bufs=5)
+            product(bank, lambda t: fp4_slice(1, t), words[:, c0 : c0 + BANK], scales[:, c0 : c0 + BANK])
+            c, c0, whole = holder(y_cuts, j)
+            q, q0, q_whole = holder(q_cuts, j)
+            rounded = y_bf[q][:, q0 * PACK : (q0 + BANK) * PACK]
+            if j // BANK in ROUND_FIRST:
+                nc.scalar.copy(out=rounded.rearrange("p (j t) -> p j t", t=PACK), in_=bank[:].rearrange("p t j -> p j t"))
+            nc.scalar.copy(out=y_f[c][:, :, c0 : c0 + BANK], in_=bank[:])
+            if whole:
+                j0, n = y_cuts[c]
+                nc.sync.dma_start(out=y_rows[:, :, j0 : j0 + n], in_=y_f[c][:])
+            if j // BANK not in ROUND_FIRST and j // BANK not in VECTOR_ROUNDS:
+                nc.scalar.copy(out=rounded.rearrange("p (j t) -> p j t", t=PACK), in_=bank[:].rearrange("p t j -> p j t"))
 
-        def stage_yq(c):
-            if c < nchunks - SCALAR_ROUNDS:
+        def stage_planes(j):
+            q, q0, q_whole = holder(q_cuts, j)
+            if j // BANK in VECTOR_ROUNDS:
+                c, c0, whole = holder(y_cuts, j)
                 nc.vector.tensor_copy(
-                    out=y_bf[c][:].rearrange("p (g e t) -> p g t e", e=4, t=PACK),
-                    in_=y_fs[c][:].rearrange("p t (g e) -> p g t e", e=4),
+                    out=y_bf[q][:, q0 * PACK : (q0 + BANK) * PACK].rearrange("p (g e t) -> p g t e", e=4, t=PACK),
+                    in_=y_f[c][:, :, c0 : c0 + BANK].rearrange("p t (g e) -> p g t e", e=4),
                 )
-            cols = slice(c * CHUNK, (c + 1) * CHUNK)
-            words = keep.tile([P, CHUNK], U32, name="y_w%d" % c, align_bytes=64)
-            nc.vector.quantize_mx(out=words[:].bitcast(E4M3), scales=y_s[:, cols], in_=y_bf[c][:])
-            nc.sync.dma_start(out=y_words[:, cols], in_=words[:].bitcast(I32))
+            if q_whole:
+                j0, n = q_cuts[q]
+                nc.vector.quantize_mx(out=y_w[:, j0 : j0 + n].bitcast(E4M3), scales=y_s[:, j0 : j0 + n], in_=y_bf[q][:])
+            w, w0, w_whole = holder(w_cuts, j)
+            if w_whole:
+                j0, n = w_cuts[w]
+                nc.sync.dma_start(out=y_words[:, j0 : j0 + n], in_=y_w[:, j0 : j0 + n].bitcast(I32))
 
-        stages = [(stage_x, 0), (stage_y, 4), (stage_hq, 3), (stage_h, 2), (stage_yq, 6)]
-        for step in range(nchunks + 6):
-            for stage, lag in stages:
-                if 0 <= step - lag < nchunks:
-                    stage(step - lag)
+        last = len(x_cuts) - 1
+        for c in range(2):
+            finish_x(c)
+            quantise_x(c)
+        for c in range(2, last):
+            finish_x(c)
+        for j in range(0, J, BANK):
+            c, c0, whole = holder(x_cuts, j)
+            if whole and 1 <= c < last:
+                quantise_x(c + 1)
+            stage_h(j)
+            if j == 0:
+                finish_x(last)
+            finish_h(j)
+        for j in range(0, J, BANK):
+            stage_planes(j)
         for q in range(4):
             queue = nc.scalar if q % 2 else nc.sync
             queue.dma_start(

@@ -54,20 +54,17 @@ def tile_list_htabg_mul_noneP_kernel(
         w4_w_raw = keep.tile([P, 4 * K], U8, name="w4_w_raw", align_bytes=64)
         wgt = [keep.tile([P, HALF], F32, name="wgt%d" % h) for h in range(2)]
         x_planes = [keep.tile([P, T], F32, name="x_plane%d" % i) for i in range(PACK)]
-        wb_raw = [keep.tile([P, PACK, K // 2], F32, name="wb_raw%d" % h) for h in range(2)]
+        wb_raw = keep.tile([P, PACK, K], F32, name="wb_raw")
 
+        nc.gpsimd.memset(tab_s[:].bitcast(I32), 0)
         nc.gpsimd.memset(w4_s_raw[:].bitcast(I32), 0)
 
         x_rows = xT.rearrange("(p i) t -> p i t", i=PACK)
         wb_rows = wb.rearrange("(p i) r -> p i r", i=PACK)
         nc.sync.dma_start(tab_list[:], offs)
-        for q in range(4):
-            nc.sync.dma_start(
-                out=tab_s[32 * q : 32 * (q + 1), :].bitcast(I32),
-                in_=tab_scales[0, 4 * q : 4 * q + 4, :].bitcast(I32).partition_broadcast(8),
-            )
-        nc.sync.dma_start(out=wb_raw[0][:], in_=wb_rows[:, :, 0 : K // 2])
-        nc.sync.dma_start(out=wb_raw[1][:], in_=wb_rows[:, :, K // 2 : K])
+        nc.sync.dma_start(out=wb_raw[:, 0:2, :], in_=wb_rows[:, 0:2, :])
+        load_scale_rows(nc.sync, tab_s, tab_scales[0])
+        nc.sync.dma_start(out=wb_raw[:, 2:4, :], in_=wb_rows[:, 2:4, :])
         nc.sync.dma_start(out=w4_w_raw[:, 0 : 2 * K].bitcast(I32), in_=wa_words[0].bitcast(I32))
         nc.sync.dma_start(out=w4_w_raw[:, 2 * K : 4 * K].bitcast(I32), in_=wd_words[0].bitcast(I32))
         nc.sync.dma_start(out=tab_w[:].bitcast(I32), in_=tab_words[0].rearrange("p t i -> p (t i)").bitcast(I32))
@@ -87,11 +84,10 @@ def tile_list_htabg_mul_noneP_kernel(
         wb_bf = keep.tile([P, K * PACK], BF16, name="wb_bf", align_bytes=64)
         wb_w = keep.tile([P, K], U32, name="wb_w", align_bytes=64)
         wb_s = keep.tile([P, K], U8, name="wb_s", align_bytes=64)
-        wb_to = wb_bf[:].rearrange("p (t m i) -> p m i t", t=PACK, i=PACK)
-        for h in range(2):
-            nc.scalar.copy(
-                out=wb_to[:, h * P // 2 : (h + 1) * P // 2], in_=wb_raw[h][:].rearrange("p i (m t) -> p m i t", t=PACK)
-            )
+        wb_to = wb_bf[:].rearrange("p (t m i) -> p m t i", t=PACK, i=PACK)
+        wb_from = wb_raw[:].rearrange("p i (m t) -> p m t i", t=PACK)
+        for u in range(2):
+            nc.scalar.copy(out=wb_to[:, :, :, 2 * u : 2 * u + 2], in_=wb_from[:, :, :, 2 * u : 2 * u + 2])
 
         w4_w = keep.tile([P, 4 * K], U8, name="w4_w", align_bytes=64)
         w4_s = [keep.tile([P, K], U8, name="w4_s%d" % w, align_bytes=64) for w in range(2)]

@@ -1,6 +1,7 @@
 from contextlib import ExitStack
 
 import concourse.mybir as mybir
+from concourse.masks import make_identity
 
 K, T, J = 512, 2048, 1024
 FLOPS = 3 * 2 * K * K * J
@@ -57,10 +58,14 @@ def tile_list_htabg_mul_noneP_kernel(
         wb_raw = keep.tile([P, PACK, K], F32, name="wb_raw")
 
         nc.gpsimd.memset(tab_s[:].bitcast(I32), 0)
+        identity = keep.tile([P, P], F32, name="identity")
+        make_identity(nc, identity[:])
         nc.gpsimd.memset(w4_s_raw[:].bitcast(I32), 0)
+        wgt_rows = keep.tile([P, P], F32, name="wgt_rows")
 
         x_rows = xT.rearrange("(p i) t -> p i t", i=PACK)
         wb_rows = wb.rearrange("(p i) r -> p i r", i=PACK)
+        nc.sync.dma_start(out=wgt_rows[:], in_=wgt2[0:P:8, :].rearrange("a (b d) -> a b d", d=P))
         nc.sync.dma_start(tab_list[:], offs)
         nc.sync.dma_start(out=wb_raw[:, 0:2, :], in_=wb_rows[:, 0:2, :])
         load_scale_rows(nc.sync, tab_s, tab_scales[0])
@@ -70,13 +75,29 @@ def tile_list_htabg_mul_noneP_kernel(
         nc.sync.dma_start(out=tab_w[:].bitcast(I32), in_=tab_words[0].rearrange("p t i -> p (t i)").bitcast(I32))
         load_scale_rows(nc.sync, w4_s_raw[:, 0:K], wa_scales[0])
         nc.sync.dma_start(x_lists[:], offs2)
-        nc.sync.dma_start(out=wgt[0][:], in_=wgt2[:, 0:HALF])
         nc.sync.dma_start(out=x_planes[0][:], in_=x_rows[:, 0, :])
-        nc.sync.dma_start(out=wgt[1][:], in_=wgt2[:, HALF:J])
         nc.sync.dma_start(out=x_planes[1][:], in_=x_rows[:, 1, :])
         load_scale_rows(nc.sync, w4_s_raw[:, K : 2 * K], wd_scales[0])
         nc.sync.dma_start(out=x_planes[2][:], in_=x_rows[:, 2, :])
         nc.sync.dma_start(out=x_planes[3][:], in_=x_rows[:, 3, :])
+
+        spread = [keep.tile([P, PACK, P], F32, name="spread%d" % h) for h in range(2)]
+        for h in range(2):
+            bank = psum.tile([P, PACK, BANK], F32, name="ya_bank", bufs=3)
+            nc.tensor.transpose(bank[:, 0, :], wgt_rows[:], identity[:])
+            by_group = bank[:, 0, :].rearrange("d (g x) -> d x g", x=STRIPE)[:, PACK * h : PACK * (h + 1), :]
+            repeated = by_group.unsqueeze(3).to_broadcast([P, PACK, P // STRIPE, STRIPE])
+            spread_to = spread[h][:].rearrange("d b (g r) -> d b g r", r=STRIPE)
+            if h:
+                nc.scalar.copy(out=spread_to, in_=repeated)
+            else:
+                nc.vector.tensor_copy(out=spread_to, in_=repeated)
+
+        def finish_wgt(h):
+            bank = psum.tile([P, PACK, BANK], F32, name="out_bank", bufs=5)
+            for b in range(PACK):
+                nc.tensor.transpose(bank[:, b, :], spread[h][:, b, :], identity[:])
+            nc.scalar.copy(out=wgt[h][:], in_=bank[:].rearrange("p b d -> p (b d)"))
 
         v_s = keep.tile([P, J], U8, name="v_s", align_bytes=64)
         nc.vector.tensor_copy(v_s[:], tab_s[:].indirect(tab_list[:]))
@@ -88,6 +109,9 @@ def tile_list_htabg_mul_noneP_kernel(
         wb_from = wb_raw[:].rearrange("p i (m t) -> p m t i", t=PACK)
         for u in range(2):
             nc.scalar.copy(out=wb_to[:, :, :, 2 * u : 2 * u + 2], in_=wb_from[:, :, :, 2 * u : 2 * u + 2])
+
+        for h in range(2):
+            finish_wgt(h)
 
         w4_w = keep.tile([P, 4 * K], U8, name="w4_w", align_bytes=64)
         w4_s = [keep.tile([P, K], U8, name="w4_s%d" % w, align_bytes=64) for w in range(2)]

@@ -24,11 +24,12 @@ STRIPE = 16
 V_WIDTHS = [256, 768]
 X_WIDTHS = [128, 128, 256, 256, 256]
 H_WIDTHS = [128, 128, 256, 256, 128, 128]
-Y_WIDTHS = [128, 128, 256, 256, 128, 128]
+Y_WIDTHS = [128, 128, 128, 128, 128, 128, 128, 128]
 Q_WIDTHS = [256, 256, 256, 128, 128]
 W_WIDTHS = [512, 384, 128]
-VECTOR_ROUNDS = (4, 5, 6)
-ROUND_FIRST = (7,)
+VECTOR_ROUNDS = (3, 4, 5, 6, 7)
+ROUND_FIRST = ()
+PLANES_LAG = 6 * BANK
 
 
 def cuts(widths):
@@ -81,24 +82,6 @@ def tile_list_htabg_mul_noneP_kernel(
         nc.sync.dma_start(out=x_planes[2][:], in_=x_rows[:, 2, :])
         nc.sync.dma_start(out=x_planes[3][:], in_=x_rows[:, 3, :])
 
-        spread = [keep.tile([P, PACK, P], F32, name="spread%d" % h) for h in range(2)]
-        for h in range(2):
-            bank = psum.tile([P, PACK, BANK], F32, name="ya_bank", bufs=3)
-            nc.tensor.transpose(bank[:, 0, :], wgt_rows[:], identity[:])
-            by_group = bank[:, 0, :].rearrange("d (g x) -> d x g", x=STRIPE)[:, PACK * h : PACK * (h + 1), :]
-            repeated = by_group.unsqueeze(3).to_broadcast([P, PACK, P // STRIPE, STRIPE])
-            spread_to = spread[h][:].rearrange("d b (g r) -> d b g r", r=STRIPE)
-            if h:
-                nc.scalar.copy(out=spread_to, in_=repeated)
-            else:
-                nc.vector.tensor_copy(out=spread_to, in_=repeated)
-
-        def finish_wgt(h):
-            bank = psum.tile([P, PACK, BANK], F32, name="out_bank", bufs=5)
-            for b in range(PACK):
-                nc.tensor.transpose(bank[:, b, :], spread[h][:, b, :], identity[:])
-            nc.scalar.copy(out=wgt[h][:], in_=bank[:].rearrange("p b d -> p (b d)"))
-
         v_s = keep.tile([P, J], U8, name="v_s", align_bytes=64)
         nc.vector.tensor_copy(v_s[:], tab_s[:].indirect(tab_list[:]))
 
@@ -109,6 +92,21 @@ def tile_list_htabg_mul_noneP_kernel(
         wb_from = wb_raw[:].rearrange("p i (m t) -> p m t i", t=PACK)
         for u in range(2):
             nc.scalar.copy(out=wb_to[:, :, :, 2 * u : 2 * u + 2], in_=wb_from[:, :, :, 2 * u : 2 * u + 2])
+
+        spread = [keep.tile([P, PACK, P], F32, name="spread%d" % h) for h in range(2)]
+        for h in range(2):
+            bank = psum.tile([P, PACK, BANK], F32, name="ya_bank", bufs=3)
+            nc.tensor.transpose(bank[:, 0, :], wgt_rows[:], identity[:])
+            by_group = bank[:, 0, :].rearrange("d (g x) -> d x g", x=STRIPE)[:, PACK * h : PACK * (h + 1), :]
+            repeated = by_group.unsqueeze(3).to_broadcast([P, PACK, P // STRIPE, STRIPE])
+            spread_to = spread[h][:].rearrange("d b (g r) -> d b g r", r=STRIPE)
+            nc.scalar.copy(out=spread_to, in_=repeated)
+
+        def finish_wgt(h):
+            bank = psum.tile([P, PACK, BANK], F32, name="out_bank", bufs=5)
+            for b in range(PACK):
+                nc.tensor.transpose(bank[:, b, :], spread[h][:, b, :], identity[:])
+            nc.scalar.copy(out=wgt[h][:], in_=bank[:].rearrange("p b d -> p (b d)"))
 
         for h in range(2):
             finish_wgt(h)
@@ -286,7 +284,9 @@ def tile_list_htabg_mul_noneP_kernel(
             if j == 0:
                 finish_x(last)
             finish_h(j)
-        for j in range(0, J, BANK):
+            if j >= PLANES_LAG:
+                stage_planes(j - PLANES_LAG)
+        for j in range(J - PLANES_LAG, J, BANK):
             stage_planes(j)
         for q in range(4):
             queue = nc.scalar if q % 2 else nc.sync

@@ -111,13 +111,19 @@ def tile_list_htabg_mul_noneP_kernel(
         for h in range(2):
             finish_wgt(h)
 
-        w4_w = keep.tile([P, 4 * K], U8, name="w4_w", align_bytes=64)
+        wa_w = keep.tile([P, 2 * K], U8, name="wa_w", align_bytes=64)
         w4_s = [keep.tile([P, K], U8, name="w4_s%d" % w, align_bytes=64) for w in range(2)]
         nc.vector.tensor_copy(
-            out=w4_w[:].bitcast(U16).rearrange("p (w t m) -> p w t m", w=2, t=PACK),
-            in_=w4_w_raw[:].bitcast(U16).rearrange("p (w m t) -> p w t m", w=2, t=PACK),
+            out=wa_w[:].bitcast(U16).rearrange("p (t m) -> p t m", t=PACK),
+            in_=w4_w_raw[:, 0 : 2 * K].bitcast(U16).rearrange("p (m t) -> p t m", t=PACK),
         )
         nc.vector.quantize_mx(out=wb_w[:].bitcast(E4M3), scales=wb_s[:], in_=wb_bf[:])
+        wd_w = keep.tile([P, 2 * K], U8, name="wb_bf", align_bytes=64)
+        nc.gpsimd.tensor_copy(
+            out=wd_w[:].rearrange("p (t m b) -> p t m b", t=PACK, b=2),
+            in_=w4_w_raw[:, 2 * K : 4 * K].rearrange("p (m t b) -> p t m b", t=PACK, b=2),
+        )
+        w4_w = [wa_w, wd_w]
 
         v_w = keep.tile([P, J], U32, name="v_w", align_bytes=64)
         for j0, n in cuts(V_WIDTHS):
@@ -126,7 +132,7 @@ def tile_list_htabg_mul_noneP_kernel(
             )
 
         def deal_scales(w):
-            nc.vector.tensor_copy(
+            (nc.vector if w else nc.gpsimd).tensor_copy(
                 out=w4_s[w][:].rearrange("p (t m) -> p t m", t=PACK),
                 in_=w4_s_raw[:, w * K : (w + 1) * K].rearrange("p (m t) -> p t m", t=PACK),
             )
@@ -161,8 +167,7 @@ def tile_list_htabg_mul_noneP_kernel(
             deal_scales(i)
 
         def fp4_slice(w, t):
-            c0 = w * K + t * P
-            return w4_w[:, 2 * c0 : 2 * (c0 + P)].bitcast(E2M1), w4_s[w][:, t * P : (t + 1) * P]
+            return w4_w[w][:, 2 * t * P : 2 * (t + 1) * P].bitcast(E2M1), w4_s[w][:, t * P : (t + 1) * P]
 
         def wb_slice(t):
             return wb_w[:, t * P : (t + 1) * P].bitcast(E4M3), wb_s[:, t * P : (t + 1) * P]

@@ -1,7 +1,6 @@
 from contextlib import ExitStack
 
 import concourse.mybir as mybir
-from concourse.masks import make_identity
 
 K, T, J = 512, 2048, 1024
 FLOPS = 3 * 2 * K * K * J
@@ -23,11 +22,11 @@ HALF = 512
 STRIPE = 16
 V_WIDTHS = [256, 768]
 X_WIDTHS = [128, 128, 256, 256, 256]
-H_WIDTHS = [128, 128, 256, 256, 128, 128]
+H_WIDTHS = [128, 128, 128, 128, 128, 128, 128, 128]
 Y_WIDTHS = [128, 128, 128, 128, 128, 128, 128, 128]
 Q_WIDTHS = [256, 256, 256, 128, 128]
 W_WIDTHS = [512, 384, 128]
-VECTOR_ROUNDS = (3, 4, 5, 6, 7)
+VECTOR_ROUNDS = (2, 3, 4, 5, 6)
 ROUND_FIRST = ()
 PLANES_LAG = 6 * BANK
 
@@ -54,13 +53,21 @@ def tile_list_htabg_mul_noneP_kernel(
         tab_w = keep.tile([P, T], U32, name="tab_w", align_bytes=64)
         w4_s_raw = keep.tile([P, 2 * K], U8, name="w4_s_raw", align_bytes=64)
         w4_w_raw = keep.tile([P, 4 * K], U8, name="w4_w_raw", align_bytes=64)
-        wgt = [keep.tile([P, HALF], F32, name="wgt%d" % h) for h in range(2)]
         x_planes = [keep.tile([P, T], F32, name="x_plane%d" % i) for i in range(PACK)]
         wb_raw = keep.tile([P, PACK, K], F32, name="wb_raw")
 
         nc.gpsimd.memset(tab_s[:].bitcast(I32), 0)
         identity = keep.tile([P, P], F32, name="identity")
-        make_identity(nc, identity[:])
+        ones = keep.tile([P, 32], F32, name="ones")
+        count = keep.tile([P, 32], F32, name="count", align_bytes=64)
+        count_down = keep.tile([P, 32], F32, name="count_down", align_bytes=64)
+        nc.vector.memset(ones[:], 1.0)
+        nc.vector.memset(identity[:], 0.0)
+        nc.vector.tensor_tensor_scan(count[:], ones[:], ones[:], 0.0, MULT, mybir.AluOpType.add)
+        nc.vector.transpose(count_down[:], count[:])
+        for q in range(4):
+            rows = slice(32 * q, 32 * (q + 1))
+            nc.vector.tensor_tensor(identity[rows, rows], count[rows, :], count_down[rows, :], mybir.AluOpType.is_equal)
         nc.gpsimd.memset(w4_s_raw[:].bitcast(I32), 0)
         wgt_rows = keep.tile([P, P], F32, name="wgt_rows")
 
@@ -71,16 +78,28 @@ def tile_list_htabg_mul_noneP_kernel(
         nc.sync.dma_start(out=wb_raw[:, 0:2, :], in_=wb_rows[:, 0:2, :])
         load_scale_rows(nc.sync, tab_s, tab_scales[0])
         nc.sync.dma_start(out=wb_raw[:, 2:4, :], in_=wb_rows[:, 2:4, :])
-        nc.sync.dma_start(out=w4_w_raw[:, 0 : 2 * K].bitcast(I32), in_=wa_words[0].bitcast(I32))
-        nc.sync.dma_start(out=w4_w_raw[:, 2 * K : 4 * K].bitcast(I32), in_=wd_words[0].bitcast(I32))
         nc.sync.dma_start(out=tab_w[:].bitcast(I32), in_=tab_words[0].rearrange("p t i -> p (t i)").bitcast(I32))
-        load_scale_rows(nc.sync, w4_s_raw[:, 0:K], wa_scales[0])
+        nc.sync.dma_start(out=w4_w_raw[:, 0 : 2 * K].bitcast(I32), in_=wa_words[0].bitcast(I32))
         nc.sync.dma_start(x_lists[:], offs2)
+        load_scale_rows(nc.sync, w4_s_raw[:, 0:K], wa_scales[0])
         nc.sync.dma_start(out=x_planes[0][:], in_=x_rows[:, 0, :])
         nc.sync.dma_start(out=x_planes[1][:], in_=x_rows[:, 1, :])
+        nc.sync.dma_start(out=w4_w_raw[:, 2 * K : 4 * K].bitcast(I32), in_=wd_words[0].bitcast(I32))
         load_scale_rows(nc.sync, w4_s_raw[:, K : 2 * K], wd_scales[0])
         nc.sync.dma_start(out=x_planes[2][:], in_=x_rows[:, 2, :])
         nc.sync.dma_start(out=x_planes[3][:], in_=x_rows[:, 3, :])
+
+        bank = psum.tile([P, PACK, BANK], F32, name="ya_bank", bufs=3)
+        nc.tensor.transpose(bank[:, 0, :], wgt_rows[:], identity[:])
+        turned = keep.tile([P, P], F32, name="turned")
+        nc.scalar.copy(out=turned[:], in_=bank[:, 0, :])
+        spread = [keep.tile([P, PACK, P], F32, name="spread%d" % h) for h in range(2)]
+        for h in range(2):
+            by_group = turned[:].rearrange("d (g x) -> d x g", x=STRIPE)[:, PACK * h : PACK * (h + 1), :]
+            nc.gpsimd.tensor_copy(
+                out=spread[h][:].rearrange("d b (g r) -> d b g r", r=STRIPE),
+                in_=by_group.unsqueeze(3).to_broadcast([P, PACK, P // STRIPE, STRIPE]),
+            )
 
         v_s = keep.tile([P, J], U8, name="v_s", align_bytes=64)
         nc.vector.tensor_copy(v_s[:], tab_s[:].indirect(tab_list[:]))
@@ -90,52 +109,47 @@ def tile_list_htabg_mul_noneP_kernel(
         wb_s = keep.tile([P, K], U8, name="wb_s", align_bytes=64)
         wb_to = wb_bf[:].rearrange("p (t m i) -> p m t i", t=PACK, i=PACK)
         wb_from = wb_raw[:].rearrange("p i (m t) -> p m t i", t=PACK)
-        for u in range(2):
-            nc.scalar.copy(out=wb_to[:, :, :, 2 * u : 2 * u + 2], in_=wb_from[:, :, :, 2 * u : 2 * u + 2])
-
-        spread = [keep.tile([P, PACK, P], F32, name="spread%d" % h) for h in range(2)]
-        for h in range(2):
-            bank = psum.tile([P, PACK, BANK], F32, name="ya_bank", bufs=3)
-            nc.tensor.transpose(bank[:, 0, :], wgt_rows[:], identity[:])
-            by_group = bank[:, 0, :].rearrange("d (g x) -> d x g", x=STRIPE)[:, PACK * h : PACK * (h + 1), :]
-            repeated = by_group.unsqueeze(3).to_broadcast([P, PACK, P // STRIPE, STRIPE])
-            spread_to = spread[h][:].rearrange("d b (g r) -> d b g r", r=STRIPE)
-            nc.scalar.copy(out=spread_to, in_=repeated)
+        nc.scalar.copy(out=wb_to[:, :, :, 0:2], in_=wb_from[:, :, :, 0:2])
+        nc.scalar.copy(out=wb_to[:, 0 : P // 2, :, 2:4], in_=wb_from[:, 0 : P // 2, :, 2:4])
+        nc.gpsimd.tensor_scalar(
+            wb_to[:, P // 2 :, :, 2:4], wb_from[:, P // 2 :, :, 2:4], 1.0, 0.0, MULT, mybir.AluOpType.add
+        )
 
         def finish_wgt(h):
             bank = psum.tile([P, PACK, BANK], F32, name="out_bank", bufs=5)
             for b in range(PACK):
                 nc.tensor.transpose(bank[:, b, :], spread[h][:, b, :], identity[:])
-            nc.scalar.copy(out=wgt[h][:], in_=bank[:].rearrange("p b d -> p (b d)"))
+            nc.scalar.copy(out=wgt[h], in_=bank[:].rearrange("p b d -> p (b d)"))
 
+        wgt_all = keep.tile([P, J], F32, name="wb_raw")
+        wgt = [wgt_all[:, h * HALF : (h + 1) * HALF] for h in range(2)]
         for h in range(2):
             finish_wgt(h)
 
-        wa_w = keep.tile([P, 2 * K], U8, name="wa_w", align_bytes=64)
-        w4_s = [keep.tile([P, K], U8, name="w4_s%d" % w, align_bytes=64) for w in range(2)]
-        nc.vector.tensor_copy(
-            out=wa_w[:].bitcast(U16).rearrange("p (t m) -> p t m", t=PACK),
-            in_=w4_w_raw[:, 0 : 2 * K].bitcast(U16).rearrange("p (m t) -> p t m", t=PACK),
-        )
         nc.vector.quantize_mx(out=wb_w[:].bitcast(E4M3), scales=wb_s[:], in_=wb_bf[:])
-        wd_w = keep.tile([P, 2 * K], U8, name="wb_bf", align_bytes=64)
+        wa_dealt = keep.tile([P, 3 * K], U8, name="wa_dealt", align_bytes=64)
         nc.gpsimd.tensor_copy(
-            out=wd_w[:].rearrange("p (t m b) -> p t m b", t=PACK, b=2),
-            in_=w4_w_raw[:, 2 * K : 4 * K].rearrange("p (m t b) -> p t m b", t=PACK, b=2),
+            out=wa_dealt[:, 0 : 2 * K].rearrange("p (t m b) -> p t m b", t=PACK, b=2),
+            in_=w4_w_raw[:, 0 : 2 * K].rearrange("p (m t b) -> p t m b", t=PACK, b=2),
         )
-        w4_w = [wa_w, wd_w]
+        nc.gpsimd.tensor_copy(
+            out=wa_dealt[:, 2 * K :].rearrange("p (t m) -> p t m", t=PACK),
+            in_=w4_s_raw[:, 0:K].rearrange("p (m t) -> p t m", t=PACK),
+        )
+        dealt = [wa_dealt]
 
-        v_w = keep.tile([P, J], U32, name="v_w", align_bytes=64)
+        v_w = keep.tile([P, J], U32, name="wb_bf", align_bytes=64)
         for j0, n in cuts(V_WIDTHS):
             nc.vector.tensor_copy(
                 v_w[:, j0 : j0 + n], tab_w[:].indirect(tab_list[:, j0 // STRIPE : (j0 + n) // STRIPE])
             )
 
-        def deal_scales(w):
-            (nc.vector if w else nc.gpsimd).tensor_copy(
-                out=w4_s[w][:].rearrange("p (t m) -> p t m", t=PACK),
-                in_=w4_s_raw[:, w * K : (w + 1) * K].rearrange("p (m t) -> p t m", t=PACK),
-            )
+        wd_dealt = keep.tile([P, 3 * K], U8, name="wd_dealt", align_bytes=64)
+        nc.vector.tensor_copy(
+            out=wd_dealt[:, 0 : 2 * K].bitcast(U16).rearrange("p (t m) -> p t m", t=PACK),
+            in_=w4_w_raw[:, 2 * K : 4 * K].bitcast(U16).rearrange("p (m t) -> p t m", t=PACK),
+        )
+        dealt.append(wd_dealt)
 
         late = keep.tile([P, 2 * HALF + 2 * BANK], F32, name="late", align_bytes=64)
         picked = [[keep.tile([P, 2, HALF], F32, name="picked%d_%d" % (u, h))[:] for h in range(2 - u)] for u in range(2)]
@@ -164,10 +178,14 @@ def tile_list_htabg_mul_noneP_kernel(
         for i in range(2):
             for h in range(2):
                 gather(i, h * HALF, HALF)
-            deal_scales(i)
+
+        nc.vector.tensor_copy(
+            out=wd_dealt[:, 2 * K :].rearrange("p (t m) -> p t m", t=PACK),
+            in_=w4_s_raw[:, K : 2 * K].rearrange("p (m t) -> p t m", t=PACK),
+        )
 
         def fp4_slice(w, t):
-            return w4_w[w][:, 2 * t * P : 2 * (t + 1) * P].bitcast(E2M1), w4_s[w][:, t * P : (t + 1) * P]
+            return dealt[w][:, 2 * t * P : 2 * (t + 1) * P].bitcast(E2M1), dealt[w][:, 2 * K + t * P : 2 * K + (t + 1) * P]
 
         def wb_slice(t):
             return wb_w[:, t * P : (t + 1) * P].bitcast(E4M3), wb_s[:, t * P : (t + 1) * P]

@@ -26,8 +26,8 @@ H_WIDTHS = [128, 128, 128, 128, 128, 128, 128, 128]
 Y_WIDTHS = [128, 128, 128, 128, 128, 128, 128, 128]
 Q_WIDTHS = [256, 256, 256, 128, 128]
 W_WIDTHS = [512, 384, 128]
-VECTOR_ROUNDS = (2, 3, 4, 5, 6)
-ROUND_FIRST = ()
+VECTOR_ROUNDS = (3, 4, 5, 6)
+ROUND_FIRST = (7,)
 PLANES_LAG = 6 * BANK
 
 
@@ -41,6 +41,7 @@ def tile_list_htabg_mul_noneP_kernel(
     nc = tc.nc
     with ExitStack() as ctx:
         keep = ctx.enter_context(tc.tile_pool(name="keep", bufs=1))
+        reused = ctx.enter_context(tc.tile_pool(name="reused", bufs=1))
         psum = ctx.enter_context(tc.psum_pool(name="psum", bufs=1))
 
         def load_scale_rows(queue, plane, rows):
@@ -54,7 +55,7 @@ def tile_list_htabg_mul_noneP_kernel(
         w4_s_raw = keep.tile([P, 2 * K], U8, name="w4_s_raw", align_bytes=64)
         w4_w_raw = keep.tile([P, 4 * K], U8, name="w4_w_raw", align_bytes=64)
         x_planes = [keep.tile([P, T], F32, name="x_plane%d" % i) for i in range(PACK)]
-        wb_raw = keep.tile([P, PACK, K], F32, name="wb_raw")
+        wb_raw = reused.tile([P, PACK, K], F32, name="wb_raw", offset=0, align_bytes=64)
 
         nc.gpsimd.memset(tab_s[:].bitcast(I32), 0)
         identity = keep.tile([P, P], F32, name="identity")
@@ -121,7 +122,7 @@ def tile_list_htabg_mul_noneP_kernel(
                 nc.tensor.transpose(bank[:, b, :], spread[h][:, b, :], identity[:])
             nc.scalar.copy(out=wgt[h], in_=bank[:].rearrange("p b d -> p (b d)"))
 
-        wgt_all = keep.tile([P, J], F32, name="wb_raw")
+        wgt_all = reused.tile([P, J], F32, name="wgt_all", offset=0, align_bytes=64)
         wgt = [wgt_all[:, h * HALF : (h + 1) * HALF] for h in range(2)]
         for h in range(2):
             finish_wgt(h)
@@ -138,7 +139,7 @@ def tile_list_htabg_mul_noneP_kernel(
         )
         dealt = [wa_dealt]
 
-        v_w = keep.tile([P, J], U32, name="wb_bf", align_bytes=64)
+        v_w = reused.tile([P, J], U32, name="v_w", offset=4 * J, align_bytes=64)
         for j0, n in cuts(V_WIDTHS):
             nc.vector.tensor_copy(
                 v_w[:, j0 : j0 + n], tab_w[:].indirect(tab_list[:, j0 // STRIPE : (j0 + n) // STRIPE])
@@ -273,7 +274,8 @@ def tile_list_htabg_mul_noneP_kernel(
             nc.scalar.copy(out=y_f[c][:, :, c0 : c0 + BANK], in_=bank[:])
             if whole:
                 j0, n = y_cuts[c]
-                nc.sync.dma_start(out=y_rows[:, :, j0 : j0 + n], in_=y_f[c][:])
+                queue = nc.scalar if j0 + n == J else nc.sync
+                queue.dma_start(out=y_rows[:, :, j0 : j0 + n], in_=y_f[c][:])
             if j // BANK not in ROUND_FIRST and j // BANK not in VECTOR_ROUNDS:
                 nc.scalar.copy(out=rounded.rearrange("p (j t) -> p j t", t=PACK), in_=bank[:].rearrange("p t j -> p j t"))
 
@@ -312,7 +314,7 @@ def tile_list_htabg_mul_noneP_kernel(
         for j in range(J - PLANES_LAG, J, BANK):
             stage_planes(j)
         for q in range(4):
-            queue = nc.scalar if q % 2 else nc.sync
+            queue = nc.sync
             queue.dma_start(
                 out=out_2[0, 4 * q : 4 * q + 4, :].bitcast(I32), in_=y_s[32 * q : 32 * q + 4, :].bitcast(I32)
             )

@@ -20,7 +20,7 @@ PACK = 4
 BANK = 128
 HALF = 512
 STRIPE = 16
-V_WIDTHS = [256, 768]
+V_WIDTHS = [128, 128, 256, 512]
 X_WIDTHS = [128, 128, 256, 256, 256]
 H_WIDTHS = [128, 128, 128, 128, 128, 128, 128, 128]
 Y_WIDTHS = [128, 128, 128, 128, 128, 128, 128, 128]
@@ -28,6 +28,7 @@ Q_WIDTHS = [256, 256, 256, 128, 128]
 W_WIDTHS = [512, 384, 128]
 VECTOR_ROUNDS = (3, 4, 5, 6)
 ROUND_FIRST = (7,)
+WB_SPLIT = 48
 PLANES_LAG = 6 * BANK
 
 
@@ -53,7 +54,8 @@ def tile_list_htabg_mul_noneP_kernel(
         tab_s = keep.tile([P, T], U8, name="tab_s", align_bytes=64)
         tab_w = keep.tile([P, T], U32, name="tab_w", align_bytes=64)
         w4_s_raw = keep.tile([P, 2 * K], U8, name="w4_s_raw", align_bytes=64)
-        w4_w_raw = keep.tile([P, 4 * K], U8, name="w4_w_raw", align_bytes=64)
+        wa_raw = keep.tile([P, K], U16, name="wa_raw", align_bytes=64)
+        wd_raw = keep.tile([P, K], U16, name="wd_raw", align_bytes=64)
         x_planes = [keep.tile([P, T], F32, name="x_plane%d" % i) for i in range(PACK)]
         wb_raw = reused.tile([P, PACK, K], F32, name="wb_raw", offset=0, align_bytes=64)
 
@@ -80,12 +82,12 @@ def tile_list_htabg_mul_noneP_kernel(
         load_scale_rows(nc.sync, tab_s, tab_scales[0])
         nc.sync.dma_start(out=wb_raw[:, 2:4, :], in_=wb_rows[:, 2:4, :])
         nc.sync.dma_start(out=tab_w[:].bitcast(I32), in_=tab_words[0].rearrange("p t i -> p (t i)").bitcast(I32))
-        nc.sync.dma_start(out=w4_w_raw[:, 0 : 2 * K].bitcast(I32), in_=wa_words[0].bitcast(I32))
         nc.sync.dma_start(x_lists[:], offs2)
         load_scale_rows(nc.sync, w4_s_raw[:, 0:K], wa_scales[0])
         nc.sync.dma_start(out=x_planes[0][:], in_=x_rows[:, 0, :])
+        nc.sync.dma_start(out=wa_raw[:].bitcast(I32), in_=wa_words[0].bitcast(I32))
         nc.sync.dma_start(out=x_planes[1][:], in_=x_rows[:, 1, :])
-        nc.sync.dma_start(out=w4_w_raw[:, 2 * K : 4 * K].bitcast(I32), in_=wd_words[0].bitcast(I32))
+        nc.sync.dma_start(out=wd_raw[:].bitcast(I32), in_=wd_words[0].bitcast(I32))
         load_scale_rows(nc.sync, w4_s_raw[:, K : 2 * K], wd_scales[0])
         nc.sync.dma_start(out=x_planes[2][:], in_=x_rows[:, 2, :])
         nc.sync.dma_start(out=x_planes[3][:], in_=x_rows[:, 3, :])
@@ -111,9 +113,9 @@ def tile_list_htabg_mul_noneP_kernel(
         wb_to = wb_bf[:].rearrange("p (t m i) -> p m t i", t=PACK, i=PACK)
         wb_from = wb_raw[:].rearrange("p i (m t) -> p m t i", t=PACK)
         nc.scalar.copy(out=wb_to[:, :, :, 0:2], in_=wb_from[:, :, :, 0:2])
-        nc.scalar.copy(out=wb_to[:, 0 : P // 2, :, 2:4], in_=wb_from[:, 0 : P // 2, :, 2:4])
+        nc.scalar.copy(out=wb_to[:, 0:WB_SPLIT, :, 2:4], in_=wb_from[:, 0:WB_SPLIT, :, 2:4])
         nc.gpsimd.tensor_scalar(
-            wb_to[:, P // 2 :, :, 2:4], wb_from[:, P // 2 :, :, 2:4], 1.0, 0.0, MULT, mybir.AluOpType.add
+            wb_to[:, WB_SPLIT:, :, 2:4], wb_from[:, WB_SPLIT:, :, 2:4], 1.0, 0.0, MULT, mybir.AluOpType.add
         )
 
         def finish_wgt(h):
@@ -130,10 +132,6 @@ def tile_list_htabg_mul_noneP_kernel(
         nc.vector.quantize_mx(out=wb_w[:].bitcast(E4M3), scales=wb_s[:], in_=wb_bf[:])
         wa_dealt = keep.tile([P, 3 * K], U8, name="wa_dealt", align_bytes=64)
         nc.gpsimd.tensor_copy(
-            out=wa_dealt[:, 0 : 2 * K].rearrange("p (t m b) -> p t m b", t=PACK, b=2),
-            in_=w4_w_raw[:, 0 : 2 * K].rearrange("p (m t b) -> p t m b", t=PACK, b=2),
-        )
-        nc.gpsimd.tensor_copy(
             out=wa_dealt[:, 2 * K :].rearrange("p (t m) -> p t m", t=PACK),
             in_=w4_s_raw[:, 0:K].rearrange("p (m t) -> p t m", t=PACK),
         )
@@ -146,10 +144,6 @@ def tile_list_htabg_mul_noneP_kernel(
             )
 
         wd_dealt = keep.tile([P, 3 * K], U8, name="wd_dealt", align_bytes=64)
-        nc.vector.tensor_copy(
-            out=wd_dealt[:, 0 : 2 * K].bitcast(U16).rearrange("p (t m) -> p t m", t=PACK),
-            in_=w4_w_raw[:, 2 * K : 4 * K].bitcast(U16).rearrange("p (m t) -> p t m", t=PACK),
-        )
         dealt.append(wd_dealt)
 
         late = keep.tile([P, 2 * HALF + 2 * BANK], F32, name="late", align_bytes=64)
@@ -207,6 +201,11 @@ def tile_list_htabg_mul_noneP_kernel(
             product(bank, wb_slice, v_w[:, cols], v_s[:, cols])
             nc.scalar.copy(out=yb[b], in_=bank[:].rearrange("p t j -> p j t"))
 
+        for w, raw in enumerate((wa_raw, wd_raw)):
+            nc.scalar.copy(
+                out=dealt[w][:, 0 : 2 * K].bitcast(U16).rearrange("p (t m) -> p t m", t=PACK),
+                in_=raw[:].rearrange("p (m t) -> p t m", t=PACK),
+            )
         weave(0, 0)
         for h in range(2):
             gather(2, h * HALF, HALF)

@@ -25,7 +25,7 @@ X_WIDTHS = [128, 128, 256, 256, 256]
 H_WIDTHS = [128, 128, 128, 128, 128, 128, 128, 128]
 Y_WIDTHS = [128, 128, 128, 128, 128, 128, 128, 128]
 Q_WIDTHS = [256, 256, 256, 128, 128]
-W_WIDTHS = [512, 384, 128]
+W_WIDTHS = [256, 512, 256]
 VECTOR_ROUNDS = (3, 4, 5, 6)
 ROUND_FIRST = (7,)
 WB_SPLIT = 48

@@ -24,10 +24,10 @@ V_WIDTHS = [128, 128, 256, 512]
 X_WIDTHS = [128, 128, 256, 256, 256]
 H_WIDTHS = [128, 128, 128, 128, 128, 128, 128, 128]
 Y_WIDTHS = [128, 128, 128, 128, 128, 128, 128, 128]
-Q_WIDTHS = [256, 256, 256, 128, 128]
+Q_WIDTHS = [256, 256, 256, 256]
 W_WIDTHS = [256, 512, 256]
-VECTOR_ROUNDS = (3, 4, 5, 6)
-ROUND_FIRST = (7,)
+VECTOR_ROUNDS = (3, 4, 5, 6, 7)
+ROUND_FIRST = ()
 WB_SPLIT = 48
 PLANES_LAG = 6 * BANK
 
@@ -87,10 +87,10 @@ def tile_list_htabg_mul_noneP_kernel(
         nc.sync.dma_start(out=x_planes[0][:], in_=x_rows[:, 0, :])
         nc.sync.dma_start(out=wa_raw[:].bitcast(I32), in_=wa_words[0].bitcast(I32))
         nc.sync.dma_start(out=x_planes[1][:], in_=x_rows[:, 1, :])
-        nc.sync.dma_start(out=wd_raw[:].bitcast(I32), in_=wd_words[0].bitcast(I32))
         load_scale_rows(nc.sync, w4_s_raw[:, K : 2 * K], wd_scales[0])
         nc.sync.dma_start(out=x_planes[2][:], in_=x_rows[:, 2, :])
         nc.sync.dma_start(out=x_planes[3][:], in_=x_rows[:, 3, :])
+        nc.sync.dma_start(out=wd_raw[:].bitcast(I32), in_=wd_words[0].bitcast(I32))
 
         bank = psum.tile([P, PACK, BANK], F32, name="ya_bank", bufs=3)
         nc.tensor.transpose(bank[:, 0, :], wgt_rows[:], identity[:])
@@ -201,11 +201,13 @@ def tile_list_htabg_mul_noneP_kernel(
             product(bank, wb_slice, v_w[:, cols], v_s[:, cols])
             nc.scalar.copy(out=yb[b], in_=bank[:].rearrange("p t j -> p j t"))
 
-        for w, raw in enumerate((wa_raw, wd_raw)):
+        def deal_words(w, raw):
             nc.scalar.copy(
                 out=dealt[w][:, 0 : 2 * K].bitcast(U16).rearrange("p (t m) -> p t m", t=PACK),
                 in_=raw[:].rearrange("p (m t) -> p t m", t=PACK),
             )
+
+        deal_words(0, wa_raw)
         weave(0, 0)
         for h in range(2):
             gather(2, h * HALF, HALF)
@@ -300,6 +302,8 @@ def tile_list_htabg_mul_noneP_kernel(
             quantise_x(c)
         for c in range(2, last):
             finish_x(c)
+            if c == 2:
+                deal_words(1, wd_raw)
         for j in range(0, J, BANK):
             c, c0, whole = holder(x_cuts, j)
             if whole and 1 <= c < last:

@@ -24,10 +24,10 @@ V_WIDTHS = [128, 128, 256, 512]
 X_WIDTHS = [128, 128, 256, 256, 256]
 H_WIDTHS = [128, 128, 128, 128, 128, 128, 128, 128]
 Y_WIDTHS = [128, 128, 128, 128, 128, 128, 128, 128]
-Q_WIDTHS = [256, 256, 256, 256]
+Q_WIDTHS = [256, 256, 256, 128, 128]
 W_WIDTHS = [256, 512, 256]
-VECTOR_ROUNDS = (3, 4, 5, 6, 7)
-ROUND_FIRST = ()
+VECTOR_ROUNDS = (3, 4, 5, 6)
+ROUND_FIRST = (7,)
 WB_SPLIT = 48
 PLANES_LAG = 6 * BANK
 

@@ -24,12 +24,13 @@ V_WIDTHS = [128, 128, 256, 512]
 X_WIDTHS = [128, 128, 256, 256, 256]
 H_WIDTHS = [128, 128, 128, 128, 128, 128, 128, 128]
 Y_WIDTHS = [128, 128, 128, 128, 128, 128, 128, 128]
-Q_WIDTHS = [256, 256, 256, 128, 128]
+Q_WIDTHS = [128, 128, 128, 128, 256, 128, 128]
 W_WIDTHS = [256, 512, 256]
-VECTOR_ROUNDS = (3, 4, 5, 6)
+VECTOR_ROUNDS = (5, 6)
+GPSIMD_ROUNDS = (1, 3)
+PLANES_ORDER = (0, 1, 2, 4, 5, 3, 6, 7)
 ROUND_FIRST = (7,)
 WB_SPLIT = 48
-PLANES_LAG = 6 * BANK
 
 
 def cuts(widths):
@@ -217,10 +218,22 @@ def tile_list_htabg_mul_noneP_kernel(
         y_rows = out_0.rearrange("(p t) j -> p t j", t=PACK)
         y_words = out_1[0].rearrange("p j i -> p (j i)").bitcast(I32)
         h_cuts, y_cuts, q_cuts, w_cuts = cuts(H_WIDTHS), cuts(Y_WIDTHS), cuts(Q_WIDTHS), cuts(W_WIDTHS)
-        h_bf = [keep.tile([P, n * PACK], BF16, name="h_bf%d" % j0, align_bytes=64) for j0, n in h_cuts]
+        h_all = keep.tile([P, J * PACK], BF16, name="h_all", align_bytes=64)
+        h_bf = [h_all[:, j0 * PACK : (j0 + n) * PACK] for j0, n in h_cuts]
         y_f = [keep.tile([P, PACK, n], F32, name="y_f%d" % j0) for j0, n in y_cuts]
-        y_bf = [keep.tile([P, n * PACK], BF16, name="y_bf%d" % j0, align_bytes=64) for j0, n in q_cuts]
-        x_q, h_q = {}, {}
+        half = BANK * PACK // 2
+        y_bf = [
+            h_all[:, (2 * q + 5) * half : (2 * q + 7) * half] if q in GPSIMD_ROUNDS
+            else keep.tile([P, n * PACK], BF16, name="y_bf%d" % j0, align_bytes=64)[:]
+            for q, (j0, n) in enumerate(q_cuts)
+        ]
+
+        def round_half(b, u):
+            to = y_bf[b][:, u * half : (u + 1) * half].rearrange("p (g e t) -> p g t e", e=4, t=PACK)
+            src = y_f[b][:, :, u * BANK // 2 : (u + 1) * BANK // 2].rearrange("p t (g e) -> p g t e", e=4)
+            nc.gpsimd.tensor_scalar(to, src, 1.0, 0.0, MULT, mybir.AluOpType.add)
+
+        x_q, h_q, done = {}, {}, set()
 
         def holder(pieces, j):
             for c, (j0, n) in enumerate(pieces):
@@ -258,7 +271,10 @@ def tile_list_htabg_mul_noneP_kernel(
         def finish_h(j):
             c, c0, whole = holder(h_cuts, j)
             if whole:
-                h_q[c] = quantised("h%d" % c, h_bf[c][:], h_cuts[c][1])
+                h_q[c] = quantised("h%d" % c, h_bf[c], h_cuts[c][1])
+                for u in range(2):
+                    if c - 2 - u in GPSIMD_ROUNDS:
+                        round_half(c - 2 - u, u)
                 for jj in range(h_cuts[c][0], j + BANK, BANK):
                     stage_y(jj)
 
@@ -277,7 +293,7 @@ def tile_list_htabg_mul_noneP_kernel(
                 j0, n = y_cuts[c]
                 queue = nc.scalar if j0 + n == J else nc.sync
                 queue.dma_start(out=y_rows[:, :, j0 : j0 + n], in_=y_f[c][:])
-            if j // BANK not in ROUND_FIRST and j // BANK not in VECTOR_ROUNDS:
+            if j // BANK not in ROUND_FIRST + VECTOR_ROUNDS + GPSIMD_ROUNDS:
                 nc.scalar.copy(out=rounded.rearrange("p (j t) -> p j t", t=PACK), in_=bank[:].rearrange("p t j -> p j t"))
 
         def stage_planes(j):
@@ -290,10 +306,11 @@ def tile_list_htabg_mul_noneP_kernel(
                 )
             if q_whole:
                 j0, n = q_cuts[q]
-                nc.vector.quantize_mx(out=y_w[:, j0 : j0 + n].bitcast(E4M3), scales=y_s[:, j0 : j0 + n], in_=y_bf[q][:])
+                nc.vector.quantize_mx(out=y_w[:, j0 : j0 + n].bitcast(E4M3), scales=y_s[:, j0 : j0 + n], in_=y_bf[q])
+            done.add(j)
             w, w0, w_whole = holder(w_cuts, j)
-            if w_whole:
-                j0, n = w_cuts[w]
+            j0, n = w_cuts[w]
+            if all(jj in done for jj in range(j0, j0 + n, BANK)):
                 nc.sync.dma_start(out=y_words[:, j0 : j0 + n], in_=y_w[:, j0 : j0 + n].bitcast(I32))
 
         last = len(x_cuts) - 1
@@ -306,16 +323,16 @@ def tile_list_htabg_mul_noneP_kernel(
                 deal_words(1, wd_raw)
         for j in range(0, J, BANK):
             c, c0, whole = holder(x_cuts, j)
-            if whole and 1 <= c < last:
+            if whole and c == 1:
                 quantise_x(c + 1)
             stage_h(j)
+            if not whole and 2 <= c < last:
+                quantise_x(c + 1)
             if j == 0:
                 finish_x(last)
             finish_h(j)
-            if j >= PLANES_LAG:
-                stage_planes(j - PLANES_LAG)
-        for j in range(J - PLANES_LAG, J, BANK):
-            stage_planes(j)
+        for b in PLANES_ORDER:
+            stage_planes(b * BANK)
         for q in range(4):
             queue = nc.sync
             queue.dma_start(

@@ -73,6 +73,9 @@ def tile_list_htabg_mul_noneP_kernel(
             rows = slice(32 * q, 32 * (q + 1))
             nc.vector.tensor_tensor(identity[rows, rows], count[rows, :], count_down[rows, :], mybir.AluOpType.is_equal)
         nc.gpsimd.memset(w4_s_raw[:].bitcast(I32), 0)
+        w4_s_dealt = keep.tile([P, 2 * K], U8, name="w4_s_dealt", align_bytes=64)
+        w4_s = keep.tile([P, 2 * K], U8, name="w4_s", align_bytes=64)
+        nc.vector.memset(w4_s[:].bitcast(I32), 0)
         wgt_rows = keep.tile([P, P], F32, name="wgt_rows")
 
         x_rows = xT.rearrange("(p i) t -> p i t", i=PACK)
@@ -84,11 +87,11 @@ def tile_list_htabg_mul_noneP_kernel(
         nc.sync.dma_start(out=wb_raw[:, 2:4, :], in_=wb_rows[:, 2:4, :])
         nc.sync.dma_start(out=tab_w[:].bitcast(I32), in_=tab_words[0].rearrange("p t i -> p (t i)").bitcast(I32))
         nc.sync.dma_start(x_lists[:], offs2)
-        load_scale_rows(nc.sync, w4_s_raw[:, 0:K], wa_scales[0])
+        nc.sync.dma_start(out=w4_s_raw[0:P:8, 0:K].bitcast(I32), in_=wa_scales[0].bitcast(I32))
+        nc.sync.dma_start(out=w4_s_raw[0:P:8, K : 2 * K].bitcast(I32), in_=wd_scales[0].bitcast(I32))
         nc.sync.dma_start(out=x_planes[0][:], in_=x_rows[:, 0, :])
         nc.sync.dma_start(out=wa_raw[:].bitcast(I32), in_=wa_words[0].bitcast(I32))
         nc.sync.dma_start(out=x_planes[1][:], in_=x_rows[:, 1, :])
-        load_scale_rows(nc.sync, w4_s_raw[:, K : 2 * K], wd_scales[0])
         nc.sync.dma_start(out=x_planes[2][:], in_=x_rows[:, 2, :])
         nc.sync.dma_start(out=x_planes[3][:], in_=x_rows[:, 3, :])
         nc.sync.dma_start(out=wd_raw[:].bitcast(I32), in_=wd_words[0].bitcast(I32))
@@ -131,12 +134,13 @@ def tile_list_htabg_mul_noneP_kernel(
             finish_wgt(h)
 
         nc.vector.quantize_mx(out=wb_w[:].bitcast(E4M3), scales=wb_s[:], in_=wb_bf[:])
-        wa_dealt = keep.tile([P, 3 * K], U8, name="wa_dealt", align_bytes=64)
-        nc.gpsimd.tensor_copy(
-            out=wa_dealt[:, 2 * K :].rearrange("p (t m) -> p t m", t=PACK),
-            in_=w4_s_raw[:, 0:K].rearrange("p (m t) -> p t m", t=PACK),
-        )
-        dealt = [wa_dealt]
+        for w in range(2):
+            nc.gpsimd.tensor_copy(
+                out=w4_s_dealt[:, w * K : (w + 1) * K].rearrange("p (t m) -> p t m", t=PACK),
+                in_=w4_s_raw[:, w * K : (w + 1) * K].rearrange("p (m t) -> p t m", t=PACK),
+            )
+        for q in range(0, P, 32):
+            nc.sync.dma_start(out=w4_s[q : q + 4, :].bitcast(I32), in_=w4_s_dealt[q : q + 32 : 8, :].bitcast(I32))
 
         v_w = reused.tile([P, J], U32, name="v_w", offset=4 * J, align_bytes=64)
         for j0, n in cuts(V_WIDTHS):
@@ -144,44 +148,36 @@ def tile_list_htabg_mul_noneP_kernel(
                 v_w[:, j0 : j0 + n], tab_w[:].indirect(tab_list[:, j0 // STRIPE : (j0 + n) // STRIPE])
             )
 
-        wd_dealt = keep.tile([P, 3 * K], U8, name="wd_dealt", align_bytes=64)
-        dealt.append(wd_dealt)
+        wd_dealt = keep.tile([P, 2 * K], U8, name="wd_dealt", align_bytes=64)
 
-        late = keep.tile([P, 2 * HALF + 2 * BANK], F32, name="late", align_bytes=64)
-        picked = [[keep.tile([P, 2, HALF], F32, name="picked%d_%d" % (u, h))[:] for h in range(2 - u)] for u in range(2)]
-        picked[1].append(late[:, 0 : 2 * HALF].rearrange("p (e j) -> p e j", e=2))
+        late = keep.tile([P, 2 * J + 2 * BANK], F32, name="late", align_bytes=64)
+        early = keep.tile([P, 2 * J], F32, name="early", align_bytes=64)
+        picked = [pair[:, 0 : 2 * J].rearrange("p (e j) -> p e j", e=2) for pair in (early, late)]
         x_cuts = cuts(X_WIDTHS)
-        x_bf = [late[:, HALF : HALF + 2 * BANK].bitcast(BF16)]
+        x_bf = [late[:, J + HALF : J + HALF + 2 * BANK].bitcast(BF16)]
         x_bf.extend(keep.tile([P, n * PACK], BF16, name="x_bf%d" % j0, align_bytes=64)[:] for j0, n in x_cuts[1:])
 
         def weave(u, c):
             j0, n = x_cuts[c]
-            h, c0 = divmod(j0, HALF)
             nc.scalar.copy(
                 out=x_bf[c].rearrange("p (j u e) -> p j u e", u=2, e=2)[:, :, u, :],
-                in_=picked[u][h][:, :, c0 : c0 + n].rearrange("p e j -> p j e"),
+                in_=picked[u][:, :, j0 : j0 + n].rearrange("p e j -> p j e"),
             )
 
         def gather(i, j0, n):
-            h, c0 = divmod(j0, HALF)
             nc.vector.tensor_tensor(
-                picked[i // 2][h][:, i % 2, c0 : c0 + n],
+                picked[i // 2][:, i % 2, j0 : j0 + n],
                 x_planes[i][:].indirect(x_lists[:, j0 // STRIPE : (j0 + n) // STRIPE]),
-                wgt[h][:, c0 : c0 + n],
+                wgt_all[:, j0 : j0 + n],
                 MULT,
             )
 
-        for i in range(2):
-            for h in range(2):
-                gather(i, h * HALF, HALF)
-
-        nc.vector.tensor_copy(
-            out=wd_dealt[:, 2 * K :].rearrange("p (t m) -> p t m", t=PACK),
-            in_=w4_s_raw[:, K : 2 * K].rearrange("p (m t) -> p t m", t=PACK),
-        )
+        gather(0, 0, J)
+        for h in range(2):
+            gather(1, h * HALF, HALF)
 
         def fp4_slice(w, t):
-            return dealt[w][:, 2 * t * P : 2 * (t + 1) * P].bitcast(E2M1), dealt[w][:, 2 * K + t * P : 2 * K + (t + 1) * P]
+            return dealt[w][:, 2 * t * P : 2 * (t + 1) * P].bitcast(E2M1), w4_s[:, w * K + t * P : w * K + (t + 1) * P]
 
         def wb_slice(t):
             return wb_w[:, t * P : (t + 1) * P].bitcast(E4M3), wb_s[:, t * P : (t + 1) * P]
@@ -194,13 +190,16 @@ def tile_list_htabg_mul_noneP_kernel(
                     start=True, stop=True,
                 )
 
-        yb = [late[:, HALF + 2 * BANK :].rearrange("p (j t) -> p j t", t=PACK)]
+        yb = [late[:, J + HALF + 2 * BANK :].rearrange("p (j t) -> p j t", t=PACK)]
         yb.extend(keep.tile([P, BANK, PACK], F32, name="yb%d" % b)[:] for b in range(1, J // BANK))
         for b in range(J // BANK):
             cols = slice(b * BANK, (b + 1) * BANK)
             bank = psum.tile([P, PACK, BANK], F32, name="out_bank", bufs=5)
             product(bank, wb_slice, v_w[:, cols], v_s[:, cols])
             nc.scalar.copy(out=yb[b], in_=bank[:].rearrange("p t j -> p j t"))
+
+        wa_dealt = reused.tile([P, 2 * K], U8, name="wa_dealt", offset=4 * J, align_bytes=64)
+        dealt = [wa_dealt, wd_dealt]
 
         def deal_words(w, raw):
             nc.scalar.copy(
@@ -210,8 +209,7 @@ def tile_list_htabg_mul_noneP_kernel(
 
         deal_words(0, wa_raw)
         weave(0, 0)
-        for h in range(2):
-            gather(2, h * HALF, HALF)
+        gather(2, 0, J)
 
         y_s = keep.tile([P, J], U8, name="y_s", align_bytes=64)
         y_w = keep.tile([P, J], U32, name="y_w", align_bytes=64)
@@ -240,9 +238,15 @@ def tile_list_htabg_mul_noneP_kernel(
                 if j0 <= j < j0 + n:
                     return c, j - j0, j + BANK == j0 + n
 
-        def quantised(name, src, n):
-            words = keep.tile([P, n], U32, name=name + "_w", align_bytes=64)
-            scales = keep.tile([P, n], U8, name=name + "_s", align_bytes=64)
+        def quantised(name, src, n, words_at=None, scales_at=None):
+            if words_at is None:
+                words = keep.tile([P, n], U32, name=name + "_w", align_bytes=64)
+            else:
+                words = reused.tile([P, n], U32, name=name + "_w", offset=words_at, align_bytes=64)
+            if scales_at is None:
+                scales = keep.tile([P, n], U8, name=name + "_s", align_bytes=64)
+            else:
+                scales = reused.tile([P, n], U8, name=name + "_s", offset=scales_at, align_bytes=64)
             nc.vector.quantize_mx(out=words[:].bitcast(E4M3), scales=scales[:], in_=src)
             return words, scales
 
@@ -253,7 +257,9 @@ def tile_list_htabg_mul_noneP_kernel(
             weave(1, c)
 
         def quantise_x(c):
-            x_q[c] = quantised("x%d" % c, x_bf[c], x_cuts[c][1])
+            words_at = 4 * (PACK * K + x_cuts[c][0])
+            scales_at = 4 * (PACK * K + x_cuts[c - 2][0]) if c >= 2 else None
+            x_q[c] = quantised("x%d" % c, x_bf[c], x_cuts[c][1], words_at, scales_at)
 
         def stage_h(j):
             c, c0, whole = holder(x_cuts, j)

@@ -14,23 +14,20 @@ U8 = mybir.dt.uint8
 E4M3 = mybir.dt.float8_e4m3fn_x4
 E2M1 = mybir.dt.float4_e2m1fn_x4
 MULT = mybir.AluOpType.mult
+ADD = mybir.AluOpType.add
 
 P = 128
 PACK = 4
 BANK = 128
 HALF = 512
 STRIPE = 16
-V_WIDTHS = [128, 128, 256, 512]
+LINE = 4
+BANKS = J // BANK
+V_WIDTHS = [512, 512]
 X_WIDTHS = [128, 128, 256, 256, 256]
-H_WIDTHS = [128, 128, 128, 128, 128, 128, 128, 128]
-Y_WIDTHS = [128, 128, 128, 128, 128, 128, 128, 128]
-Q_WIDTHS = [128, 128, 128, 128, 256, 128, 128]
-W_WIDTHS = [256, 512, 256]
-VECTOR_ROUNDS = (5, 6)
-GPSIMD_ROUNDS = (1, 3)
-PLANES_ORDER = (0, 1, 2, 4, 5, 3, 6, 7)
-ROUND_FIRST = (7,)
-WB_SPLIT = 48
+FIRST = 256
+HELD = 384
+WB_SPLIT = 80
 
 
 def cuts(widths):
@@ -45,10 +42,6 @@ def tile_list_htabg_mul_noneP_kernel(
         keep = ctx.enter_context(tc.tile_pool(name="keep", bufs=1))
         reused = ctx.enter_context(tc.tile_pool(name="reused", bufs=1))
         psum = ctx.enter_context(tc.psum_pool(name="psum", bufs=1))
-
-        def load_scale_rows(queue, plane, rows):
-            for q in range(4):
-                queue.dma_start(out=plane[32 * q : 32 * q + 4, :].bitcast(I32), in_=rows[4 * q : 4 * q + 4, :].bitcast(I32))
 
         tab_list = keep.tile([P, J // STRIPE], U16, name="tab_list")
         x_lists = keep.tile([P, J // STRIPE], U16, name="x_lists")
@@ -67,7 +60,7 @@ def tile_list_htabg_mul_noneP_kernel(
         count_down = keep.tile([P, 32], F32, name="count_down", align_bytes=64)
         nc.vector.memset(ones[:], 1.0)
         nc.vector.memset(identity[:], 0.0)
-        nc.vector.tensor_tensor_scan(count[:], ones[:], ones[:], 0.0, MULT, mybir.AluOpType.add)
+        nc.vector.tensor_tensor_scan(count[:], ones[:], ones[:], 0.0, MULT, ADD)
         nc.vector.transpose(count_down[:], count[:])
         for q in range(4):
             rows = slice(32 * q, 32 * (q + 1))
@@ -83,7 +76,10 @@ def tile_list_htabg_mul_noneP_kernel(
         nc.sync.dma_start(out=wgt_rows[:], in_=wgt2[0:P:8, :].rearrange("a (b d) -> a b d", d=P))
         nc.sync.dma_start(tab_list[:], offs)
         nc.sync.dma_start(out=wb_raw[:, 0:2, :], in_=wb_rows[:, 0:2, :])
-        load_scale_rows(nc.sync, tab_s, tab_scales[0])
+        for q in range(4):
+            nc.sync.dma_start(
+                out=tab_s[32 * q : 32 * q + 4, :].bitcast(I32), in_=tab_scales[0, 4 * q : 4 * q + 4, :].bitcast(I32)
+            )
         nc.sync.dma_start(out=wb_raw[:, 2:4, :], in_=wb_rows[:, 2:4, :])
         nc.sync.dma_start(out=tab_w[:].bitcast(I32), in_=tab_words[0].rearrange("p t i -> p (t i)").bitcast(I32))
         nc.sync.dma_start(x_lists[:], offs2)
@@ -92,18 +88,16 @@ def tile_list_htabg_mul_noneP_kernel(
         nc.sync.dma_start(out=x_planes[0][:], in_=x_rows[:, 0, :])
         nc.sync.dma_start(out=wa_raw[:].bitcast(I32), in_=wa_words[0].bitcast(I32))
         nc.sync.dma_start(out=x_planes[1][:], in_=x_rows[:, 1, :])
-        nc.sync.dma_start(out=x_planes[2][:], in_=x_rows[:, 2, :])
-        nc.sync.dma_start(out=x_planes[3][:], in_=x_rows[:, 3, :])
         nc.sync.dma_start(out=wd_raw[:].bitcast(I32), in_=wd_words[0].bitcast(I32))
+        for i in range(2, PACK):
+            nc.sync.dma_start(out=x_planes[i][:], in_=x_rows[:, i, :])
 
         bank = psum.tile([P, PACK, BANK], F32, name="ya_bank", bufs=3)
         nc.tensor.transpose(bank[:, 0, :], wgt_rows[:], identity[:])
-        turned = keep.tile([P, P], F32, name="turned")
-        nc.scalar.copy(out=turned[:], in_=bank[:, 0, :])
         spread = [keep.tile([P, PACK, P], F32, name="spread%d" % h) for h in range(2)]
         for h in range(2):
-            by_group = turned[:].rearrange("d (g x) -> d x g", x=STRIPE)[:, PACK * h : PACK * (h + 1), :]
-            nc.gpsimd.tensor_copy(
+            by_group = bank[:, 0, :].rearrange("d (g x) -> d x g", x=STRIPE)[:, PACK * h : PACK * (h + 1), :]
+            nc.scalar.copy(
                 out=spread[h][:].rearrange("d b (g r) -> d b g r", r=STRIPE),
                 in_=by_group.unsqueeze(3).to_broadcast([P, PACK, P // STRIPE, STRIPE]),
             )
@@ -114,24 +108,20 @@ def tile_list_htabg_mul_noneP_kernel(
         wb_bf = keep.tile([P, K * PACK], BF16, name="wb_bf", align_bytes=64)
         wb_w = keep.tile([P, K], U32, name="wb_w", align_bytes=64)
         wb_s = keep.tile([P, K], U8, name="wb_s", align_bytes=64)
-        wb_to = wb_bf[:].rearrange("p (t m i) -> p m t i", t=PACK, i=PACK)
-        wb_from = wb_raw[:].rearrange("p i (m t) -> p m t i", t=PACK)
-        nc.scalar.copy(out=wb_to[:, :, :, 0:2], in_=wb_from[:, :, :, 0:2])
-        nc.scalar.copy(out=wb_to[:, 0:WB_SPLIT, :, 2:4], in_=wb_from[:, 0:WB_SPLIT, :, 2:4])
+        wb_to = wb_bf[:].rearrange("p (t m i) -> p m i t", t=PACK, i=PACK)
+        wb_from = wb_raw[:].rearrange("p i (m t) -> p m i t", t=PACK)
+        nc.scalar.copy(out=wb_to[:, 0:WB_SPLIT], in_=wb_from[:, 0:WB_SPLIT])
         nc.gpsimd.tensor_scalar(
-            wb_to[:, WB_SPLIT:, :, 2:4], wb_from[:, WB_SPLIT:, :, 2:4], 1.0, 0.0, MULT, mybir.AluOpType.add
+            wb_to[:, WB_SPLIT:].rearrange("p m i t -> p m t i"), wb_from[:, WB_SPLIT:].rearrange("p m i t -> p m t i"),
+            1.0, 0.0, MULT, ADD,
         )
 
-        def finish_wgt(h):
+        wgt_all = reused.tile([P, J], F32, name="wgt_all", offset=0, align_bytes=64)
+        for h in range(2):
             bank = psum.tile([P, PACK, BANK], F32, name="out_bank", bufs=5)
             for b in range(PACK):
                 nc.tensor.transpose(bank[:, b, :], spread[h][:, b, :], identity[:])
-            nc.scalar.copy(out=wgt[h], in_=bank[:].rearrange("p b d -> p (b d)"))
-
-        wgt_all = reused.tile([P, J], F32, name="wgt_all", offset=0, align_bytes=64)
-        wgt = [wgt_all[:, h * HALF : (h + 1) * HALF] for h in range(2)]
-        for h in range(2):
-            finish_wgt(h)
+            nc.scalar.copy(out=wgt_all[:, h * HALF : (h + 1) * HALF], in_=bank[:].rearrange("p b d -> p (b d)"))
 
         nc.vector.quantize_mx(out=wb_w[:].bitcast(E4M3), scales=wb_s[:], in_=wb_bf[:])
         for w in range(2):
@@ -148,33 +138,22 @@ def tile_list_htabg_mul_noneP_kernel(
                 v_w[:, j0 : j0 + n], tab_w[:].indirect(tab_list[:, j0 // STRIPE : (j0 + n) // STRIPE])
             )
 
-        wd_dealt = keep.tile([P, 2 * K], U8, name="wd_dealt", align_bytes=64)
+        picked = keep.tile([P, PACK * J], F32, name="picked", align_bytes=64)
 
-        late = keep.tile([P, 2 * J + 2 * BANK], F32, name="late", align_bytes=64)
-        early = keep.tile([P, 2 * J], F32, name="early", align_bytes=64)
-        picked = [pair[:, 0 : 2 * J].rearrange("p (e j) -> p e j", e=2) for pair in (early, late)]
-        x_cuts = cuts(X_WIDTHS)
-        x_bf = [late[:, J + HALF : J + HALF + 2 * BANK].bitcast(BF16)]
-        x_bf.extend(keep.tile([P, n * PACK], BF16, name="x_bf%d" % j0, align_bytes=64)[:] for j0, n in x_cuts[1:])
-
-        def weave(u, c):
-            j0, n = x_cuts[c]
-            nc.scalar.copy(
-                out=x_bf[c].rearrange("p (j u e) -> p j u e", u=2, e=2)[:, :, u, :],
-                in_=picked[u][:, :, j0 : j0 + n].rearrange("p e j -> p j e"),
-            )
+        def picked_at(j0, n):
+            return picked[:].rearrange("p (i j) -> p i j", i=PACK)[:, :, j0 : j0 + n]
 
         def gather(i, j0, n):
             nc.vector.tensor_tensor(
-                picked[i // 2][:, i % 2, j0 : j0 + n],
+                picked_at(j0, n)[:, i, :],
                 x_planes[i][:].indirect(x_lists[:, j0 // STRIPE : (j0 + n) // STRIPE]),
                 wgt_all[:, j0 : j0 + n],
                 MULT,
             )
 
-        gather(0, 0, J)
-        for h in range(2):
-            gather(1, h * HALF, HALF)
+        for i in range(PACK - 1):
+            gather(i, 0, J)
+
 
         def fp4_slice(w, t):
             return dealt[w][:, 2 * t * P : 2 * (t + 1) * P].bitcast(E2M1), w4_s[:, w * K + t * P : w * K + (t + 1) * P]
@@ -190,157 +169,185 @@ def tile_list_htabg_mul_noneP_kernel(
                     start=True, stop=True,
                 )
 
-        yb = [late[:, J + HALF + 2 * BANK :].rearrange("p (j t) -> p j t", t=PACK)]
-        yb.extend(keep.tile([P, BANK, PACK], F32, name="yb%d" % b)[:] for b in range(1, J // BANK))
-        for b in range(J // BANK):
+        yb = [keep.tile([P, BANK, PACK], F32, name="yb%d" % b) for b in range(BANKS)]
+        for b in range(BANKS):
             cols = slice(b * BANK, (b + 1) * BANK)
             bank = psum.tile([P, PACK, BANK], F32, name="out_bank", bufs=5)
             product(bank, wb_slice, v_w[:, cols], v_s[:, cols])
-            nc.scalar.copy(out=yb[b], in_=bank[:].rearrange("p t j -> p j t"))
+            nc.scalar.copy(out=yb[b][:], in_=bank[:].rearrange("p t j -> p j t"))
 
         wa_dealt = reused.tile([P, 2 * K], U8, name="wa_dealt", offset=4 * J, align_bytes=64)
+        wd_dealt = reused.tile([P, 2 * K], U8, name="wd_dealt", offset=4 * J + 2 * K, align_bytes=64)
         dealt = [wa_dealt, wd_dealt]
 
         def deal_words(w, raw):
             nc.scalar.copy(
-                out=dealt[w][:, 0 : 2 * K].bitcast(U16).rearrange("p (t m) -> p t m", t=PACK),
+                out=dealt[w][:].bitcast(U16).rearrange("p (t m) -> p t m", t=PACK),
                 in_=raw[:].rearrange("p (m t) -> p t m", t=PACK),
             )
 
         deal_words(0, wa_raw)
-        weave(0, 0)
-        gather(2, 0, J)
+        deal_words(1, wd_raw)
 
+        x_cuts = cuts(X_WIDTHS)
+        last = len(x_cuts) - 1
+        codes_at = 4 * PACK * K
+        x_bf, x_q, ya, h_q, y_bank = {}, {}, {}, {}, {}
         y_s = keep.tile([P, J], U8, name="y_s", align_bytes=64)
         y_w = keep.tile([P, J], U32, name="y_w", align_bytes=64)
         y_rows = out_0.rearrange("(p t) j -> p t j", t=PACK)
         y_words = out_1[0].rearrange("p j i -> p (j i)").bitcast(I32)
-        h_cuts, y_cuts, q_cuts, w_cuts = cuts(H_WIDTHS), cuts(Y_WIDTHS), cuts(Q_WIDTHS), cuts(W_WIDTHS)
-        h_all = keep.tile([P, J * PACK], BF16, name="h_all", align_bytes=64)
-        h_bf = [h_all[:, j0 * PACK : (j0 + n) * PACK] for j0, n in h_cuts]
-        y_f = [keep.tile([P, PACK, n], F32, name="y_f%d" % j0) for j0, n in y_cuts]
-        half = BANK * PACK // 2
-        y_bf = [
-            h_all[:, (2 * q + 5) * half : (2 * q + 7) * half] if q in GPSIMD_ROUNDS
-            else keep.tile([P, n * PACK], BF16, name="y_bf%d" % j0, align_bytes=64)[:]
-            for q, (j0, n) in enumerate(q_cuts)
-        ]
+        width = BANK * PACK
+        h_order = [2, 4, None, 6, None, 0, 1, 3, 5, 7]
+        h_all = keep.tile([P, len(h_order) * width], BF16, name="h_all", align_bytes=64)
+        h_bf = [h_all[:, h_order.index(b) * width : (h_order.index(b) + 1) * width] for b in range(BANKS)]
+        y_late = keep.tile([P, (BANKS - 4) * width], BF16, name="y_late", align_bytes=64)
+        y_f = [keep.tile([P, PACK, BANK], F32, name="y_f%d" % b) for b in range(BANKS)]
 
-        def round_half(b, u):
-            to = y_bf[b][:, u * half : (u + 1) * half].rearrange("p (g e t) -> p g t e", e=4, t=PACK)
-            src = y_f[b][:, :, u * BANK // 2 : (u + 1) * BANK // 2].rearrange("p t (g e) -> p g t e", e=4)
-            nc.gpsimd.tensor_scalar(to, src, 1.0, 0.0, MULT, mybir.AluOpType.add)
+        def y_bf(b, banks=1):
+            return h_all[:, b * width : (b + banks) * width] if b < 4 else y_late[:, (b - 4) * width : (b - 4 + banks) * width]
 
-        x_q, h_q, done = {}, {}, set()
-
-        def holder(pieces, j):
-            for c, (j0, n) in enumerate(pieces):
-                if j0 <= j < j0 + n:
-                    return c, j - j0, j + BANK == j0 + n
-
-        def quantised(name, src, n, words_at=None, scales_at=None):
-            if words_at is None:
-                words = keep.tile([P, n], U32, name=name + "_w", align_bytes=64)
-            else:
-                words = reused.tile([P, n], U32, name=name + "_w", offset=words_at, align_bytes=64)
-            if scales_at is None:
-                scales = keep.tile([P, n], U8, name=name + "_s", align_bytes=64)
-            else:
-                scales = reused.tile([P, n], U8, name=name + "_s", offset=scales_at, align_bytes=64)
-            nc.vector.quantize_mx(out=words[:].bitcast(E4M3), scales=scales[:], in_=src)
-            return words, scales
-
-        def finish_x(c):
-            gather(3, *x_cuts[c])
-            if c:
-                weave(0, c)
-            weave(1, c)
-
-        def quantise_x(c):
-            words_at = 4 * (PACK * K + x_cuts[c][0])
-            scales_at = 4 * (PACK * K + x_cuts[c - 2][0]) if c >= 2 else None
-            x_q[c] = quantised("x%d" % c, x_bf[c], x_cuts[c][1], words_at, scales_at)
-
-        def stage_h(j):
-            c, c0, whole = holder(x_cuts, j)
-            words, scales = x_q[c]
-            bank = psum.tile([P, PACK, BANK], F32, name="ya_bank", bufs=3)
-            product(bank, lambda t: fp4_slice(0, t), words[:, c0 : c0 + BANK], scales[:, c0 : c0 + BANK])
-            c, c0, whole = holder(h_cuts, j)
-            nc.vector.tensor_tensor(
-                h_bf[c][:, c0 * PACK : (c0 + BANK) * PACK].rearrange("p (j t) -> p j t", t=PACK),
-                bank[:].rearrange("p t j -> p j t"),
-                yb[j // BANK],
-                MULT,
+        def weave(c):
+            j0, n = x_cuts[c]
+            if c == last:
+                n = BANK
+            elif c:
+                x_bf[c] = keep.tile([P, n * PACK], BF16, name="x_bf%d" % c, align_bytes=64)[:]
+            nc.scalar.copy(
+                out=x_bf[c][:, 0 : n * PACK].rearrange("p (g e i) -> p g i e", e=LINE, i=PACK),
+                in_=picked_at(j0, n).rearrange("p i (g e) -> p g i e", e=LINE),
             )
 
-        def finish_h(j):
-            c, c0, whole = holder(h_cuts, j)
-            if whole:
-                h_q[c] = quantised("h%d" % c, h_bf[c], h_cuts[c][1])
-                for u in range(2):
-                    if c - 2 - u in GPSIMD_ROUNDS:
-                        round_half(c - 2 - u, u)
-                for jj in range(h_cuts[c][0], j + BANK, BANK):
-                    stage_y(jj)
+        x_bf[last] = h_all[:, (h_order.index(0) - 1) * width : (h_order.index(0) + 1) * width]
 
-        def stage_y(j):
-            c, c0, whole = holder(h_cuts, j)
-            words, scales = h_q[c]
-            bank = psum.tile([P, PACK, BANK], F32, name="out_bank", bufs=5)
-            product(bank, lambda t: fp4_slice(1, t), words[:, c0 : c0 + BANK], scales[:, c0 : c0 + BANK])
-            c, c0, whole = holder(y_cuts, j)
-            q, q0, q_whole = holder(q_cuts, j)
-            rounded = y_bf[q][:, q0 * PACK : (q0 + BANK) * PACK]
-            if j // BANK in ROUND_FIRST:
-                nc.scalar.copy(out=rounded.rearrange("p (j t) -> p j t", t=PACK), in_=bank[:].rearrange("p t j -> p j t"))
-            nc.scalar.copy(out=y_f[c][:, :, c0 : c0 + BANK], in_=bank[:])
-            if whole:
-                j0, n = y_cuts[c]
-                queue = nc.scalar if j0 + n == J else nc.sync
-                queue.dma_start(out=y_rows[:, :, j0 : j0 + n], in_=y_f[c][:])
-            if j // BANK not in ROUND_FIRST + VECTOR_ROUNDS + GPSIMD_ROUNDS:
-                nc.scalar.copy(out=rounded.rearrange("p (j t) -> p j t", t=PACK), in_=bank[:].rearrange("p t j -> p j t"))
+        x_bf[0] = picked[:, PACK * J - HELD : PACK * J - HELD + width // 2].bitcast(BF16)
 
-        def stage_planes(j):
-            q, q0, q_whole = holder(q_cuts, j)
-            if j // BANK in VECTOR_ROUNDS:
-                c, c0, whole = holder(y_cuts, j)
-                nc.vector.tensor_copy(
-                    out=y_bf[q][:, q0 * PACK : (q0 + BANK) * PACK].rearrange("p (g e t) -> p g t e", e=4, t=PACK),
-                    in_=y_f[c][:, :, c0 : c0 + BANK].rearrange("p t (g e) -> p g t e", e=4),
-                )
-            if q_whole:
-                j0, n = q_cuts[q]
-                nc.vector.quantize_mx(out=y_w[:, j0 : j0 + n].bitcast(E4M3), scales=y_s[:, j0 : j0 + n], in_=y_bf[q])
-            done.add(j)
-            w, w0, w_whole = holder(w_cuts, j)
-            j0, n = w_cuts[w]
-            if all(jj in done for jj in range(j0, j0 + n, BANK)):
-                nc.sync.dma_start(out=y_words[:, j0 : j0 + n], in_=y_w[:, j0 : j0 + n].bitcast(I32))
+        def weave_gpsimd():
+            nc.gpsimd.tensor_scalar(
+                x_bf[last][:, width:].rearrange("p (j i) -> p j i", i=PACK),
+                picked_at(J - BANK, BANK).rearrange("p i j -> p j i"), 1.0, 0.0, MULT, ADD,
+            )
 
-        last = len(x_cuts) - 1
-        for c in range(2):
-            finish_x(c)
-            quantise_x(c)
-        for c in range(2, last):
-            finish_x(c)
-            if c == 2:
-                deal_words(1, wd_raw)
-        for j in range(0, J, BANK):
-            c, c0, whole = holder(x_cuts, j)
-            if whole and c == 1:
-                quantise_x(c + 1)
-            stage_h(j)
-            if not whole and 2 <= c < last:
-                quantise_x(c + 1)
-            if j == 0:
-                finish_x(last)
-            finish_h(j)
-        for b in PLANES_ORDER:
-            stage_planes(b * BANK)
+        def quantise_x(c):
+            j0, n = x_cuts[c]
+            words = reused.tile([P, n], U32, name="x%d_w" % c, offset=codes_at + 4 * j0, align_bytes=64)
+            if c >= 2:
+                scales = reused.tile([P, n], U8, name="x%d_s" % c, offset=codes_at + 4 * x_cuts[c - 2][0], align_bytes=64)
+            else:
+                scales = keep.tile([P, n], U8, name="x%d_s" % c, align_bytes=64)
+            nc.vector.quantize_mx(out=words[:].bitcast(E4M3), scales=scales[:], in_=x_bf[c])
+            for c0 in range(0, n, BANK):
+                x_q[(j0 + c0) // BANK] = words[:, c0 : c0 + BANK], scales[:, c0 : c0 + BANK]
+
+        def product_a(b):
+            ya[b] = psum.tile([P, PACK, BANK], F32, name="ya_bank", bufs=3)
+            product(ya[b], lambda t: fp4_slice(0, t), *x_q[b])
+
+        def multiply(b):
+            nc.vector.tensor_tensor(
+                h_bf[b].rearrange("p (j t) -> p j t", t=PACK), ya[b][:].rearrange("p t j -> p j t"), yb[b][:], MULT
+            )
+
+        def quantise_h(b):
+            words = keep.tile([P, BANK], U32, name="h%d_w" % b, align_bytes=64)
+            scales = keep.tile([P, BANK], U8, name="h%d_s" % b, align_bytes=64)
+            nc.vector.quantize_mx(out=words[:].bitcast(E4M3), scales=scales[:], in_=h_bf[b])
+            y_bank[b] = psum.tile([P, PACK, BANK], F32, name="out_bank", bufs=5)
+            product(y_bank[b], lambda t: fp4_slice(1, t), words[:], scales[:])
+
+        def store_y(b):
+            nc.scalar.copy(out=y_f[b][:], in_=y_bank[b][:])
+            queue = nc.scalar if b == BANKS - 1 else nc.sync
+            queue.dma_start(out=y_rows[:, :, b * BANK : (b + 1) * BANK], in_=y_f[b][:])
+
+        def round_scalar(b):
+            nc.scalar.copy(out=y_bf(b).rearrange("p (j t) -> p j t", t=PACK), in_=y_bank[b][:].rearrange("p t j -> p j t"))
+
+        def round_vector(b, c0=0):
+            nc.vector.tensor_copy(
+                out=y_bf(b)[:, c0 * PACK :].rearrange("p (g e t) -> p g t e", e=LINE, t=PACK),
+                in_=y_f[b][:, :, c0:].rearrange("p t (g e) -> p g t e", e=LINE),
+            )
+
+        def round_gpsimd(b, n=BANK):
+            nc.gpsimd.tensor_scalar(
+                y_bf(b)[:, 0 : n * PACK].rearrange("p (j t) -> p j t", t=PACK),
+                y_f[b][:, :, 0:n].rearrange("p t j -> p j t"), 1.0, 0.0, MULT, ADD,
+            )
+
+        def quantise_y(b, banks):
+            cols = slice(b * BANK, (b + banks) * BANK)
+            nc.vector.quantize_mx(out=y_w[:, cols].bitcast(E4M3), scales=y_s[:, cols], in_=y_bf(b, banks))
+
+        def store_words(b, banks):
+            cols = slice(b * BANK, (b + banks) * BANK)
+            nc.sync.dma_start(out=y_words[:, cols], in_=y_w[:, cols].bitcast(I32))
+
+        gather(3, 0, BANK)
+        weave(0)
+        gather(3, BANK, BANK)
+        weave(1)
+        gather(3, FIRST, J - FIRST - HELD)
+        quantise_x(0)
+        product_a(0)
+        gather(3, J - HELD, HELD)
+        quantise_x(1)
+        product_a(1)
+        weave(2)
+        multiply(0)
+        quantise_x(2)
+        product_a(2)
+        quantise_h(0)
+        weave_gpsimd()
+        multiply(1)
+        product_a(3)
+        weave(3)
+        weave(4)
+        store_y(0)
+        multiply(2)
+        quantise_h(1)
+        quantise_x(3)
+        product_a(4)
+        quantise_h(2)
+        round_gpsimd(0)
+        store_y(1)
+        store_y(2)
+        round_scalar(2)
+        multiply(3)
+        product_a(5)
+        multiply(4)
+        quantise_h(3)
+        quantise_x(4)
+        product_a(6)
+        quantise_h(4)
+        round_gpsimd(1)
+        store_y(3)
+        store_y(4)
+        round_scalar(4)
+        multiply(5)
+        product_a(7)
+        multiply(6)
+        quantise_h(5)
+        quantise_h(6)
+        round_gpsimd(3, BANK // 2)
+        store_y(5)
+        store_y(6)
+        multiply(7)
+        quantise_y(0, 2)
+        store_words(0, 2)
+        quantise_h(7)
+        round_scalar(7)
+        store_y(7)
+        round_vector(3, BANK // 2)
+        round_vector(5)
+        quantise_y(2, 2)
+        round_vector(6)
+        quantise_y(4, 2)
+        store_words(2, 4)
+        quantise_y(6, 1)
+        quantise_y(7, 1)
+        store_words(6, 2)
         for q in range(4):
-            queue = nc.sync
-            queue.dma_start(
+            nc.sync.dma_start(
                 out=out_2[0, 4 * q : 4 * q + 4, :].bitcast(I32), in_=y_s[32 * q : 32 * q + 4, :].bitcast(I32)
             )

@@ -28,6 +28,9 @@ X_WIDTHS = [128, 128, 256, 256, 256]
 FIRST = 256
 HELD = 384
 WB_SPLIT = 80
+TAB_S_AT = 4 * PACK * K
+V_W_AT = TAB_S_AT + 64 - 4 * J
+PLANE_AT = TAB_S_AT + T - 64
 
 
 def cuts(widths):
@@ -45,12 +48,12 @@ def tile_list_htabg_mul_noneP_kernel(
 
         tab_list = keep.tile([P, J // STRIPE], U16, name="tab_list")
         x_lists = keep.tile([P, J // STRIPE], U16, name="x_lists")
-        tab_s = keep.tile([P, T], U8, name="tab_s", align_bytes=64)
+        tab_s = reused.tile([P, T], U8, name="tab_s", offset=TAB_S_AT, align_bytes=64)
         tab_w = keep.tile([P, T], U32, name="tab_w", align_bytes=64)
         w4_s_raw = keep.tile([P, 2 * K], U8, name="w4_s_raw", align_bytes=64)
         wa_raw = keep.tile([P, K], U16, name="wa_raw", align_bytes=64)
         wd_raw = keep.tile([P, K], U16, name="wd_raw", align_bytes=64)
-        x_planes = [keep.tile([P, T], F32, name="x_plane%d" % i) for i in range(PACK)]
+        x_planes = {i: keep.tile([P, T], F32, name="x_plane%d" % i) for i in (0, 2, 3)}
         wb_raw = reused.tile([P, PACK, K], F32, name="wb_raw", offset=0, align_bytes=64)
 
         nc.gpsimd.memset(tab_s[:].bitcast(I32), 0)
@@ -69,6 +72,8 @@ def tile_list_htabg_mul_noneP_kernel(
         w4_s_dealt = keep.tile([P, 2 * K], U8, name="w4_s_dealt", align_bytes=64)
         w4_s = keep.tile([P, 2 * K], U8, name="w4_s", align_bytes=64)
         nc.vector.memset(w4_s[:].bitcast(I32), 0)
+        v_s = keep.tile([P, J], U8, name="v_s", align_bytes=64)
+        nc.vector.memset(v_s[:].bitcast(I32), 0)
         wgt_rows = keep.tile([P, P], F32, name="wgt_rows")
 
         x_rows = xT.rearrange("(p i) t -> p i t", i=PACK)
@@ -76,21 +81,13 @@ def tile_list_htabg_mul_noneP_kernel(
         nc.sync.dma_start(out=wgt_rows[:], in_=wgt2[0:P:8, :].rearrange("a (b d) -> a b d", d=P))
         nc.sync.dma_start(tab_list[:], offs)
         nc.sync.dma_start(out=wb_raw[:, 0:2, :], in_=wb_rows[:, 0:2, :])
-        for q in range(4):
-            nc.sync.dma_start(
-                out=tab_s[32 * q : 32 * q + 4, :].bitcast(I32), in_=tab_scales[0, 4 * q : 4 * q + 4, :].bitcast(I32)
-            )
+        nc.sync.dma_start(out=tab_s[0:P:8, :].bitcast(I32), in_=tab_scales[0].bitcast(I32))
         nc.sync.dma_start(out=wb_raw[:, 2:4, :], in_=wb_rows[:, 2:4, :])
         nc.sync.dma_start(out=tab_w[:].bitcast(I32), in_=tab_words[0].rearrange("p t i -> p (t i)").bitcast(I32))
         nc.sync.dma_start(x_lists[:], offs2)
         nc.sync.dma_start(out=w4_s_raw[0:P:8, 0:K].bitcast(I32), in_=wa_scales[0].bitcast(I32))
         nc.sync.dma_start(out=w4_s_raw[0:P:8, K : 2 * K].bitcast(I32), in_=wd_scales[0].bitcast(I32))
         nc.sync.dma_start(out=x_planes[0][:], in_=x_rows[:, 0, :])
-        nc.sync.dma_start(out=wa_raw[:].bitcast(I32), in_=wa_words[0].bitcast(I32))
-        nc.sync.dma_start(out=x_planes[1][:], in_=x_rows[:, 1, :])
-        nc.sync.dma_start(out=wd_raw[:].bitcast(I32), in_=wd_words[0].bitcast(I32))
-        for i in range(2, PACK):
-            nc.sync.dma_start(out=x_planes[i][:], in_=x_rows[:, i, :])
 
         bank = psum.tile([P, PACK, BANK], F32, name="ya_bank", bufs=3)
         nc.tensor.transpose(bank[:, 0, :], wgt_rows[:], identity[:])
@@ -102,12 +99,20 @@ def tile_list_htabg_mul_noneP_kernel(
                 in_=by_group.unsqueeze(3).to_broadcast([P, PACK, P // STRIPE, STRIPE]),
             )
 
-        v_s = keep.tile([P, J], U8, name="v_s", align_bytes=64)
-        nc.vector.tensor_copy(v_s[:], tab_s[:].indirect(tab_list[:]))
+        v_s_apart = keep.tile([P, J], U8, name="v_s_apart", align_bytes=64)
+        nc.vector.tensor_copy(v_s_apart[:], tab_s[:].indirect(tab_list[:]))
+        for q in range(0, P, 32):
+            nc.sync.dma_start(out=v_s[q : q + 4, :].bitcast(I32), in_=v_s_apart[q : q + 32 : 8, :].bitcast(I32))
+        x_planes[1] = reused.tile([P, T], F32, name="x_plane1", offset=PLANE_AT, align_bytes=64)
+        nc.sync.dma_start(out=x_planes[1][:], in_=x_rows[:, 1, :])
+        nc.sync.dma_start(out=wa_raw[:].bitcast(I32), in_=wa_words[0].bitcast(I32))
+        nc.sync.dma_start(out=x_planes[2][:], in_=x_rows[:, 2, :])
+        nc.sync.dma_start(out=wd_raw[:].bitcast(I32), in_=wd_words[0].bitcast(I32))
+        nc.sync.dma_start(out=x_planes[3][:], in_=x_rows[:, 3, :])
 
         wb_bf = keep.tile([P, K * PACK], BF16, name="wb_bf", align_bytes=64)
         wb_w = keep.tile([P, K], U32, name="wb_w", align_bytes=64)
-        wb_s = keep.tile([P, K], U8, name="wb_s", align_bytes=64)
+        wb_s = reused.tile([P, K], U8, name="wb_s", offset=TAB_S_AT + K, align_bytes=64)
         wb_to = wb_bf[:].rearrange("p (t m i) -> p m i t", t=PACK, i=PACK)
         wb_from = wb_raw[:].rearrange("p i (m t) -> p m i t", t=PACK)
         nc.scalar.copy(out=wb_to[:, 0:WB_SPLIT], in_=wb_from[:, 0:WB_SPLIT])
@@ -132,7 +137,7 @@ def tile_list_htabg_mul_noneP_kernel(
         for q in range(0, P, 32):
             nc.sync.dma_start(out=w4_s[q : q + 4, :].bitcast(I32), in_=w4_s_dealt[q : q + 32 : 8, :].bitcast(I32))
 
-        v_w = reused.tile([P, J], U32, name="v_w", offset=4 * J, align_bytes=64)
+        v_w = reused.tile([P, J], U32, name="v_w", offset=V_W_AT, align_bytes=64)
         for j0, n in cuts(V_WIDTHS):
             nc.vector.tensor_copy(
                 v_w[:, j0 : j0 + n], tab_w[:].indirect(tab_list[:, j0 // STRIPE : (j0 + n) // STRIPE])
@@ -176,8 +181,8 @@ def tile_list_htabg_mul_noneP_kernel(
             product(bank, wb_slice, v_w[:, cols], v_s[:, cols])
             nc.scalar.copy(out=yb[b][:], in_=bank[:].rearrange("p t j -> p j t"))
 
-        wa_dealt = reused.tile([P, 2 * K], U8, name="wa_dealt", offset=4 * J, align_bytes=64)
-        wd_dealt = reused.tile([P, 2 * K], U8, name="wd_dealt", offset=4 * J + 2 * K, align_bytes=64)
+        wa_dealt = reused.tile([P, 2 * K], U8, name="wa_dealt", offset=V_W_AT, align_bytes=64)
+        wd_dealt = reused.tile([P, 2 * K], U8, name="wd_dealt", offset=V_W_AT + 2 * K, align_bytes=64)
         dealt = [wa_dealt, wd_dealt]
 
         def deal_words(w, raw):
@@ -191,7 +196,7 @@ def tile_list_htabg_mul_noneP_kernel(
 
         x_cuts = cuts(X_WIDTHS)
         last = len(x_cuts) - 1
-        codes_at = 4 * PACK * K
+        codes_at = PLANE_AT + 4 * T
         x_bf, x_q, ya, h_q, y_bank = {}, {}, {}, {}, {}
         y_s = keep.tile([P, J], U8, name="y_s", align_bytes=64)
         y_w = keep.tile([P, J], U32, name="y_w", align_bytes=64)

@@ -23,7 +23,6 @@ HALF = 512
 STRIPE = 16
 LINE = 4
 BANKS = J // BANK
-V_WIDTHS = [512, 512]
 X_WIDTHS = [128, 128, 256, 256, 256]
 FIRST = 256
 HELD = 384
@@ -105,10 +104,10 @@ def tile_list_htabg_mul_noneP_kernel(
             nc.sync.dma_start(out=v_s[q : q + 4, :].bitcast(I32), in_=v_s_apart[q : q + 32 : 8, :].bitcast(I32))
         x_planes[1] = reused.tile([P, T], F32, name="x_plane1", offset=PLANE_AT, align_bytes=64)
         nc.sync.dma_start(out=x_planes[1][:], in_=x_rows[:, 1, :])
-        nc.sync.dma_start(out=wa_raw[:].bitcast(I32), in_=wa_words[0].bitcast(I32))
         nc.sync.dma_start(out=x_planes[2][:], in_=x_rows[:, 2, :])
-        nc.sync.dma_start(out=wd_raw[:].bitcast(I32), in_=wd_words[0].bitcast(I32))
+        nc.sync.dma_start(out=wa_raw[:].bitcast(I32), in_=wa_words[0].bitcast(I32))
         nc.sync.dma_start(out=x_planes[3][:], in_=x_rows[:, 3, :])
+        nc.sync.dma_start(out=wd_raw[:].bitcast(I32), in_=wd_words[0].bitcast(I32))
 
         wb_bf = keep.tile([P, K * PACK], BF16, name="wb_bf", align_bytes=64)
         wb_w = keep.tile([P, K], U32, name="wb_w", align_bytes=64)
@@ -138,10 +137,7 @@ def tile_list_htabg_mul_noneP_kernel(
             nc.sync.dma_start(out=w4_s[q : q + 4, :].bitcast(I32), in_=w4_s_dealt[q : q + 32 : 8, :].bitcast(I32))
 
         v_w = reused.tile([P, J], U32, name="v_w", offset=V_W_AT, align_bytes=64)
-        for j0, n in cuts(V_WIDTHS):
-            nc.vector.tensor_copy(
-                v_w[:, j0 : j0 + n], tab_w[:].indirect(tab_list[:, j0 // STRIPE : (j0 + n) // STRIPE])
-            )
+        nc.vector.tensor_copy(v_w[:], tab_w[:].indirect(tab_list[:]))
 
         picked = keep.tile([P, PACK * J], F32, name="picked", align_bytes=64)
 
@@ -192,7 +188,6 @@ def tile_list_htabg_mul_noneP_kernel(
             )
 
         deal_words(0, wa_raw)
-        deal_words(1, wd_raw)
 
         x_cuts = cuts(X_WIDTHS)
         last = len(x_cuts) - 1
@@ -299,6 +294,7 @@ def tile_list_htabg_mul_noneP_kernel(
         quantise_x(1)
         product_a(1)
         weave(2)
+        deal_words(1, wd_raw)
         multiply(0)
         quantise_x(2)
         product_a(2)
@@ -307,8 +303,8 @@ def tile_list_htabg_mul_noneP_kernel(
         multiply(1)
         product_a(3)
         weave(3)
-        weave(4)
         store_y(0)
+        weave(4)
         multiply(2)
         quantise_h(1)
         quantise_x(3)

@@ -19,21 +19,20 @@ ADD = mybir.AluOpType.add
 P = 128
 PACK = 4
 BANK = 128
+BANKS = J // BANK
 HALF = 512
 STRIPE = 16
 LINE = 4
-BANKS = J // BANK
+QUADRANT = 32
+APART = 8
+YA_BANKS, OUT_BANKS = 3, 5
 X_WIDTHS = [128, 128, 256, 256, 256]
-FIRST = 256
 HELD = 384
-WB_SPLIT = 80
+WB_SPLIT = 74
 TAB_S_AT = 4 * PACK * K
 V_W_AT = TAB_S_AT + 64 - 4 * J
 PLANE_AT = TAB_S_AT + T - 64
-
-
-def cuts(widths):
-    return [(sum(widths[:c]), n) for c, n in enumerate(widths)]
+CODES_AT = PLANE_AT + 4 * T
 
 
 def tile_list_htabg_mul_noneP_kernel(
@@ -57,15 +56,15 @@ def tile_list_htabg_mul_noneP_kernel(
 
         nc.gpsimd.memset(tab_s[:].bitcast(I32), 0)
         identity = keep.tile([P, P], F32, name="identity")
-        ones = keep.tile([P, 32], F32, name="ones")
-        count = keep.tile([P, 32], F32, name="count", align_bytes=64)
-        count_down = keep.tile([P, 32], F32, name="count_down", align_bytes=64)
+        ones = keep.tile([P, QUADRANT], F32, name="ones")
+        count = keep.tile([P, QUADRANT], F32, name="count", align_bytes=64)
+        count_down = keep.tile([P, QUADRANT], F32, name="count_down", align_bytes=64)
         nc.vector.memset(ones[:], 1.0)
         nc.vector.memset(identity[:], 0.0)
         nc.vector.tensor_tensor_scan(count[:], ones[:], ones[:], 0.0, MULT, ADD)
         nc.vector.transpose(count_down[:], count[:])
-        for q in range(4):
-            rows = slice(32 * q, 32 * (q + 1))
+        for q in range(0, P, QUADRANT):
+            rows = slice(q, q + QUADRANT)
             nc.vector.tensor_tensor(identity[rows, rows], count[rows, :], count_down[rows, :], mybir.AluOpType.is_equal)
         nc.gpsimd.memset(w4_s_raw[:].bitcast(I32), 0)
         w4_s_dealt = keep.tile([P, 2 * K], U8, name="w4_s_dealt", align_bytes=64)
@@ -77,18 +76,18 @@ def tile_list_htabg_mul_noneP_kernel(
 
         x_rows = xT.rearrange("(p i) t -> p i t", i=PACK)
         wb_rows = wb.rearrange("(p i) r -> p i r", i=PACK)
-        nc.sync.dma_start(out=wgt_rows[:], in_=wgt2[0:P:8, :].rearrange("a (b d) -> a b d", d=P))
+        nc.sync.dma_start(out=wgt_rows[:], in_=wgt2[0:P:APART, :].rearrange("a (b d) -> a b d", d=P))
         nc.sync.dma_start(tab_list[:], offs)
         nc.sync.dma_start(out=wb_raw[:, 0:2, :], in_=wb_rows[:, 0:2, :])
-        nc.sync.dma_start(out=tab_s[0:P:8, :].bitcast(I32), in_=tab_scales[0].bitcast(I32))
+        nc.sync.dma_start(out=tab_s[0:P:APART, :].bitcast(I32), in_=tab_scales[0].bitcast(I32))
         nc.sync.dma_start(out=wb_raw[:, 2:4, :], in_=wb_rows[:, 2:4, :])
         nc.sync.dma_start(out=tab_w[:].bitcast(I32), in_=tab_words[0].rearrange("p t i -> p (t i)").bitcast(I32))
         nc.sync.dma_start(x_lists[:], offs2)
-        nc.sync.dma_start(out=w4_s_raw[0:P:8, 0:K].bitcast(I32), in_=wa_scales[0].bitcast(I32))
-        nc.sync.dma_start(out=w4_s_raw[0:P:8, K : 2 * K].bitcast(I32), in_=wd_scales[0].bitcast(I32))
+        nc.sync.dma_start(out=w4_s_raw[0:P:APART, 0:K].bitcast(I32), in_=wa_scales[0].bitcast(I32))
+        nc.sync.dma_start(out=w4_s_raw[0:P:APART, K : 2 * K].bitcast(I32), in_=wd_scales[0].bitcast(I32))
         nc.sync.dma_start(out=x_planes[0][:], in_=x_rows[:, 0, :])
 
-        bank = psum.tile([P, PACK, BANK], F32, name="ya_bank", bufs=3)
+        bank = psum.tile([P, PACK, BANK], F32, name="ya_bank", bufs=YA_BANKS)
         nc.tensor.transpose(bank[:, 0, :], wgt_rows[:], identity[:])
         spread = [keep.tile([P, PACK, P], F32, name="spread%d" % h) for h in range(2)]
         for h in range(2):
@@ -98,10 +97,15 @@ def tile_list_htabg_mul_noneP_kernel(
                 in_=by_group.unsqueeze(3).to_broadcast([P, PACK, P // STRIPE, STRIPE]),
             )
 
+        def carry_home(home, apart):
+            for q in range(0, P, QUADRANT):
+                nc.sync.dma_start(
+                    out=home[q : q + PACK, :].bitcast(I32), in_=apart[q : q + QUADRANT : APART, :].bitcast(I32)
+                )
+
         v_s_apart = keep.tile([P, J], U8, name="v_s_apart", align_bytes=64)
         nc.vector.tensor_copy(v_s_apart[:], tab_s[:].indirect(tab_list[:]))
-        for q in range(0, P, 32):
-            nc.sync.dma_start(out=v_s[q : q + 4, :].bitcast(I32), in_=v_s_apart[q : q + 32 : 8, :].bitcast(I32))
+        carry_home(v_s, v_s_apart)
         x_planes[1] = reused.tile([P, T], F32, name="x_plane1", offset=PLANE_AT, align_bytes=64)
         nc.sync.dma_start(out=x_planes[1][:], in_=x_rows[:, 1, :])
         nc.sync.dma_start(out=x_planes[2][:], in_=x_rows[:, 2, :])
@@ -122,7 +126,7 @@ def tile_list_htabg_mul_noneP_kernel(
 
         wgt_all = reused.tile([P, J], F32, name="wgt_all", offset=0, align_bytes=64)
         for h in range(2):
-            bank = psum.tile([P, PACK, BANK], F32, name="out_bank", bufs=5)
+            bank = psum.tile([P, PACK, BANK], F32, name="out_bank", bufs=OUT_BANKS)
             for b in range(PACK):
                 nc.tensor.transpose(bank[:, b, :], spread[h][:, b, :], identity[:])
             nc.scalar.copy(out=wgt_all[:, h * HALF : (h + 1) * HALF], in_=bank[:].rearrange("p b d -> p (b d)"))
@@ -133,8 +137,7 @@ def tile_list_htabg_mul_noneP_kernel(
                 out=w4_s_dealt[:, w * K : (w + 1) * K].rearrange("p (t m) -> p t m", t=PACK),
                 in_=w4_s_raw[:, w * K : (w + 1) * K].rearrange("p (m t) -> p t m", t=PACK),
             )
-        for q in range(0, P, 32):
-            nc.sync.dma_start(out=w4_s[q : q + 4, :].bitcast(I32), in_=w4_s_dealt[q : q + 32 : 8, :].bitcast(I32))
+        carry_home(w4_s, w4_s_dealt)
 
         v_w = reused.tile([P, J], U32, name="v_w", offset=V_W_AT, align_bytes=64)
         nc.vector.tensor_copy(v_w[:], tab_w[:].indirect(tab_list[:]))
@@ -155,7 +158,6 @@ def tile_list_htabg_mul_noneP_kernel(
         for i in range(PACK - 1):
             gather(i, 0, J)
 
-
         def fp4_slice(w, t):
             return dealt[w][:, 2 * t * P : 2 * (t + 1) * P].bitcast(E2M1), w4_s[:, w * K + t * P : w * K + (t + 1) * P]
 
@@ -173,7 +175,7 @@ def tile_list_htabg_mul_noneP_kernel(
         yb = [keep.tile([P, BANK, PACK], F32, name="yb%d" % b) for b in range(BANKS)]
         for b in range(BANKS):
             cols = slice(b * BANK, (b + 1) * BANK)
-            bank = psum.tile([P, PACK, BANK], F32, name="out_bank", bufs=5)
+            bank = psum.tile([P, PACK, BANK], F32, name="out_bank", bufs=OUT_BANKS)
             product(bank, wb_slice, v_w[:, cols], v_s[:, cols])
             nc.scalar.copy(out=yb[b][:], in_=bank[:].rearrange("p t j -> p j t"))
 
@@ -189,10 +191,9 @@ def tile_list_htabg_mul_noneP_kernel(
 
         deal_words(0, wa_raw)
 
-        x_cuts = cuts(X_WIDTHS)
+        x_cuts = [(sum(X_WIDTHS[:c]), n) for c, n in enumerate(X_WIDTHS)]
         last = len(x_cuts) - 1
-        codes_at = PLANE_AT + 4 * T
-        x_bf, x_q, ya, h_q, y_bank = {}, {}, {}, {}, {}
+        x_bf, x_q, ya, y_bank = {}, {}, {}, {}
         y_s = keep.tile([P, J], U8, name="y_s", align_bytes=64)
         y_w = keep.tile([P, J], U32, name="y_w", align_bytes=64)
         y_rows = out_0.rearrange("(p t) j -> p t j", t=PACK)
@@ -201,17 +202,19 @@ def tile_list_htabg_mul_noneP_kernel(
         h_order = [2, 4, None, 6, None, 0, 1, 3, 5, 7]
         h_all = keep.tile([P, len(h_order) * width], BF16, name="h_all", align_bytes=64)
         h_bf = [h_all[:, h_order.index(b) * width : (h_order.index(b) + 1) * width] for b in range(BANKS)]
-        y_late = keep.tile([P, (BANKS - 4) * width], BF16, name="y_late", align_bytes=64)
+        shared_slots = 4
+        y_late = keep.tile([P, (BANKS - shared_slots) * width], BF16, name="y_late", align_bytes=64)
         y_f = [keep.tile([P, PACK, BANK], F32, name="y_f%d" % b) for b in range(BANKS)]
 
         def y_bf(b, banks=1):
-            return h_all[:, b * width : (b + banks) * width] if b < 4 else y_late[:, (b - 4) * width : (b - 4 + banks) * width]
+            home, slot = (h_all, b) if b < shared_slots else (y_late, b - shared_slots)
+            return home[:, slot * width : (slot + banks) * width]
 
         def weave(c):
             j0, n = x_cuts[c]
             if c == last:
-                n = BANK
-            elif c:
+                n = n - BANK
+            elif c not in x_bf:
                 x_bf[c] = keep.tile([P, n * PACK], BF16, name="x_bf%d" % c, align_bytes=64)[:]
             nc.scalar.copy(
                 out=x_bf[c][:, 0 : n * PACK].rearrange("p (g e i) -> p g i e", e=LINE, i=PACK),
@@ -219,7 +222,6 @@ def tile_list_htabg_mul_noneP_kernel(
             )
 
         x_bf[last] = h_all[:, (h_order.index(0) - 1) * width : (h_order.index(0) + 1) * width]
-
         x_bf[0] = picked[:, PACK * J - HELD : PACK * J - HELD + width // 2].bitcast(BF16)
 
         def weave_gpsimd():
@@ -230,9 +232,9 @@ def tile_list_htabg_mul_noneP_kernel(
 
         def quantise_x(c):
             j0, n = x_cuts[c]
-            words = reused.tile([P, n], U32, name="x%d_w" % c, offset=codes_at + 4 * j0, align_bytes=64)
+            words = reused.tile([P, n], U32, name="x%d_w" % c, offset=CODES_AT + 4 * j0, align_bytes=64)
             if c >= 2:
-                scales = reused.tile([P, n], U8, name="x%d_s" % c, offset=codes_at + 4 * x_cuts[c - 2][0], align_bytes=64)
+                scales = reused.tile([P, n], U8, name="x%d_s" % c, offset=CODES_AT + 4 * x_cuts[c - 2][0], align_bytes=64)
             else:
                 scales = keep.tile([P, n], U8, name="x%d_s" % c, align_bytes=64)
             nc.vector.quantize_mx(out=words[:].bitcast(E4M3), scales=scales[:], in_=x_bf[c])
@@ -240,7 +242,7 @@ def tile_list_htabg_mul_noneP_kernel(
                 x_q[(j0 + c0) // BANK] = words[:, c0 : c0 + BANK], scales[:, c0 : c0 + BANK]
 
         def product_a(b):
-            ya[b] = psum.tile([P, PACK, BANK], F32, name="ya_bank", bufs=3)
+            ya[b] = psum.tile([P, PACK, BANK], F32, name="ya_bank", bufs=YA_BANKS)
             product(ya[b], lambda t: fp4_slice(0, t), *x_q[b])
 
         def multiply(b):
@@ -252,7 +254,7 @@ def tile_list_htabg_mul_noneP_kernel(
             words = keep.tile([P, BANK], U32, name="h%d_w" % b, align_bytes=64)
             scales = keep.tile([P, BANK], U8, name="h%d_s" % b, align_bytes=64)
             nc.vector.quantize_mx(out=words[:].bitcast(E4M3), scales=scales[:], in_=h_bf[b])
-            y_bank[b] = psum.tile([P, PACK, BANK], F32, name="out_bank", bufs=5)
+            y_bank[b] = psum.tile([P, PACK, BANK], F32, name="out_bank", bufs=OUT_BANKS)
             product(y_bank[b], lambda t: fp4_slice(1, t), words[:], scales[:])
 
         def store_y(b):
@@ -283,14 +285,14 @@ def tile_list_htabg_mul_noneP_kernel(
             cols = slice(b * BANK, (b + banks) * BANK)
             nc.sync.dma_start(out=y_words[:, cols], in_=y_w[:, cols].bitcast(I32))
 
-        gather(3, 0, BANK)
-        weave(0)
-        gather(3, BANK, BANK)
-        weave(1)
-        gather(3, FIRST, J - FIRST - HELD)
+        plane = PACK - 1
+        for c in range(2):
+            gather(plane, *x_cuts[c])
+            weave(c)
+        gather(plane, 2 * BANK, J - 2 * BANK - HELD)
         quantise_x(0)
         product_a(0)
-        gather(3, J - HELD, HELD)
+        gather(plane, J - HELD, HELD)
         quantise_x(1)
         product_a(1)
         weave(2)
@@ -300,39 +302,28 @@ def tile_list_htabg_mul_noneP_kernel(
         product_a(2)
         quantise_h(0)
         weave_gpsimd()
-        multiply(1)
-        product_a(3)
-        weave(3)
-        store_y(0)
-        weave(4)
-        multiply(2)
-        quantise_h(1)
-        quantise_x(3)
-        product_a(4)
-        quantise_h(2)
-        round_gpsimd(0)
-        store_y(1)
-        store_y(2)
-        round_scalar(2)
-        multiply(3)
-        product_a(5)
-        multiply(4)
-        quantise_h(3)
-        quantise_x(4)
-        product_a(6)
-        quantise_h(4)
-        round_gpsimd(1)
-        store_y(3)
-        store_y(4)
-        round_scalar(4)
-        multiply(5)
-        product_a(7)
-        multiply(6)
-        quantise_h(5)
-        quantise_h(6)
-        round_gpsimd(3, BANK // 2)
-        store_y(5)
-        store_y(6)
+        for pair, b in enumerate(range(1, BANKS - 1, 2)):
+            more_x = pair + 3 <= last
+            multiply(b)
+            product_a(b + 2)
+            if pair == 0:
+                weave(last - 1)
+                store_y(0)
+                weave(last)
+            multiply(b + 1)
+            quantise_h(b)
+            if more_x:
+                quantise_x(pair + 3)
+                product_a(b + 3)
+            quantise_h(b + 1)
+            if more_x:
+                round_gpsimd(pair)
+            else:
+                round_gpsimd(3, BANK // 2)
+            store_y(b)
+            store_y(b + 1)
+            if more_x:
+                round_scalar(b + 1)
         multiply(7)
         quantise_y(0, 2)
         store_words(0, 2)
@@ -348,7 +339,8 @@ def tile_list_htabg_mul_noneP_kernel(
         quantise_y(6, 1)
         quantise_y(7, 1)
         store_words(6, 2)
-        for q in range(4):
+        for q in range(P // QUADRANT):
             nc.sync.dma_start(
-                out=out_2[0, 4 * q : 4 * q + 4, :].bitcast(I32), in_=y_s[32 * q : 32 * q + 4, :].bitcast(I32)
+                out=out_2[0, PACK * q : PACK * (q + 1), :].bitcast(I32),
+                in_=y_s[QUADRANT * q : QUADRANT * q + PACK, :].bitcast(I32),
             )

@@ -60,7 +60,7 @@ def tile_list_htabg_mul_noneP_kernel(
         count = keep.tile([P, QUADRANT], F32, name="count", align_bytes=64)
         count_down = keep.tile([P, QUADRANT], F32, name="count_down", align_bytes=64)
         nc.vector.memset(ones[:], 1.0)
-        nc.vector.memset(identity[:], 0.0)
+        nc.scalar.mul(identity[:], ones[:, 0:1].to_broadcast([P, P]), 0.0)
         nc.vector.tensor_tensor_scan(count[:], ones[:], ones[:], 0.0, MULT, ADD)
         nc.vector.transpose(count_down[:], count[:])
         for q in range(0, P, QUADRANT):
@@ -76,26 +76,16 @@ def tile_list_htabg_mul_noneP_kernel(
 
         x_rows = xT.rearrange("(p i) t -> p i t", i=PACK)
         wb_rows = wb.rearrange("(p i) r -> p i r", i=PACK)
-        nc.sync.dma_start(out=wgt_rows[:], in_=wgt2[0:P:APART, :].rearrange("a (b d) -> a b d", d=P))
-        nc.sync.dma_start(tab_list[:], offs)
         nc.sync.dma_start(out=wb_raw[:, 0:2, :], in_=wb_rows[:, 0:2, :])
+        nc.sync.dma_start(tab_list[:], offs)
         nc.sync.dma_start(out=tab_s[0:P:APART, :].bitcast(I32), in_=tab_scales[0].bitcast(I32))
         nc.sync.dma_start(out=wb_raw[:, 2:4, :], in_=wb_rows[:, 2:4, :])
+        nc.sync.dma_start(out=wgt_rows[:], in_=wgt2[0:P:APART, :].rearrange("a (b d) -> a b d", d=P))
         nc.sync.dma_start(out=tab_w[:].bitcast(I32), in_=tab_words[0].rearrange("p t i -> p (t i)").bitcast(I32))
         nc.sync.dma_start(x_lists[:], offs2)
         nc.sync.dma_start(out=w4_s_raw[0:P:APART, 0:K].bitcast(I32), in_=wa_scales[0].bitcast(I32))
         nc.sync.dma_start(out=w4_s_raw[0:P:APART, K : 2 * K].bitcast(I32), in_=wd_scales[0].bitcast(I32))
         nc.sync.dma_start(out=x_planes[0][:], in_=x_rows[:, 0, :])
-
-        bank = psum.tile([P, PACK, BANK], F32, name="ya_bank", bufs=YA_BANKS)
-        nc.tensor.transpose(bank[:, 0, :], wgt_rows[:], identity[:])
-        spread = [keep.tile([P, PACK, P], F32, name="spread%d" % h) for h in range(2)]
-        for h in range(2):
-            by_group = bank[:, 0, :].rearrange("d (g x) -> d x g", x=STRIPE)[:, PACK * h : PACK * (h + 1), :]
-            nc.scalar.copy(
-                out=spread[h][:].rearrange("d b (g r) -> d b g r", r=STRIPE),
-                in_=by_group.unsqueeze(3).to_broadcast([P, PACK, P // STRIPE, STRIPE]),
-            )
 
         def carry_home(home, apart):
             for q in range(0, P, QUADRANT):
@@ -123,6 +113,16 @@ def tile_list_htabg_mul_noneP_kernel(
             wb_to[:, WB_SPLIT:].rearrange("p m i t -> p m t i"), wb_from[:, WB_SPLIT:].rearrange("p m i t -> p m t i"),
             1.0, 0.0, MULT, ADD,
         )
+
+        bank = psum.tile([P, PACK, BANK], F32, name="ya_bank", bufs=YA_BANKS)
+        nc.tensor.transpose(bank[:, 0, :], wgt_rows[:], identity[:])
+        spread = [keep.tile([P, PACK, P], F32, name="spread%d" % h) for h in range(2)]
+        for h in range(2):
+            by_group = bank[:, 0, :].rearrange("d (g x) -> d x g", x=STRIPE)[:, PACK * h : PACK * (h + 1), :]
+            nc.scalar.copy(
+                out=spread[h][:].rearrange("d b (g r) -> d b g r", r=STRIPE),
+                in_=by_group.unsqueeze(3).to_broadcast([P, PACK, P // STRIPE, STRIPE]),
+            )
 
         wgt_all = reused.tile([P, J], F32, name="wgt_all", offset=0, align_bytes=64)
         for h in range(2):

@@ -33,6 +33,7 @@ TAB_S_AT = 4 * PACK * K
 V_W_AT = TAB_S_AT + 64 - 4 * J
 PLANE_AT = TAB_S_AT + T - 64
 CODES_AT = PLANE_AT + 4 * T
+WD_S_AT = CODES_AT + 4 * J
 
 
 def tile_list_htabg_mul_noneP_kernel(
@@ -48,7 +49,8 @@ def tile_list_htabg_mul_noneP_kernel(
         x_lists = keep.tile([P, J // STRIPE], U16, name="x_lists")
         tab_s = reused.tile([P, T], U8, name="tab_s", offset=TAB_S_AT, align_bytes=64)
         tab_w = keep.tile([P, T], U32, name="tab_w", align_bytes=64)
-        w4_s_raw = keep.tile([P, 2 * K], U8, name="w4_s_raw", align_bytes=64)
+        wa_s_raw = keep.tile([P, K], U8, name="wa_s_raw", align_bytes=64)
+        wd_s_raw = reused.tile([P, K], U8, name="wd_s_raw", offset=WD_S_AT, align_bytes=64)
         wa_raw = keep.tile([P, K], U16, name="wa_raw", align_bytes=64)
         wd_raw = keep.tile([P, K], U16, name="wd_raw", align_bytes=64)
         x_planes = {i: keep.tile([P, T], F32, name="x_plane%d" % i) for i in (0, 2, 3)}
@@ -66,8 +68,8 @@ def tile_list_htabg_mul_noneP_kernel(
         for q in range(0, P, QUADRANT):
             rows = slice(q, q + QUADRANT)
             nc.vector.tensor_tensor(identity[rows, rows], count[rows, :], count_down[rows, :], mybir.AluOpType.is_equal)
-        nc.gpsimd.memset(w4_s_raw[:].bitcast(I32), 0)
-        w4_s_dealt = keep.tile([P, 2 * K], U8, name="w4_s_dealt", align_bytes=64)
+        nc.gpsimd.memset(wd_s_raw[:].bitcast(I32), 0)
+        nc.gpsimd.memset(wa_s_raw[:].bitcast(I32), 0)
         w4_s = keep.tile([P, 2 * K], U8, name="w4_s", align_bytes=64)
         nc.vector.memset(w4_s[:].bitcast(I32), 0)
         v_s = keep.tile([P, J], U8, name="v_s", align_bytes=64)
@@ -79,12 +81,12 @@ def tile_list_htabg_mul_noneP_kernel(
         nc.sync.dma_start(out=wb_raw[:, 0:2, :], in_=wb_rows[:, 0:2, :])
         nc.sync.dma_start(tab_list[:], offs)
         nc.sync.dma_start(out=tab_s[0:P:APART, :].bitcast(I32), in_=tab_scales[0].bitcast(I32))
+        nc.sync.dma_start(out=wd_s_raw[0:P:APART, :].bitcast(I32), in_=wd_scales[0].bitcast(I32))
         nc.sync.dma_start(out=wb_raw[:, 2:4, :], in_=wb_rows[:, 2:4, :])
         nc.sync.dma_start(out=wgt_rows[:], in_=wgt2[0:P:APART, :].rearrange("a (b d) -> a b d", d=P))
         nc.sync.dma_start(out=tab_w[:].bitcast(I32), in_=tab_words[0].rearrange("p t i -> p (t i)").bitcast(I32))
         nc.sync.dma_start(x_lists[:], offs2)
-        nc.sync.dma_start(out=w4_s_raw[0:P:APART, 0:K].bitcast(I32), in_=wa_scales[0].bitcast(I32))
-        nc.sync.dma_start(out=w4_s_raw[0:P:APART, K : 2 * K].bitcast(I32), in_=wd_scales[0].bitcast(I32))
+        nc.sync.dma_start(out=wa_s_raw[0:P:APART, :].bitcast(I32), in_=wa_scales[0].bitcast(I32))
         nc.sync.dma_start(out=x_planes[0][:], in_=x_rows[:, 0, :])
 
         def carry_home(home, apart):
@@ -96,6 +98,15 @@ def tile_list_htabg_mul_noneP_kernel(
         v_s_apart = keep.tile([P, J], U8, name="v_s_apart", align_bytes=64)
         nc.vector.tensor_copy(v_s_apart[:], tab_s[:].indirect(tab_list[:]))
         carry_home(v_s, v_s_apart)
+        w4_s_dealt = keep.tile([P, 2 * K], U8, name="w4_s_dealt", align_bytes=64)
+
+        def deal_scales(engine, w, raw):
+            engine.tensor_copy(
+                out=w4_s_dealt[:, w * K : (w + 1) * K].rearrange("p (t m) -> p t m", t=PACK),
+                in_=raw[:].rearrange("p (m t) -> p t m", t=PACK),
+            )
+
+        deal_scales(nc.gpsimd, 1, wd_s_raw)
         x_planes[1] = reused.tile([P, T], F32, name="x_plane1", offset=PLANE_AT, align_bytes=64)
         nc.sync.dma_start(out=x_planes[1][:], in_=x_rows[:, 1, :])
         nc.sync.dma_start(out=x_planes[2][:], in_=x_rows[:, 2, :])
@@ -103,7 +114,7 @@ def tile_list_htabg_mul_noneP_kernel(
         nc.sync.dma_start(out=x_planes[3][:], in_=x_rows[:, 3, :])
         nc.sync.dma_start(out=wd_raw[:].bitcast(I32), in_=wd_words[0].bitcast(I32))
 
-        wb_bf = keep.tile([P, K * PACK], BF16, name="wb_bf", align_bytes=64)
+        wb_bf = reused.tile([P, K * PACK], BF16, name="wb_bf", offset=WD_S_AT, align_bytes=64)
         wb_w = keep.tile([P, K], U32, name="wb_w", align_bytes=64)
         wb_s = reused.tile([P, K], U8, name="wb_s", offset=TAB_S_AT + K, align_bytes=64)
         wb_to = wb_bf[:].rearrange("p (t m i) -> p m i t", t=PACK, i=PACK)
@@ -132,11 +143,7 @@ def tile_list_htabg_mul_noneP_kernel(
             nc.scalar.copy(out=wgt_all[:, h * HALF : (h + 1) * HALF], in_=bank[:].rearrange("p b d -> p (b d)"))
 
         nc.vector.quantize_mx(out=wb_w[:].bitcast(E4M3), scales=wb_s[:], in_=wb_bf[:])
-        for w in range(2):
-            nc.gpsimd.tensor_copy(
-                out=w4_s_dealt[:, w * K : (w + 1) * K].rearrange("p (t m) -> p t m", t=PACK),
-                in_=w4_s_raw[:, w * K : (w + 1) * K].rearrange("p (m t) -> p t m", t=PACK),
-            )
+        deal_scales(nc.gpsimd, 0, wa_s_raw)
         carry_home(w4_s, w4_s_dealt)
 
         v_w = reused.tile([P, J], U32, name="v_w", offset=V_W_AT, align_bytes=64)

@@ -28,6 +28,7 @@ APART = 8
 YA_BANKS, OUT_BANKS = 3, 5
 X_WIDTHS = [128, 128, 256, 256, 256]
 HELD = 384
+BESIDE_PAIR = 96
 WB_SPLIT = 74
 TAB_S_AT = 4 * PACK * K
 V_W_AT = TAB_S_AT + 64 - 4 * J
@@ -220,7 +221,7 @@ def tile_list_htabg_mul_noneP_kernel(
         def weave(c):
             j0, n = x_cuts[c]
             if c == last:
-                n = n - BANK
+                n = n - BESIDE_PAIR
             elif c not in x_bf:
                 x_bf[c] = keep.tile([P, n * PACK], BF16, name="x_bf%d" % c, align_bytes=64)[:]
             nc.scalar.copy(
@@ -233,8 +234,8 @@ def tile_list_htabg_mul_noneP_kernel(
 
         def weave_gpsimd():
             nc.gpsimd.tensor_scalar(
-                x_bf[last][:, width:].rearrange("p (j i) -> p j i", i=PACK),
-                picked_at(J - BANK, BANK).rearrange("p i j -> p j i"), 1.0, 0.0, MULT, ADD,
+                x_bf[last][:, 2 * width - BESIDE_PAIR * PACK :].rearrange("p (j i) -> p j i", i=PACK),
+                picked_at(J - BESIDE_PAIR, BESIDE_PAIR).rearrange("p i j -> p j i"), 1.0, 0.0, MULT, ADD,
             )
 
         def quantise_x(c):
@@ -269,8 +270,11 @@ def tile_list_htabg_mul_noneP_kernel(
             queue = nc.scalar if b == BANKS - 1 else nc.sync
             queue.dma_start(out=y_rows[:, :, b * BANK : (b + 1) * BANK], in_=y_f[b][:])
 
-        def round_scalar(b):
-            nc.scalar.copy(out=y_bf(b).rearrange("p (j t) -> p j t", t=PACK), in_=y_bank[b][:].rearrange("p t j -> p j t"))
+        def round_scalar(b, c0=0):
+            nc.scalar.copy(
+                out=y_bf(b)[:, c0 * PACK :].rearrange("p (j t) -> p j t", t=PACK),
+                in_=y_bank[b][:, :, c0:].rearrange("p t j -> p j t"),
+            )
 
         def round_vector(b, c0=0):
             nc.vector.tensor_copy(
@@ -323,7 +327,10 @@ def tile_list_htabg_mul_noneP_kernel(
                 quantise_x(pair + 3)
                 product_a(b + 3)
             quantise_h(b + 1)
-            if more_x:
+            if pair == 0:
+                round_gpsimd(0, BESIDE_PAIR)
+                round_scalar(0, BESIDE_PAIR)
+            elif more_x:
                 round_gpsimd(pair)
             else:
                 round_gpsimd(3, BANK // 2)

from contextlib import ExitStack

import concourse.mybir as mybir

K, T, J = 512, 2048, 1024
FLOPS = 3 * 2 * K * K * J

F32 = mybir.dt.float32
BF16 = mybir.dt.bfloat16
I32 = mybir.dt.int32
U32 = mybir.dt.uint32
U16 = mybir.dt.uint16
U8 = mybir.dt.uint8
E4M3 = mybir.dt.float8_e4m3fn_x4
E2M1 = mybir.dt.float4_e2m1fn_x4
MULT = mybir.AluOpType.mult
ADD = mybir.AluOpType.add

P = 128
PACK = 4
BANK = 128
BANKS = J // BANK
HALF = 512
STRIPE = 16
LINE = 4
QUADRANT = 32
APART = 8
YA_BANKS, OUT_BANKS = 3, 5
X_WIDTHS = [128, 128, 256, 256, 256]
HELD = 384
BESIDE_PAIR = 96
WB_SPLIT = 74
TAB_S_AT = 4 * PACK * K
V_W_AT = TAB_S_AT + 64 - 4 * J
PLANE_AT = TAB_S_AT + T - 64
CODES_AT = PLANE_AT + 4 * T
WD_S_AT = CODES_AT + 4 * J


def tile_list_htabg_mul_noneP_kernel(
    tc, tab_words, tab_scales, xT, wgt2, wa_words, wa_scales, wb, wd_words, wd_scales, offs, offs2, out_0, out_1, out_2
):
    nc = tc.nc
    with ExitStack() as ctx:
        keep = ctx.enter_context(tc.tile_pool(name="keep", bufs=1))
        reused = ctx.enter_context(tc.tile_pool(name="reused", bufs=1))
        psum = ctx.enter_context(tc.psum_pool(name="psum", bufs=1))

        tab_list = keep.tile([P, J // STRIPE], U16, name="tab_list")
        x_lists = keep.tile([P, J // STRIPE], U16, name="x_lists")
        tab_s = reused.tile([P, T], U8, name="tab_s", offset=TAB_S_AT, align_bytes=64)
        tab_w = keep.tile([P, T], U32, name="tab_w", align_bytes=64)
        wa_s_raw = keep.tile([P, K], U8, name="wa_s_raw", align_bytes=64)
        wd_s_raw = reused.tile([P, K], U8, name="wd_s_raw", offset=WD_S_AT, align_bytes=64)
        wa_raw = keep.tile([P, K], U16, name="wa_raw", align_bytes=64)
        wd_raw = keep.tile([P, K], U16, name="wd_raw", align_bytes=64)
        x_planes = {i: keep.tile([P, T], F32, name="x_plane%d" % i) for i in (0, 2, 3)}
        wb_raw = reused.tile([P, PACK, K], F32, name="wb_raw", offset=0, align_bytes=64)

        nc.gpsimd.memset(tab_s[:].bitcast(I32), 0)
        identity = keep.tile([P, P], F32, name="identity")
        ones = keep.tile([P, QUADRANT], F32, name="ones")
        count = keep.tile([P, QUADRANT], F32, name="count", align_bytes=64)
        count_down = keep.tile([P, QUADRANT], F32, name="count_down", align_bytes=64)
        nc.vector.memset(ones[:], 1.0)
        nc.scalar.mul(identity[:], ones[:, 0:1].to_broadcast([P, P]), 0.0)
        nc.vector.tensor_tensor_scan(count[:], ones[:], ones[:], 0.0, MULT, ADD)
        nc.vector.transpose(count_down[:], count[:])
        for q in range(0, P, QUADRANT):
            rows = slice(q, q + QUADRANT)
            nc.vector.tensor_tensor(identity[rows, rows], count[rows, :], count_down[rows, :], mybir.AluOpType.is_equal)
        nc.gpsimd.memset(wd_s_raw[:].bitcast(I32), 0)
        nc.gpsimd.memset(wa_s_raw[:].bitcast(I32), 0)
        w4_s = keep.tile([P, 2 * K], U8, name="w4_s", align_bytes=64)
        nc.vector.memset(w4_s[:].bitcast(I32), 0)
        v_s = keep.tile([P, J], U8, name="v_s", align_bytes=64)
        nc.vector.memset(v_s[:].bitcast(I32), 0)
        wgt_rows = keep.tile([P, P], F32, name="wgt_rows")

        x_rows = xT.rearrange("(p i) t -> p i t", i=PACK)
        wb_rows = wb.rearrange("(p i) r -> p i r", i=PACK)
        nc.sync.dma_start(out=wb_raw[:, 0:2, :], in_=wb_rows[:, 0:2, :])
        nc.sync.dma_start(tab_list[:], offs)
        nc.sync.dma_start(out=tab_s[0:P:APART, :].bitcast(I32), in_=tab_scales[0].bitcast(I32))
        nc.sync.dma_start(out=wd_s_raw[0:P:APART, :].bitcast(I32), in_=wd_scales[0].bitcast(I32))
        nc.sync.dma_start(out=wb_raw[:, 2:4, :], in_=wb_rows[:, 2:4, :])
        nc.sync.dma_start(out=wgt_rows[:], in_=wgt2[0:P:APART, :].rearrange("a (b d) -> a b d", d=P))
        nc.sync.dma_start(out=tab_w[:].bitcast(I32), in_=tab_words[0].rearrange("p t i -> p (t i)").bitcast(I32))
        nc.sync.dma_start(x_lists[:], offs2)
        nc.sync.dma_start(out=wa_s_raw[0:P:APART, :].bitcast(I32), in_=wa_scales[0].bitcast(I32))
        nc.sync.dma_start(out=x_planes[0][:], in_=x_rows[:, 0, :])

        def carry_home(home, apart):
            for q in range(0, P, QUADRANT):
                nc.sync.dma_start(
                    out=home[q : q + PACK, :].bitcast(I32), in_=apart[q : q + QUADRANT : APART, :].bitcast(I32)
                )

        v_s_apart = keep.tile([P, J], U8, name="v_s_apart", align_bytes=64)
        nc.vector.tensor_copy(v_s_apart[:], tab_s[:].indirect(tab_list[:]))
        carry_home(v_s, v_s_apart)
        w4_s_dealt = keep.tile([P, 2 * K], U8, name="w4_s_dealt", align_bytes=64)

        def deal_scales(engine, w, raw):
            engine.tensor_copy(
                out=w4_s_dealt[:, w * K : (w + 1) * K].rearrange("p (t m) -> p t m", t=PACK),
                in_=raw[:].rearrange("p (m t) -> p t m", t=PACK),
            )

        deal_scales(nc.gpsimd, 1, wd_s_raw)
        x_planes[1] = reused.tile([P, T], F32, name="x_plane1", offset=PLANE_AT, align_bytes=64)
        nc.sync.dma_start(out=x_planes[1][:], in_=x_rows[:, 1, :])
        nc.sync.dma_start(out=x_planes[2][:], in_=x_rows[:, 2, :])
        nc.sync.dma_start(out=wa_raw[:].bitcast(I32), in_=wa_words[0].bitcast(I32))
        nc.sync.dma_start(out=x_planes[3][:], in_=x_rows[:, 3, :])
        nc.sync.dma_start(out=wd_raw[:].bitcast(I32), in_=wd_words[0].bitcast(I32))

        wb_bf = reused.tile([P, K * PACK], BF16, name="wb_bf", offset=WD_S_AT, align_bytes=64)
        wb_w = keep.tile([P, K], U32, name="wb_w", align_bytes=64)
        wb_s = reused.tile([P, K], U8, name="wb_s", offset=TAB_S_AT + K, align_bytes=64)
        wb_to = wb_bf[:].rearrange("p (t m i) -> p m i t", t=PACK, i=PACK)
        wb_from = wb_raw[:].rearrange("p i (m t) -> p m i t", t=PACK)
        nc.scalar.copy(out=wb_to[:, 0:WB_SPLIT], in_=wb_from[:, 0:WB_SPLIT])
        nc.gpsimd.tensor_scalar(
            wb_to[:, WB_SPLIT:].rearrange("p m i t -> p m t i"), wb_from[:, WB_SPLIT:].rearrange("p m i t -> p m t i"),
            1.0, 0.0, MULT, ADD,
        )

        bank = psum.tile([P, PACK, BANK], F32, name="ya_bank", bufs=YA_BANKS)
        nc.tensor.transpose(bank[:, 0, :], wgt_rows[:], identity[:])
        spread = [keep.tile([P, PACK, P], F32, name="spread%d" % h) for h in range(2)]
        for h in range(2):
            by_group = bank[:, 0, :].rearrange("d (g x) -> d x g", x=STRIPE)[:, PACK * h : PACK * (h + 1), :]
            nc.scalar.copy(
                out=spread[h][:].rearrange("d b (g r) -> d b g r", r=STRIPE),
                in_=by_group.unsqueeze(3).to_broadcast([P, PACK, P // STRIPE, STRIPE]),
            )

        wgt_all = reused.tile([P, J], F32, name="wgt_all", offset=0, align_bytes=64)
        for h in range(2):
            bank = psum.tile([P, PACK, BANK], F32, name="out_bank", bufs=OUT_BANKS)
            for b in range(PACK):
                nc.tensor.transpose(bank[:, b, :], spread[h][:, b, :], identity[:])
            nc.scalar.copy(out=wgt_all[:, h * HALF : (h + 1) * HALF], in_=bank[:].rearrange("p b d -> p (b d)"))

        nc.vector.quantize_mx(out=wb_w[:].bitcast(E4M3), scales=wb_s[:], in_=wb_bf[:])
        deal_scales(nc.gpsimd, 0, wa_s_raw)
        carry_home(w4_s, w4_s_dealt)

        v_w = reused.tile([P, J], U32, name="v_w", offset=V_W_AT, align_bytes=64)
        nc.vector.tensor_copy(v_w[:], tab_w[:].indirect(tab_list[:]))

        picked = keep.tile([P, PACK * J], F32, name="picked", align_bytes=64)

        def picked_at(j0, n):
            return picked[:].rearrange("p (i j) -> p i j", i=PACK)[:, :, j0 : j0 + n]

        def gather(i, j0, n):
            nc.vector.tensor_tensor(
                picked_at(j0, n)[:, i, :],
                x_planes[i][:].indirect(x_lists[:, j0 // STRIPE : (j0 + n) // STRIPE]),
                wgt_all[:, j0 : j0 + n],
                MULT,
            )

        for i in range(PACK - 1):
            gather(i, 0, J)

        def fp4_slice(w, t):
            return dealt[w][:, 2 * t * P : 2 * (t + 1) * P].bitcast(E2M1), w4_s[:, w * K + t * P : w * K + (t + 1) * P]

        def wb_slice(t):
            return wb_w[:, t * P : (t + 1) * P].bitcast(E4M3), wb_s[:, t * P : (t + 1) * P]

        def product(bank, weights, words, scales):
            for t in range(PACK):
                w_words, w_scales = weights(t)
                nc.tensor.matmul_mx(
                    out=bank[:, t, :], lhsT=w_words, lhsT_scale=w_scales, rhs=words.bitcast(E4M3), rhs_scale=scales,
                    start=True, stop=True,
                )

        yb = [keep.tile([P, BANK, PACK], F32, name="yb%d" % b) for b in range(BANKS)]
        for b in range(BANKS):
            cols = slice(b * BANK, (b + 1) * BANK)
            bank = psum.tile([P, PACK, BANK], F32, name="out_bank", bufs=OUT_BANKS)
            product(bank, wb_slice, v_w[:, cols], v_s[:, cols])
            nc.scalar.copy(out=yb[b][:], in_=bank[:].rearrange("p t j -> p j t"))

        wa_dealt = reused.tile([P, 2 * K], U8, name="wa_dealt", offset=V_W_AT, align_bytes=64)
        wd_dealt = reused.tile([P, 2 * K], U8, name="wd_dealt", offset=V_W_AT + 2 * K, align_bytes=64)
        dealt = [wa_dealt, wd_dealt]

        def deal_words(w, raw):
            nc.scalar.copy(
                out=dealt[w][:].bitcast(U16).rearrange("p (t m) -> p t m", t=PACK),
                in_=raw[:].rearrange("p (m t) -> p t m", t=PACK),
            )

        deal_words(0, wa_raw)

        x_cuts = [(sum(X_WIDTHS[:c]), n) for c, n in enumerate(X_WIDTHS)]
        last = len(x_cuts) - 1
        x_bf, x_q, ya, y_bank = {}, {}, {}, {}
        y_s = keep.tile([P, J], U8, name="y_s", align_bytes=64)
        y_w = keep.tile([P, J], U32, name="y_w", align_bytes=64)
        y_rows = out_0.rearrange("(p t) j -> p t j", t=PACK)
        y_words = out_1[0].rearrange("p j i -> p (j i)").bitcast(I32)
        width = BANK * PACK
        h_order = [2, 4, None, 6, None, 0, 1, 3, 5, 7]
        h_all = keep.tile([P, len(h_order) * width], BF16, name="h_all", align_bytes=64)
        h_bf = [h_all[:, h_order.index(b) * width : (h_order.index(b) + 1) * width] for b in range(BANKS)]
        shared_slots = 4
        y_late = keep.tile([P, (BANKS - shared_slots) * width], BF16, name="y_late", align_bytes=64)
        y_f = [keep.tile([P, PACK, BANK], F32, name="y_f%d" % b) for b in range(BANKS)]

        def y_bf(b, banks=1):
            home, slot = (h_all, b) if b < shared_slots else (y_late, b - shared_slots)
            return home[:, slot * width : (slot + banks) * width]

        def weave(c):
            j0, n = x_cuts[c]
            if c == last:
                n = n - BESIDE_PAIR
            elif c not in x_bf:
                x_bf[c] = keep.tile([P, n * PACK], BF16, name="x_bf%d" % c, align_bytes=64)[:]
            nc.scalar.copy(
                out=x_bf[c][:, 0 : n * PACK].rearrange("p (g e i) -> p g i e", e=LINE, i=PACK),
                in_=picked_at(j0, n).rearrange("p i (g e) -> p g i e", e=LINE),
            )

        x_bf[last] = h_all[:, (h_order.index(0) - 1) * width : (h_order.index(0) + 1) * width]
        x_bf[0] = picked[:, PACK * J - HELD : PACK * J - HELD + width // 2].bitcast(BF16)

        def weave_gpsimd():
            nc.gpsimd.tensor_scalar(
                x_bf[last][:, 2 * width - BESIDE_PAIR * PACK :].rearrange("p (j i) -> p j i", i=PACK),
                picked_at(J - BESIDE_PAIR, BESIDE_PAIR).rearrange("p i j -> p j i"), 1.0, 0.0, MULT, ADD,
            )

        def quantise_x(c):
            j0, n = x_cuts[c]
            words = reused.tile([P, n], U32, name="x%d_w" % c, offset=CODES_AT + 4 * j0, align_bytes=64)
            if c >= 2:
                scales = reused.tile([P, n], U8, name="x%d_s" % c, offset=CODES_AT + 4 * x_cuts[c - 2][0], align_bytes=64)
            else:
                scales = keep.tile([P, n], U8, name="x%d_s" % c, align_bytes=64)
            nc.vector.quantize_mx(out=words[:].bitcast(E4M3), scales=scales[:], in_=x_bf[c])
            for c0 in range(0, n, BANK):
                x_q[(j0 + c0) // BANK] = words[:, c0 : c0 + BANK], scales[:, c0 : c0 + BANK]

        def product_a(b):
            ya[b] = psum.tile([P, PACK, BANK], F32, name="ya_bank", bufs=YA_BANKS)
            product(ya[b], lambda t: fp4_slice(0, t), *x_q[b])

        def multiply(b):
            nc.vector.tensor_tensor(
                h_bf[b].rearrange("p (j t) -> p j t", t=PACK), ya[b][:].rearrange("p t j -> p j t"), yb[b][:], MULT
            )

        def quantise_h(b):
            words = keep.tile([P, BANK], U32, name="h%d_w" % b, align_bytes=64)
            scales = keep.tile([P, BANK], U8, name="h%d_s" % b, align_bytes=64)
            nc.vector.quantize_mx(out=words[:].bitcast(E4M3), scales=scales[:], in_=h_bf[b])
            y_bank[b] = psum.tile([P, PACK, BANK], F32, name="out_bank", bufs=OUT_BANKS)
            product(y_bank[b], lambda t: fp4_slice(1, t), words[:], scales[:])

        def store_y(b):
            nc.scalar.copy(out=y_f[b][:], in_=y_bank[b][:])
            queue = nc.scalar if b == BANKS - 1 else nc.sync
            queue.dma_start(out=y_rows[:, :, b * BANK : (b + 1) * BANK], in_=y_f[b][:])

        def round_scalar(b, c0=0):
            nc.scalar.copy(
                out=y_bf(b)[:, c0 * PACK :].rearrange("p (j t) -> p j t", t=PACK),
                in_=y_bank[b][:, :, c0:].rearrange("p t j -> p j t"),
            )

        def round_vector(b, c0=0):
            nc.vector.tensor_copy(
                out=y_bf(b)[:, c0 * PACK :].rearrange("p (g e t) -> p g t e", e=LINE, t=PACK),
                in_=y_f[b][:, :, c0:].rearrange("p t (g e) -> p g t e", e=LINE),
            )

        def round_gpsimd(b, n=BANK):
            nc.gpsimd.tensor_scalar(
                y_bf(b)[:, 0 : n * PACK].rearrange("p (j t) -> p j t", t=PACK),
                y_f[b][:, :, 0:n].rearrange("p t j -> p j t"), 1.0, 0.0, MULT, ADD,
            )

        def quantise_y(b, banks):
            cols = slice(b * BANK, (b + banks) * BANK)
            nc.vector.quantize_mx(out=y_w[:, cols].bitcast(E4M3), scales=y_s[:, cols], in_=y_bf(b, banks))

        def store_words(b, banks):
            cols = slice(b * BANK, (b + banks) * BANK)
            nc.sync.dma_start(out=y_words[:, cols], in_=y_w[:, cols].bitcast(I32))

        plane = PACK - 1
        for c in range(2):
            gather(plane, *x_cuts[c])
            weave(c)
        gather(plane, 2 * BANK, J - 2 * BANK - HELD)
        quantise_x(0)
        product_a(0)
        gather(plane, J - HELD, HELD)
        quantise_x(1)
        product_a(1)
        weave(2)
        deal_words(1, wd_raw)
        multiply(0)
        quantise_x(2)
        product_a(2)
        quantise_h(0)
        weave_gpsimd()
        for pair, b in enumerate(range(1, BANKS - 1, 2)):
            more_x = pair + 3 <= last
            multiply(b)
            product_a(b + 2)
            if pair == 0:
                weave(last - 1)
                store_y(0)
                weave(last)
            multiply(b + 1)
            quantise_h(b)
            if more_x:
                quantise_x(pair + 3)
                product_a(b + 3)
            quantise_h(b + 1)
            if pair == 0:
                round_gpsimd(0, BESIDE_PAIR)
                round_scalar(0, BESIDE_PAIR)
            elif more_x:
                round_gpsimd(pair)
            else:
                round_gpsimd(3, BANK // 2)
            store_y(b)
            store_y(b + 1)
            if more_x:
                round_scalar(b + 1)
        multiply(7)
        quantise_y(0, 2)
        store_words(0, 2)
        quantise_h(7)
        round_scalar(7)
        store_y(7)
        round_vector(3, BANK // 2)
        round_vector(5)
        quantise_y(2, 2)
        round_vector(6)
        quantise_y(4, 2)
        store_words(2, 4)
        quantise_y(6, 1)
        quantise_y(7, 1)
        store_words(6, 2)
        for q in range(P // QUADRANT):
            nc.sync.dma_start(
                out=out_2[0, PACK * q : PACK * (q + 1), :].bitcast(I32),
                in_=y_s[QUADRANT * q : QUADRANT * q + PACK, :].bitcast(I32),
            )
